import numpy as np
import ml_dtypes


def mxq(x, axis, fmt="e4m3"):
    dtype, down = {"e4m3": (ml_dtypes.float8_e4m3fn, 7), "e5m2": (ml_dtypes.float8_e5m2, 14)}[fmt]
    v = np.moveaxis(np.asarray(x, np.float32).astype(ml_dtypes.bfloat16).astype(np.float64), axis, -1)
    blocks = v.reshape(v.shape[:-1] + (-1, 32))
    amax = np.abs(blocks).max(-1, keepdims=True)
    byte = np.maximum(np.where(amax > 0, np.frexp(amax)[1] - 1 + 127, 0) - down, 1)
    scale = np.exp2(byte - 127.0)
    codes = (blocks / scale).astype(np.float32).astype(dtype).astype(np.float64)
    return np.moveaxis((codes * scale).reshape(v.shape), -1, axis)


WIDE = False


def mx_kscale(k):
    if not WIDE:
        return np.ones(k)
    levels = np.array([10, -10, 5, -5, 0])
    if k % 512:
        return np.exp2(np.random.permutation(np.resize(levels, k // 32))).repeat(32)
    a = np.empty((k // 512, 16))
    for p in range(k // 512):
        a[p, :8] = np.random.permutation(np.resize(levels, 8))
        for g in range(8):
            far = levels[np.abs(levels - a[p, g]) >= 10]
            a[p, g + 8] = far[np.random.randint(len(far))]
    return np.exp2(a.ravel()).repeat(32)


BF16 = ml_dtypes.bfloat16


def bf(x):
    return np.asarray(x, np.float32).astype(BF16)


def f64(x):
    return np.asarray(x).astype(np.float64)


E2M1 = np.array([0.0, 0.5, 1.0, 1.5, 2.0, 3.0, 4.0, 6.0, -0.0, -0.5, -1.0, -1.5, -2.0, -3.0, -4.0, -6.0])


def pack_weight(w, fmt):
    k, n = w.shape
    w = f64(bf(w)).reshape(k // 32, 32, n)
    amax = np.abs(w).max(1)
    if fmt == "e4m3":
        byte = np.frexp(amax)[1] - 1 + 127 - 7
    else:
        mant, ex = np.frexp(amax / 6.0)
        byte = np.where(mant > 0.5, ex, ex - 1) + 127
    byte = np.clip(np.where(amax > 0, byte, 1), 1, 254)
    scaled = (w * np.exp2(127.0 - byte)[:, None, :]).reshape(k, n).astype(np.float32)
    by_word = np.ascontiguousarray(scaled.reshape(k // 512, 128, 4, n).transpose(0, 1, 3, 2))
    if fmt == "e4m3":
        words = by_word.astype(ml_dtypes.float8_e4m3fn).view(np.uint8)
    else:
        c = by_word.astype(ml_dtypes.float4_e2m1fn).view(np.uint8) & 0xF
        words = c[..., 0::2] | (c[..., 1::2] << 4)
    return np.ascontiguousarray(words), np.ascontiguousarray(byte.astype(np.uint8).reshape(k // 512, 16, n))


def unpack_weight(words, scales, fmt):
    g, p, n, _ = words.shape
    if fmt == "e4m3":
        vals = np.ascontiguousarray(words).view(ml_dtypes.float8_e4m3fn).astype(np.float64)
    else:
        nib = np.empty((g, p, n, 4), np.uint8)
        nib[..., 0::2] = words & 0xF
        nib[..., 1::2] = words >> 4
        vals = E2M1[nib]
    vals = vals * np.repeat(np.exp2(scales.astype(np.float64) - 127.0), 8, axis=1)[..., None]
    return vals.transpose(0, 1, 3, 2).reshape(g * 512, n)
def pack4(w):
    words, scales = pack_weight(w, "e2m1")
    return words.reshape(words.shape[0], 128, -1), scales


def unpack4(words, scales):
    return unpack_weight(words.reshape(words.shape[0], 128, -1, 2), scales, "e2m1")


M, S, E, A = 1024, 1536, 512, 1024


def draw0():
    s = mx_kscale(S)
    r = mx_kscale(E)
    t = mx_kscale(A)
    F = np.random.standard_normal((S, A)) / np.sqrt(S) / s[:, None] * t
    L = np.random.standard_normal((E, A)) / np.sqrt(E) / r[:, None] * t
    B = np.random.standard_normal((A, S)) / np.sqrt(A) / t[:, None]
    L_words, L_scales = pack4(L)
    B_words, B_scales = pack4(B)
    return {"x": bf(np.random.standard_normal((M, S)) * s),
            "e": bf(np.random.standard_normal((M, E)) * r),
            "F": bf(F),
            "L_words": L_words, "L_scales": L_scales,
            "lo": bf(-(1 + np.random.random(A)) * t),
            "hi": bf((1 + np.random.random(A)) * t),
            "B_words": B_words, "B_scales": B_scales,
            "drift": bf(np.random.standard_normal((M, S)))}


def core(x, e, F, L_words, L_scales, lo, hi, B_words, B_scales, drift):
    fb = mxq(f64(x), 1, "e4m3") @ mxq(f64(F), 0, "e4m3")
    ia = mxq(f64(e), 1, "e4m3") @ unpack4(L_words, L_scales)
    u = fb + ia
    u = np.maximum(np.minimum(u, f64(hi)), f64(lo))
    return (mxq(u, 1, "e4m3") @ unpack4(B_words, B_scales)) + f64(drift)


def e4m3fn_bytes(y):
    return np.clip(np.asarray(y, np.float64), -448.0, 448.0).astype(np.float32).astype(ml_dtypes.float8_e4m3fn).view(np.uint8)


def e4m3fn_values(b):
    return np.asarray(b, np.uint8).view(ml_dtypes.float8_e4m3fn).astype(np.float64)


def setup_inputs():
    d = draw0()
    x0 = np.asarray(d['x']).astype(np.float64)
    s = (np.max(np.abs(x0), axis=(0,), keepdims=True) / 448.0).astype(np.float32)
    out = {}
    for k, v in d.items():
        if k == 'x':
            out['x_bytes'] = e4m3fn_bytes(x0 / s.astype(np.float64))
            out['x_scale'] = s
        else:
            out[k] = v
    return out


def reference(x_bytes, x_scale, e, F, L_words, L_scales, lo, hi, B_words, B_scales, drift):
    return core(e4m3fn_values(x_bytes) * x_scale.astype(np.float64), e, F, L_words, L_scales, lo, hi, B_words, B_scales, drift)

@@ -1,0 +1,259 @@
+from contextlib import ExitStack
+
+import concourse.mybir as mybir
+from concourse.masks import make_identity
+
+M, S, E, A = 1024, 1536, 512, 1024
+FLOPS = 2 * M * A * (S + E) + 2 * M * A * S
+
+F32 = mybir.dt.float32
+BF16 = mybir.dt.bfloat16
+U32 = mybir.dt.uint32
+I32 = mybir.dt.int32
+U8 = mybir.dt.uint8
+FP8 = mybir.dt.float8_e4m3fn
+FP8X4 = mybir.dt.float8_e4m3fn_x4
+FP4X4 = mybir.dt.float4_e2m1fn_x4
+ALU = mybir.AluOpType
+P = 128
+SCRIPT = """
+LW:0 LW:1 X:1 X:0 FI:0,0 XT:0,0 XT:0,3 FI:1,0 XT:0,1 FI:2,0 XE:0,1 XE:0,0 XT:0,2 X:2
+LM: X:3 XE:0,2 LS:0 FQ:2,0 FQ:1,0 FQ:0,0 XT:1,2 XE:0,3 XT:1,0 X:5 LS:1 XQ:0,0 XE:1,2
+XT:1,3 FI:0,1 XE:1,3 XT:1,1 X:4 XE:1,1 XE:1,0 XQ:1,3 XQ:0,3 XQ:0,2 XQ:1,1 XT:2,0 XQ:1,0 FI:2,1
+FI:1,1 XQ:0,1 XQ:1,2 XT:2,1 XE:2,1 XT:2,2 XE:2,0 X:6 S1:0,0,0 X:7 S1:0,0,3 S1:0,0,2 S1:0,0,1 FQ:0,1
+XQ:2,1 UE:0,0,2 UE:0,0,0 XT:3,0 UE:0,0,3 XT:3,2 XE:2,2 FQ:1,1 FQ:2,1 XQ:2,0 XT:2,3 XE:3,0 UC:0,0,3 UE:0,0,1
+S1:0,1,0 UC:0,0,0 XE:2,3 XQ:2,2 XQ:3,0 S1:0,1,1 UE:0,1,0 UC:0,0,2 XT:3,3 XE:3,2 S1:0,1,2 XT:3,1 UC:0,0,1 UE:0,1,1
+XE:3,1 XQ:3,2 XQ:2,3 UC:0,1,0 XE:3,3 XQ:3,1 UC:0,1,1 UE:0,1,2 S1:0,1,3 XQ:3,3 S1:1,0,2 UE:0,1,3 UE:1,0,2 UI:0,0,0
+S1:1,0,1 S1:1,1,2 UC:0,1,2 UC:0,1,3 S1:1,1,0 UI:0,0,1 S1:1,0,0 UI:0,1,0 UI:0,1,1 UE:1,0,1 UE:1,1,2 UQ:0,1,0 UQ:0,0,0 S2:1,0
+S2:0,1 UE:1,0,0 AD:0,1 S2:0,2 UE:1,1,0 S1:1,0,3 SE:0,2 S1:1,1,1 AD:0,2 S2:0,0 S1:1,1,3 AD:1,0 UE:1,0,3 UC:1,1,2
+UC:1,0,1 UC:1,1,0 UE:1,1,1 S2:1,1 UQ:0,0,1 UQ:0,1,1 UC:1,0,3 UC:1,0,0 AD:0,0 UC:1,0,2 UE:1,1,3 UI:1,0,1 UC:1,1,1 S2:2,0
+UC:1,1,3 S2:1,2 UI:1,0,0 AD:1,1 SE:1,2 AD:1,2 AD:2,0 UQ:1,0,0 S2:2,1 AD:2,1 UI:1,1,0 S2:2,2 S2:3,0 SE:2,2
+S2:3,2 UQ:1,0,1 SE:3,2 UQ:1,1,0 S2:4,2 S2:5,0 AD:3,0 UI:1,1,1 AD:2,2 UQ:1,1,1 S2:5,2 SE:4,2 AD:4,2 AD:5,0
+S2:3,1 SE:5,2 S2:4,1 S2:4,0 AD:3,1 S2:5,1 S2:6,2 AD:4,1 AD:3,2 S2:6,0 AD:4,0 AD:5,1 S2:7,2 S2:7,0
+AD:5,2 AD:6,0 AD:7,0 SE:6,2 SE:7,2 S2:7,1 S2:6,1 AD:6,2 AD:7,2 AD:7,1 AD:6,1
+"""
+VF = ()
+UIV = 1
+GP = ((0, 2), (1, 2), (2, 2), (3, 2), (4, 2), (5, 2), (6, 2), (7, 2),)
+
+
+def tile_clipped_feedback_control_s3_kernel(
+    tc, x_bytes, x_scale, e, F, L_words, L_scales, lo, hi, B_words, B_scales, drift, out
+):
+    nc = tc.nc
+    with ExitStack() as ctx:
+        keep = ctx.enter_context(tc.tile_pool(name="keep", bufs=1))
+        stage = ctx.enter_context(tc.tile_pool(name="stage", bufs=4))
+        psa = ctx.enter_context(tc.psum_pool(name="psa", bufs=4))
+        psb = ctx.enter_context(tc.psum_pool(name="psb", bufs=4))
+
+        ident = keep.tile([P, P], F32, name="ident")
+        make_identity(nc, ident[:])
+        lim_bf = [keep.tile([P, 2, 4], BF16, name=f"lim_bf{k}") for k in range(2)]
+        nc.gpsimd.dma_start(out=lim_bf[0][:], in_=hi.rearrange("(g p t) -> p g t", p=P, t=4))
+        nc.gpsimd.dma_start(out=lim_bf[1][:], in_=lo.rearrange("(g p t) -> p g t", p=P, t=4))
+        l_plane = keep.tile([P, A], U8, name="l_plane", align_bytes=64)
+        b_plane = keep.tile([P, 2, S], U8, name="b_plane", align_bytes=64)
+        nc.vector.memset(l_plane[:].bitcast(I32), 0)
+        nc.vector.memset(b_plane[:].rearrange("p g n -> p (g n)").bitcast(I32), 0)
+
+        l_raw = keep.tile([P, 2 * A], U8, name="l_raw")
+        scale_bc = keep.tile([P, S], F32, name="scale_bc")
+        xb = [keep.tile([P, 2, S], U8, name=f"xb{j}") for j in range(4)]
+        eb = [keep.tile([P, 4, E], BF16, name=f"eb{h}") for h in range(2)]
+        fr = [[keep.tile([P, 4, 512], BF16, name=f"fr{c}{g}") for g in range(2)] for c in range(3)]
+        bw = keep.tile([P, 2, 2 * S], U8, name="bw", align_bytes=64)
+        dr = [keep.tile([P, S], BF16, name=f"dr{i}") for i in range(8)]
+
+        def ld_x(j):
+            nc.sync.dma_start(out=xb[j][:], in_=x_bytes[256 * j:256 * j + 256, :].rearrange("(i p) k -> p i k", p=P))
+
+        def ld_e(h):
+            nc.sync.dma_start(out=eb[h][:], in_=e[512 * h:512 * h + 512, :].rearrange("(i p) k -> p i k", p=P))
+
+        def ld_f(c, g):
+            nc.sync.dma_start(
+                out=fr[c][g][:],
+                in_=F[512 * c:512 * c + 512, 512 * g:512 * g + 512].rearrange("(p j) a -> p j a", j=4),
+            )
+
+        nc.sync.dma_start(out=l_raw[:], in_=L_words[0])
+        ld_f(0, 0)
+        ld_x(0)
+        nc.sync.dma_start(out=scale_bc[:], in_=x_scale.rearrange("o k -> (o k)").partition_broadcast(P))
+        for q in range(4):
+            nc.sync.dma_start(
+                out=l_plane[32 * q:32 * q + 4, :].bitcast(I32), in_=L_scales[0, 4 * q:4 * q + 4, :].bitcast(I32)
+            )
+        ld_f(1, 0)
+        ld_x(1)
+        ld_f(2, 0)
+        ld_e(0)
+        ld_f(0, 1)
+        ld_x(2)
+        ld_f(1, 1)
+        ld_x(3)
+        ld_f(2, 1)
+        ld_e(1)
+        nc.sync.dma_start(out=bw[:], in_=B_words.rearrange("g p n -> p g n"))
+        for q in range(4):
+            nc.sync.dma_start(
+                out=b_plane[32 * q:32 * q + 4, :, :].bitcast(I32),
+                in_=B_scales[:, 4 * q:4 * q + 4, :].rearrange("g q n -> q g n").bitcast(I32),
+            )
+        for i in range(8):
+            nc.sync.dma_start(out=dr[i][:], in_=drift[128 * i:128 * i + 128, :])
+
+        lim = keep.tile([P, 2, 2, 4], F32, name="lim")
+        lw = keep.tile([P, 2, 4, 256], U8, name="lw", align_bytes=64)
+        ls = keep.tile([P, 2, 4, P], U8, name="ls", align_bytes=64)
+        fq = [[keep.tile([P, 512], U32, name=f"fq{c}{g}", align_bytes=64) for g in range(2)] for c in range(3)]
+        fs = [[keep.tile([P, 512], U8, name=f"fs{c}{g}", align_bytes=64) for g in range(2)] for c in range(3)]
+        xq = [[keep.tile([P, 512], U32, name=f"xq{h}{c}", align_bytes=64) for c in range(4)] for h in range(2)]
+        xsc = [[keep.tile([P, 512], U8, name=f"xsc{h}{c}", align_bytes=64) for c in range(4)] for h in range(2)]
+        uq = [[keep.tile([P, 512], U32, name=f"uq{h}{g}", align_bytes=64) for g in range(2)] for h in range(2)]
+        us = [[keep.tile([P, 512], U8, name=f"us{h}{g}", align_bytes=64) for g in range(2)] for h in range(2)]
+        live = {}
+
+        def LW(g):
+            nc.vector.tensor_copy(
+                out=lw[:, g].rearrange("p t (m b) -> p t m b", b=2),
+                in_=l_raw[:, 1024 * g:1024 * g + 1024].rearrange("p (m t b) -> p t m b", t=4, b=2),
+            )
+
+        def LS(g):
+            nc.vector.tensor_copy(
+                out=ls[:, g], in_=l_plane[:, 512 * g:512 * g + 512].rearrange("p (m t) -> p t m", t=4)
+            )
+
+        def LM():
+            for k in range(2):
+                nc.vector.tensor_copy(out=lim[:, k], in_=lim_bf[k][:])
+
+        def X(i):
+            j = i // 2
+            xs = stage.tile([P, S], BF16, name=f"xs{i}", tag="xs", bufs=4)
+            live["xs", i] = xs
+            nc.vector.tensor_tensor(out=xs[:], in0=xb[j][:, i % 2, :].bitcast(FP8), in1=scale_bc[:], op=ALU.mult)
+
+        def XT(j, c):
+            bank = psb.tile([P, 2, 2, P], F32, name=f"xt{j}{c}", tag="b")
+            live["xt", j, c] = bank
+            for i in range(2):
+                src = live["xs", 2 * j + i][:] if c < 3 else eb[j // 2][:, 2 * (j % 2) + i, :]
+                words = src.bitcast(F32)
+                base = 256 * c if c < 3 else 0
+                for u in range(2):
+                    nc.tensor.transpose(bank[:, i, u, :], words[:, base + u:base + 256:2], ident[:])
+
+        def XE(j, c):
+            grp = stage.tile([P, 256, 4], BF16, name=f"xg{j}{c}", tag="xg", bufs=8, align_bytes=64)
+            live["xg", j, c] = grp
+            bank = live["xt", j, c]
+            nc.scalar.copy(
+                out=grp[:].bitcast(F32).rearrange("p (i r) u -> p i r u", i=2),
+                in_=bank[:].rearrange("p i u r -> p i r u"),
+            )
+
+        def XQ(j, c):
+            h, o = j // 2, 256 * (j % 2)
+            nc.vector.quantize_mx(
+                out=xq[h][c][:, o:o + 256].bitcast(FP8X4),
+                scales=xsc[h][c][:, o:o + 256],
+                in_=live["xg", j, c][:].rearrange("p m t -> p (m t)"),
+            )
+
+        def FI(c, g):
+            fg = stage.tile([P, 4, P, 4], BF16, name=f"fg{c}{g}", tag="fg", bufs=3, align_bytes=64)
+            live["fg", c, g] = fg
+            src = fr[c][g][:].rearrange("p j (m t) -> p t m j", t=4)
+            if (c, g) in VF:
+                nc.vector.tensor_copy(out=fg[:], in_=src)
+            else:
+                nc.scalar.copy(out=fg[:], in_=src)
+
+        def FQ(c, g):
+            nc.vector.quantize_mx(
+                out=fq[c][g][:].bitcast(FP8X4),
+                scales=fs[c][g][:],
+                in_=live["fg", c, g][:].rearrange("p t m j -> p (t m j)"),
+            )
+
+        def S1(h, g, t):
+            acc = psa.tile([P, 512], F32, name=f"acc{h}{g}{t}", tag="a")
+            live["acc", h, g, t] = acc
+            cols = slice(128 * t, 128 * t + 128)
+            for c in range(4):
+                if c < 3:
+                    w, ws = fq[c][g][:, cols].bitcast(FP8X4), fs[c][g][:, cols]
+                else:
+                    w, ws = lw[:, g, t, :].bitcast(FP4X4), ls[:, g, t, :]
+                nc.tensor.matmul_mx(
+                    out=acc[:], lhsT=w, lhsT_scale=ws,
+                    rhs=xq[h][c][:].bitcast(FP8X4), rhs_scale=xsc[h][c][:],
+                    start=(c == 0), stop=(c == 3),
+                )
+
+        def UE(h, g, t):
+            if ("up", h, g) not in live:
+                live["up", h, g] = stage.tile([P, 4, 512], BF16, name=f"up{h}{g}", tag="up", bufs=3)
+            nc.scalar.copy(out=live["up", h, g][:, t, :], in_=live["acc", h, g, t][:])
+
+        def UC(h, g, t):
+            u = live["up", h, g][:, t, :]
+            nc.vector.tensor_scalar(
+                out=u, in0=u, scalar1=lim[:, 0, g, t:t + 1], scalar2=lim[:, 1, g, t:t + 1], op0=ALU.min, op1=ALU.max
+            )
+
+        def UI(h, g, k):
+            if ("ug", h, g) not in live:
+                live["ug", h, g] = stage.tile([P, 512, 4], BF16, name=f"ug{h}{g}", tag="ug", bufs=2, align_bytes=64)
+            m = slice(256 * k, 256 * k + 256)
+            src = live["up", h, g][:, :, m].rearrange("p t m -> p m t")
+            dst = live["ug", h, g][:, m, :]
+            if k >= UIV:
+                nc.vector.tensor_copy(out=dst, in_=src)
+            else:
+                nc.scalar.copy(out=dst, in_=src)
+
+        def UQ(h, g, k):
+            m = slice(256 * k, 256 * k + 256)
+            nc.vector.quantize_mx(
+                out=uq[h][g][:, m].bitcast(FP8X4),
+                scales=us[h][g][:, m],
+                in_=live["ug", h, g][:, m, :].rearrange("p m t -> p (m t)"),
+            )
+
+        def S2(i, n):
+            h, cols = i // 4, slice(128 * (i % 4), 128 * (i % 4) + 128)
+            acc = psb.tile([P, 512], F32, name=f"y{i}{n}", tag="b")
+            live["y", i, n] = acc
+            for g in range(2):
+                nc.tensor.matmul_mx(
+                    out=acc[:],
+                    lhsT=uq[h][g][:, cols].bitcast(FP8X4), lhsT_scale=us[h][g][:, cols],
+                    rhs=bw[:, g, 1024 * n:1024 * n + 1024].bitcast(FP4X4),
+                    rhs_scale=b_plane[:, g, 512 * n:512 * n + 512],
+                    start=(g == 0), stop=(g == 1),
+                )
+
+        def SE(i, n):
+            ye = stage.tile([P, 512], F32, name=f"ye{i}{n}", tag="ye", bufs=3)
+            live["ye", i, n] = ye
+            nc.scalar.copy(out=ye[:], in_=live["y", i, n][:])
+
+        def AD(i, n):
+            cols = slice(512 * n, 512 * n + 512)
+            ot = stage.tile([P, 512], F32, name=f"ot{i}{n}", tag="ot", bufs=8)
+            if (i, n) in GP:
+                nc.gpsimd.tensor_tensor(out=ot[:], in0=live["ye", i, n][:], in1=dr[i][:, cols], op=ALU.add)
+            else:
+                nc.vector.tensor_tensor(out=ot[:], in0=live["y", i, n][:], in1=dr[i][:, cols], op=ALU.add)
+            nc.sync.dma_start(out=out[128 * i:128 * i + 128, cols], in_=ot[:])
+
+        steps = {"LW": LW, "LS": LS, "LM": LM, "X": X, "XT": XT, "XE": XE, "XQ": XQ, "FI": FI, "FQ": FQ, "S1": S1,
+                 "UE": UE, "UC": UC, "UI": UI, "UQ": UQ, "S2": S2, "SE": SE, "AD": AD}
+        with tc.manual_schedule():
+            for tok in SCRIPT.split():
+                name, args = tok.split(":")
+                steps[name](*[int(d) for d in args.split(",") if d != ""])

@@ -16,25 +16,9 @@ FP8X4 = mybir.dt.float8_e4m3fn_x4
 FP4X4 = mybir.dt.float4_e2m1fn_x4
 ALU = mybir.AluOpType
 P = 128
-SCRIPT = """
-LW:0 LW:1 X:1 X:0 FI:0,0 XT:0,0 XT:0,3 FI:1,0 XT:0,1 FI:2,0 XE:0,1 XE:0,0 XT:0,2 X:2
-LM: X:3 XE:0,2 LS:0 FQ:2,0 FQ:1,0 FQ:0,0 XT:1,2 XE:0,3 XT:1,0 X:5 LS:1 XQ:0,0 XE:1,2
-XT:1,3 FI:0,1 XE:1,3 XT:1,1 X:4 XE:1,1 XE:1,0 XQ:1,3 XQ:0,3 XQ:0,2 XQ:1,1 XT:2,0 XQ:1,0 FI:2,1
-FI:1,1 XQ:0,1 XQ:1,2 XT:2,1 XE:2,1 XT:2,2 XE:2,0 X:6 S1:0,0,0 X:7 S1:0,0,3 S1:0,0,2 S1:0,0,1 FQ:0,1
-XQ:2,1 UE:0,0,2 UE:0,0,0 XT:3,0 UE:0,0,3 XT:3,2 XE:2,2 FQ:1,1 FQ:2,1 XQ:2,0 XT:2,3 XE:3,0 UC:0,0,3 UE:0,0,1
-S1:0,1,0 UC:0,0,0 XE:2,3 XQ:2,2 XQ:3,0 S1:0,1,1 UE:0,1,0 UC:0,0,2 XT:3,3 XE:3,2 S1:0,1,2 XT:3,1 UC:0,0,1 UE:0,1,1
-XE:3,1 XQ:3,2 XQ:2,3 UC:0,1,0 XE:3,3 XQ:3,1 UC:0,1,1 UE:0,1,2 S1:0,1,3 XQ:3,3 S1:1,0,2 UE:0,1,3 UE:1,0,2 UI:0,0,0
-S1:1,0,1 S1:1,1,2 UC:0,1,2 UC:0,1,3 S1:1,1,0 UI:0,0,1 S1:1,0,0 UI:0,1,0 UI:0,1,1 UE:1,0,1 UE:1,1,2 UQ:0,1,0 UQ:0,0,0 S2:1,0
-S2:0,1 UE:1,0,0 AD:0,1 S2:0,2 UE:1,1,0 S1:1,0,3 SE:0,2 S1:1,1,1 AD:0,2 S2:0,0 S1:1,1,3 AD:1,0 UE:1,0,3 UC:1,1,2
-UC:1,0,1 UC:1,1,0 UE:1,1,1 S2:1,1 UQ:0,0,1 UQ:0,1,1 UC:1,0,3 UC:1,0,0 AD:0,0 UC:1,0,2 UE:1,1,3 UI:1,0,1 UC:1,1,1 S2:2,0
-UC:1,1,3 S2:1,2 UI:1,0,0 AD:1,1 SE:1,2 AD:1,2 AD:2,0 UQ:1,0,0 S2:2,1 AD:2,1 UI:1,1,0 S2:2,2 S2:3,0 SE:2,2
-S2:3,2 UQ:1,0,1 SE:3,2 UQ:1,1,0 S2:4,2 S2:5,0 AD:3,0 UI:1,1,1 AD:2,2 UQ:1,1,1 S2:5,2 SE:4,2 AD:4,2 AD:5,0
-S2:3,1 SE:5,2 S2:4,1 S2:4,0 AD:3,1 S2:5,1 S2:6,2 AD:4,1 AD:3,2 S2:6,0 AD:4,0 AD:5,1 S2:7,2 S2:7,0
-AD:5,2 AD:6,0 AD:7,0 SE:6,2 SE:7,2 S2:7,1 S2:6,1 AD:6,2 AD:7,2 AD:7,1 AD:6,1
-"""
-VF = ()
-UIV = 1
-GP = ((0, 2), (1, 2), (2, 2), (3, 2), (4, 2), (5, 2), (6, 2), (7, 2),)
+W = 512
+XP = S // W
+EP = XP
 
 
 def tile_clipped_feedback_control_s3_kernel(
@@ -44,216 +28,359 @@ def tile_clipped_feedback_control_s3_kernel(
     with ExitStack() as ctx:
         keep = ctx.enter_context(tc.tile_pool(name="keep", bufs=1))
         stage = ctx.enter_context(tc.tile_pool(name="stage", bufs=4))
-        psa = ctx.enter_context(tc.psum_pool(name="psa", bufs=4))
-        psb = ctx.enter_context(tc.psum_pool(name="psb", bufs=4))
+        psum = ctx.enter_context(tc.psum_pool(name="psum", bufs=4))
+        ctx.enter_context(tc.manual_schedule())
 
         ident = keep.tile([P, P], F32, name="ident")
         make_identity(nc, ident[:])
-        lim_bf = [keep.tile([P, 2, 4], BF16, name=f"lim_bf{k}") for k in range(2)]
-        nc.gpsimd.dma_start(out=lim_bf[0][:], in_=hi.rearrange("(g p t) -> p g t", p=P, t=4))
-        nc.gpsimd.dma_start(out=lim_bf[1][:], in_=lo.rearrange("(g p t) -> p g t", p=P, t=4))
+        ident_bf = keep.tile([P, P], BF16, name="ident_bf")
+        nc.vector.tensor_copy(out=ident_bf[:], in_=ident[:])
         l_plane = keep.tile([P, A], U8, name="l_plane", align_bytes=64)
         b_plane = keep.tile([P, 2, S], U8, name="b_plane", align_bytes=64)
         nc.vector.memset(l_plane[:].bitcast(I32), 0)
         nc.vector.memset(b_plane[:].rearrange("p g n -> p (g n)").bitcast(I32), 0)
 
-        l_raw = keep.tile([P, 2 * A], U8, name="l_raw")
-        scale_bc = keep.tile([P, S], F32, name="scale_bc")
+        scale_col = keep.tile([P, XP, 4], F32, name="scale_col")
+        scale_row = [keep.tile([P, W], F32, name=f"scale_row{c}") for c in range(XP)]
+        l_raw = [keep.tile([P, A], U8, name=f"l_raw{g}") for g in range(2)]
+        lim_bf = [keep.tile([P, 2, 4], BF16, name=f"lim_bf{k}") for k in range(2)]
         xb = [keep.tile([P, 2, S], U8, name=f"xb{j}") for j in range(4)]
-        eb = [keep.tile([P, 4, E], BF16, name=f"eb{h}") for h in range(2)]
-        fr = [[keep.tile([P, 4, 512], BF16, name=f"fr{c}{g}") for g in range(2)] for c in range(3)]
+        eb = [keep.tile([P, 2 * E], BF16, name=f"eb{j}") for j in range(4)]
+        fr = [[keep.tile([P, 4, W], BF16, name=f"fr{c}{g}") for g in range(2)] for c in range(XP)]
         bw = keep.tile([P, 2, 2 * S], U8, name="bw", align_bytes=64)
-        dr = [keep.tile([P, S], BF16, name=f"dr{i}") for i in range(8)]
+        dr = [keep.tile([P, 2, S], BF16, name=f"dr{j}") for j in range(4)]
 
-        def ld_x(j):
-            nc.sync.dma_start(out=xb[j][:], in_=x_bytes[256 * j:256 * j + 256, :].rearrange("(i p) k -> p i k", p=P))
+        def pair_rows(t, j):
+            return t[256 * j:256 * j + 256, :].rearrange("(p i) k -> p i k", i=2)
 
-        def ld_e(h):
-            nc.sync.dma_start(out=eb[h][:], in_=e[512 * h:512 * h + 512, :].rearrange("(i p) k -> p i k", p=P))
+        def load_x(j):
+            nc.sync.dma_start(out=xb[j][:], in_=pair_rows(x_bytes, j))
 
-        def ld_f(c, g):
+        def load_e(j):
+            nc.sync.dma_start(out=eb[j][:], in_=pair_rows(e, j).rearrange("p i k -> p (i k)"))
+
+        def load_l(g):
+            nc.sync.dma_start(out=l_raw[g][:], in_=L_words[0, :, A * g:A * g + A])
+
+        def load_f(c, g):
             nc.sync.dma_start(
-                out=fr[c][g][:],
-                in_=F[512 * c:512 * c + 512, 512 * g:512 * g + 512].rearrange("(p j) a -> p j a", j=4),
+                out=fr[c][g][:], in_=F[W * c:W * c + W, W * g:W * g + W].rearrange("(p j) a -> p j a", j=4)
             )
 
-        nc.sync.dma_start(out=l_raw[:], in_=L_words[0])
-        ld_f(0, 0)
-        ld_x(0)
-        nc.sync.dma_start(out=scale_bc[:], in_=x_scale.rearrange("o k -> (o k)").partition_broadcast(P))
+        nc.sync.dma_start(out=scale_col[:], in_=x_scale.rearrange("o (c p j) -> p (o c) j", p=P, j=4))
+        load_l(0)
+        load_x(0)
+        load_f(0, 0)
+        load_x(1)
+        load_f(1, 0)
+        load_e(0)
+        load_e(1)
+        load_f(2, 0)
         for q in range(4):
             nc.sync.dma_start(
                 out=l_plane[32 * q:32 * q + 4, :].bitcast(I32), in_=L_scales[0, 4 * q:4 * q + 4, :].bitcast(I32)
             )
-        ld_f(1, 0)
-        ld_x(1)
-        ld_f(2, 0)
-        ld_e(0)
-        ld_f(0, 1)
-        ld_x(2)
-        ld_f(1, 1)
-        ld_x(3)
-        ld_f(2, 1)
-        ld_e(1)
+        nc.sync.dma_start(out=lim_bf[0][:], in_=hi.rearrange("(g p t) -> p g t", p=P, t=4))
+        nc.sync.dma_start(out=lim_bf[1][:], in_=lo.rearrange("(g p t) -> p g t", p=P, t=4))
+        load_f(0, 1)
+        load_f(1, 1)
+        load_x(2)
+        load_f(2, 1)
+        load_x(3)
+        load_l(1)
+        load_e(2)
+        load_e(3)
         nc.sync.dma_start(out=bw[:], in_=B_words.rearrange("g p n -> p g n"))
         for q in range(4):
             nc.sync.dma_start(
                 out=b_plane[32 * q:32 * q + 4, :, :].bitcast(I32),
                 in_=B_scales[:, 4 * q:4 * q + 4, :].rearrange("g q n -> q g n").bitcast(I32),
             )
-        for i in range(8):
-            nc.sync.dma_start(out=dr[i][:], in_=drift[128 * i:128 * i + 128, :])
+        for j in range(4):
+            nc.sync.dma_start(out=dr[j][:], in_=pair_rows(drift, j))
 
         lim = keep.tile([P, 2, 2, 4], F32, name="lim")
         lw = keep.tile([P, 2, 4, 256], U8, name="lw", align_bytes=64)
         ls = keep.tile([P, 2, 4, P], U8, name="ls", align_bytes=64)
-        fq = [[keep.tile([P, 512], U32, name=f"fq{c}{g}", align_bytes=64) for g in range(2)] for c in range(3)]
-        fs = [[keep.tile([P, 512], U8, name=f"fs{c}{g}", align_bytes=64) for g in range(2)] for c in range(3)]
-        xq = [[keep.tile([P, 512], U32, name=f"xq{h}{c}", align_bytes=64) for c in range(4)] for h in range(2)]
-        xsc = [[keep.tile([P, 512], U8, name=f"xsc{h}{c}", align_bytes=64) for c in range(4)] for h in range(2)]
-        uq = [[keep.tile([P, 512], U32, name=f"uq{h}{g}", align_bytes=64) for g in range(2)] for h in range(2)]
-        us = [[keep.tile([P, 512], U8, name=f"us{h}{g}", align_bytes=64) for g in range(2)] for h in range(2)]
+        fq = [[keep.tile([P, W], U32, name=f"fq{c}{g}", align_bytes=64) for g in range(2)] for c in range(XP)]
+        fs = [[keep.tile([P, W], U8, name=f"fs{c}{g}", align_bytes=64) for g in range(2)] for c in range(XP)]
+        xq = [[keep.tile([P, W], U32, name=f"xq{h}{c}", align_bytes=64) for c in range(XP + 1)] for h in range(2)]
+        xs = [[keep.tile([P, W], U8, name=f"xs{h}{c}", align_bytes=64) for c in range(XP + 1)] for h in range(2)]
+        uq = [[keep.tile([P, W], U32, name=f"uq{h}{g}", align_bytes=64) for g in range(2)] for h in range(2)]
+        us = [[keep.tile([P, W], U8, name=f"us{h}{g}", align_bytes=64) for g in range(2)] for h in range(2)]
         live = {}
 
-        def LW(g):
+        def spread_scales(c):
+            bank = psum.tile([P, 4, P], F32, name=f"sb{c}", tag="turn")
+            for j in range(4):
+                nc.tensor.transpose(bank[:, j, :], scale_col[:, c, j:j + 1].to_broadcast([P, P]), ident[:])
+            nc.scalar.copy(out=scale_row[c][:].rearrange("p (m j) -> p m j", j=4), in_=bank[:].rearrange("p j m -> p m j"))
+
+        def permute_l_words(g):
             nc.vector.tensor_copy(
-                out=lw[:, g].rearrange("p t (m b) -> p t m b", b=2),
-                in_=l_raw[:, 1024 * g:1024 * g + 1024].rearrange("p (m t b) -> p t m b", t=4, b=2),
+                out=lw[:, g].rearrange("p t (m b) -> p m t b", b=2),
+                in_=l_raw[g][:].rearrange("p (m t b) -> p m t b", t=4, b=2),
             )
 
-        def LS(g):
+        def permute_l_scales(g):
             nc.vector.tensor_copy(
-                out=ls[:, g], in_=l_plane[:, 512 * g:512 * g + 512].rearrange("p (m t) -> p t m", t=4)
+                out=ls[:, g].rearrange("p t m -> p m t"),
+                in_=l_plane[:, W * g:W * g + W].rearrange("p (m t) -> p m t", t=4),
             )
 
-        def LM():
+        def widen_limits():
             for k in range(2):
                 nc.vector.tensor_copy(out=lim[:, k], in_=lim_bf[k][:])
 
-        def X(i):
-            j = i // 2
-            xs = stage.tile([P, S], BF16, name=f"xs{i}", tag="xs", bufs=4)
-            live["xs", i] = xs
-            nc.vector.tensor_tensor(out=xs[:], in0=xb[j][:, i % 2, :].bitcast(FP8), in1=scale_bc[:], op=ALU.mult)
-
-        def XT(j, c):
-            bank = psb.tile([P, 2, 2, P], F32, name=f"xt{j}{c}", tag="b")
-            live["xt", j, c] = bank
+        def scale_x(j, c):
             for i in range(2):
-                src = live["xs", 2 * j + i][:] if c < 3 else eb[j // 2][:, 2 * (j % 2) + i, :]
-                words = src.bitcast(F32)
-                base = 256 * c if c < 3 else 0
-                for u in range(2):
-                    nc.tensor.transpose(bank[:, i, u, :], words[:, base + u:base + 256:2], ident[:])
-
-        def XE(j, c):
-            grp = stage.tile([P, 256, 4], BF16, name=f"xg{j}{c}", tag="xg", bufs=8, align_bytes=64)
-            live["xg", j, c] = grp
-            bank = live["xt", j, c]
-            nc.scalar.copy(
-                out=grp[:].bitcast(F32).rearrange("p (i r) u -> p i r u", i=2),
-                in_=bank[:].rearrange("p i u r -> p i r u"),
-            )
-
-        def XQ(j, c):
-            h, o = j // 2, 256 * (j % 2)
-            nc.vector.quantize_mx(
-                out=xq[h][c][:, o:o + 256].bitcast(FP8X4),
-                scales=xsc[h][c][:, o:o + 256],
-                in_=live["xg", j, c][:].rearrange("p m t -> p (m t)"),
-            )
-
-        def FI(c, g):
-            fg = stage.tile([P, 4, P, 4], BF16, name=f"fg{c}{g}", tag="fg", bufs=3, align_bytes=64)
-            live["fg", c, g] = fg
-            src = fr[c][g][:].rearrange("p j (m t) -> p t m j", t=4)
-            if (c, g) in VF:
-                nc.vector.tensor_copy(out=fg[:], in_=src)
-            else:
-                nc.scalar.copy(out=fg[:], in_=src)
-
-        def FQ(c, g):
-            nc.vector.quantize_mx(
-                out=fq[c][g][:].bitcast(FP8X4),
-                scales=fs[c][g][:],
-                in_=live["fg", c, g][:].rearrange("p t m j -> p (t m j)"),
-            )
-
-        def S1(h, g, t):
-            acc = psa.tile([P, 512], F32, name=f"acc{h}{g}{t}", tag="a")
-            live["acc", h, g, t] = acc
-            cols = slice(128 * t, 128 * t + 128)
-            for c in range(4):
-                if c < 3:
-                    w, ws = fq[c][g][:, cols].bitcast(FP8X4), fs[c][g][:, cols]
-                else:
-                    w, ws = lw[:, g, t, :].bitcast(FP4X4), ls[:, g, t, :]
-                nc.tensor.matmul_mx(
-                    out=acc[:], lhsT=w, lhsT_scale=ws,
-                    rhs=xq[h][c][:].bitcast(FP8X4), rhs_scale=xsc[h][c][:],
-                    start=(c == 0), stop=(c == 3),
+                xv = stage.tile([P, W], BF16, name=f"xv{j}{c}{i}", tag="xv", bufs=8)
+                live["xv", j, c, i] = xv
+                nc.vector.tensor_tensor(
+                    out=xv[:], in0=xb[j][:, i, W * c:W * c + W].bitcast(FP8), in1=scale_row[c][:], op=ALU.mult
                 )
 
-        def UE(h, g, t):
-            if ("up", h, g) not in live:
-                live["up", h, g] = stage.tile([P, 4, 512], BF16, name=f"up{h}{g}", tag="up", bufs=3)
-            nc.scalar.copy(out=live["up", h, g][:, t, :], in_=live["acc", h, g, t][:])
+        def turn(j, c):
+            bank = psum.tile([P, 2, 2, P], F32, name=f"xt{j}{c}", tag="turn")
+            live["xt", j, c] = bank
+            for i in range(2):
+                src = live["xv", j, c, i][:] if c < XP else eb[j][:, E * i:E * i + E]
+                words = src.bitcast(F32)
+                for u in range(2):
+                    nc.tensor.transpose(bank[:, i, u, :], words[:, u::2], ident[:])
 
-        def UC(h, g, t):
+        def empty_turn(j, c):
+            h, half = divmod(j, 2)
+            if half == 0:
+                live["xg", h, c] = stage.tile([P, 4 * W], BF16, name=f"xg{h}{c}", tag="xg", bufs=4, align_bytes=64)
+            dst = live["xg", h, c][:, 2 * W * half:2 * W * half + 2 * W]
+            nc.scalar.copy(
+                out=dst.bitcast(F32).rearrange("p (i r u) -> p i r u", i=2, u=2),
+                in_=live["xt", j, c][:].rearrange("p i u r -> p i r u"),
+            )
+
+        def quantize_x(h, c):
+            nc.vector.quantize_mx(out=xq[h][c][:].bitcast(FP8X4), scales=xs[h][c][:], in_=live["xg", h, c][:])
+
+        def interleave_f(c, g, on_vector=False):
+            fg = stage.tile([P, 4 * W], BF16, name=f"fg{c}{g}", tag="fg", bufs=3, align_bytes=64)
+            live["fg", c, g] = fg
+            src = fr[c][g][:].rearrange("p j (m t) -> p m j t", t=4)
+            dst = fg[:].rearrange("p (t m j) -> p m j t", t=4, j=4)
+            if on_vector:
+                nc.vector.tensor_copy(out=dst, in_=src)
+            else:
+                nc.scalar.copy(out=dst, in_=src)
+
+        def pair_f(c, g, k):
+            if k == 0:
+                live["fg", c, g] = stage.tile([P, 4 * W], BF16, name=f"fg{c}{g}", tag="fg", bufs=3, align_bytes=64)
+            bank = psum.tile([P, 2, W], BF16, name=f"fp{c}{g}{k}", tag="turn")
+            live["fp", c, g, k] = bank
+            for u in range(2):
+                nc.tensor.matmul(
+                    bank[:, u, :], lhsT=ident_bf[:],
+                    rhs=fr[c][g][:, 2 * u:2 * u + 2, 256 * k:256 * k + 256].rearrange("p e a -> p a e"),
+                    start=True, stop=True,
+                )
+
+        def empty_pairs(c, g, k):
+            dst = live["fg", c, g][:].bitcast(F32).rearrange("p (t m u) -> p t m u", t=4, u=2)
+            src = live["fp", c, g, k][:].bitcast(F32).rearrange("p u (m t) -> p t m u", t=4)
+            nc.scalar.copy(out=dst[:, :, 64 * k:64 * k + 64, :], in_=src)
+
+        def weave_f(c, g):
+            for k in range(2):
+                pair_f(c, g, k)
+                empty_pairs(c, g, k)
+
+        def quantize_f(c, g):
+            nc.vector.quantize_mx(out=fq[c][g][:].bitcast(FP8X4), scales=fs[c][g][:], in_=live["fg", c, g][:])
+
+        def action_pass(h, g, t, c, order):
+            if c == order[0]:
+                live["acc", h, g, t] = psum.tile([P, W], F32, name=f"acc{h}{g}{t}", tag="acc")
+            cols = slice(P * t, P * t + P)
+            if c < XP:
+                w, ws = fq[c][g][:, cols].bitcast(FP8X4), fs[c][g][:, cols]
+            else:
+                w, ws = lw[:, g, t, :].bitcast(FP4X4), ls[:, g, t, :]
+            nc.tensor.matmul_mx(
+                out=live["acc", h, g, t][:], lhsT=w, lhsT_scale=ws,
+                rhs=xq[h][c][:].bitcast(FP8X4), rhs_scale=xs[h][c][:],
+                start=(c == order[0]), stop=(c == order[-1]),
+            )
+
+        def action(h, g, t):
+            for c in range(XP + 1):
+                action_pass(h, g, t, c, range(XP + 1))
+
+        def empty_action(h, g, t, on_vector=False):
+            if t == 0:
+                live["up", h, g] = stage.tile([P, 4, W], BF16, name=f"up{h}{g}", tag="up", bufs=4)
+            u = live["up", h, g][:, t, :]
+            if on_vector:
+                nc.vector.tensor_scalar(
+                    out=u, in0=live["acc", h, g, t][:], scalar1=lim[:, 0, g, t:t + 1], scalar2=lim[:, 1, g, t:t + 1],
+                    op0=ALU.min, op1=ALU.max,
+                )
+            else:
+                nc.scalar.copy(out=u, in_=live["acc", h, g, t][:])
+
+        def clip(h, g, t):
             u = live["up", h, g][:, t, :]
             nc.vector.tensor_scalar(
                 out=u, in0=u, scalar1=lim[:, 0, g, t:t + 1], scalar2=lim[:, 1, g, t:t + 1], op0=ALU.min, op1=ALU.max
             )
 
-        def UI(h, g, k):
-            if ("ug", h, g) not in live:
-                live["ug", h, g] = stage.tile([P, 512, 4], BF16, name=f"ug{h}{g}", tag="ug", bufs=2, align_bytes=64)
-            m = slice(256 * k, 256 * k + 256)
-            src = live["up", h, g][:, :, m].rearrange("p t m -> p m t")
-            dst = live["ug", h, g][:, m, :]
-            if k >= UIV:
+        def interleave_u(h, g, k, on_vector=False):
+            ug = stage.tile([P, 2 * W], BF16, name=f"ug{h}{g}{k}", tag="ug", bufs=4, align_bytes=64)
+            live["ug", h, g, k] = ug
+            src = live["up", h, g][:, :, 256 * k:256 * k + 256].rearrange("p t (c i) -> p c t i", i=4)
+            dst = ug[:].rearrange("p (c i t) -> p c t i", i=4, t=4)
+            if on_vector:
                 nc.vector.tensor_copy(out=dst, in_=src)
             else:
                 nc.scalar.copy(out=dst, in_=src)
 
-        def UQ(h, g, k):
+        def quantize_u(h, g, k):
             m = slice(256 * k, 256 * k + 256)
-            nc.vector.quantize_mx(
-                out=uq[h][g][:, m].bitcast(FP8X4),
-                scales=us[h][g][:, m],
-                in_=live["ug", h, g][:, m, :].rearrange("p m t -> p (m t)"),
-            )
+            nc.vector.quantize_mx(out=uq[h][g][:, m].bitcast(FP8X4), scales=us[h][g][:, m], in_=live["ug", h, g, k][:])
 
-        def S2(i, n):
-            h, cols = i // 4, slice(128 * (i % 4), 128 * (i % 4) + 128)
-            acc = psb.tile([P, 512], F32, name=f"y{i}{n}", tag="b")
+        def rate(i, n, tag):
+            h, cols = i // 4, slice(P * (i % 4), P * (i % 4) + P)
+            acc = psum.tile([P, W], F32, name=f"y{i}{n}", tag=tag)
             live["y", i, n] = acc
             for g in range(2):
                 nc.tensor.matmul_mx(
                     out=acc[:],
                     lhsT=uq[h][g][:, cols].bitcast(FP8X4), lhsT_scale=us[h][g][:, cols],
-                    rhs=bw[:, g, 1024 * n:1024 * n + 1024].bitcast(FP4X4),
-                    rhs_scale=b_plane[:, g, 512 * n:512 * n + 512],
+                    rhs=bw[:, g, 2 * W * n:2 * W * n + 2 * W].bitcast(FP4X4),
+                    rhs_scale=b_plane[:, g, W * n:W * n + W],
                     start=(g == 0), stop=(g == 1),
                 )
 
-        def SE(i, n):
-            ye = stage.tile([P, 512], F32, name=f"ye{i}{n}", tag="ye", bufs=3)
-            live["ye", i, n] = ye
-            nc.scalar.copy(out=ye[:], in_=live["y", i, n][:])
+        def add_drift(i, n):
+            cols = slice(W * n, W * n + W)
+            if n == 0:
+                live["ot", i] = stage.tile([P, S], F32, name=f"ot{i}", tag="ot", bufs=4)
+            ot = live["ot", i]
+            nc.vector.tensor_tensor(out=ot[:, cols], in0=live["y", i, n][:], in1=dr[i // 2][:, i % 2, cols], op=ALU.add)
+            rows = pair_rows(out, i // 2)[:, i % 2, :]
+            if i >= 6:
+                nc.sync.dma_start(out=rows[:, cols], in_=ot[:, cols])
+            elif n == 2:
+                nc.sync.dma_start(out=rows, in_=ot[:])
 
-        def AD(i, n):
-            cols = slice(512 * n, 512 * n + 512)
-            ot = stage.tile([P, 512], F32, name=f"ot{i}{n}", tag="ot", bufs=8)
-            if (i, n) in GP:
-                nc.gpsimd.tensor_tensor(out=ot[:], in0=live["ye", i, n][:], in1=dr[i][:, cols], op=ALU.add)
-            else:
-                nc.vector.tensor_tensor(out=ot[:], in0=live["y", i, n][:], in1=dr[i][:, cols], op=ALU.add)
-            nc.sync.dma_start(out=out[128 * i:128 * i + 128, cols], in_=ot[:])
+        def samples_pass(h, c):
+            for j in (2 * h, 2 * h + 1):
+                if c < XP:
+                    scale_x(j, c)
+                turn(j, c)
+                empty_turn(j, c)
 
-        steps = {"LW": LW, "LS": LS, "LM": LM, "X": X, "XT": XT, "XE": XE, "XQ": XQ, "FI": FI, "FQ": FQ, "S1": S1,
-                 "UE": UE, "UC": UC, "UI": UI, "UQ": UQ, "S2": S2, "SE": SE, "AD": AD}
-        with tc.manual_schedule():
-            for tok in SCRIPT.split():
-                name, args = tok.split(":")
-                steps[name](*[int(d) for d in args.split(",") if d != ""])
+        def block_pass(h, g, c, order):
+            for t in range(4):
+                action_pass(h, g, t, c, order)
+
+        def turn_pass(h, c):
+            for j in (2 * h, 2 * h + 1):
+                turn(j, c)
+                empty_turn(j, c)
+
+        def scale_pass(h, c):
+            for j in (2 * h, 2 * h + 1):
+                scale_x(j, c)
+
+        order = (0, 1, EP, 2)
+        for c in range(XP):
+            spread_scales(c)
+        permute_l_words(0)
+        weave_f(0, 0)
+        samples_pass(0, 0)
+        weave_f(1, 0)
+        samples_pass(0, 1)
+        quantize_f(0, 0)
+        quantize_x(0, 0)
+        interleave_f(2, 0)
+        scale_pass(0, 2)
+        turn_pass(0, EP)
+        block_pass(0, 0, 0, order)
+        turn_pass(0, 2)
+        quantize_f(1, 0)
+        quantize_x(0, 1)
+        weave_f(0, 1)
+        permute_l_scales(0)
+        quantize_x(0, EP)
+        widen_limits()
+        block_pass(0, 0, 1, order)
+        quantize_f(2, 0)
+        quantize_x(0, 2)
+        weave_f(1, 1)
+        block_pass(0, 0, EP, order)
+        interleave_f(2, 1)
+        block_pass(0, 0, 2, order)
+        permute_l_words(1)
+        permute_l_scales(1)
+        quantize_f(0, 1)
+        quantize_f(1, 1)
+        scale_x(2, 0)
+        quantize_f(2, 1)
+        scale_x(3, 0)
+        for j in (2, 3):
+            turn(j, EP)
+        for t in range(4):
+            empty_action(0, 0, t)
+        for j in (2, 3):
+            empty_turn(j, EP)
+        action(0, 1, 0)
+        for c in range(XP):
+            turn_pass(1, c)
+            if c + 1 < XP:
+                scale_pass(1, c + 1)
+            quantize_x(1, (EP, 0, 1)[c])
+            action(0, 1, c + 1)
+        for t in range(4):
+            clip(0, 0, t)
+        quantize_x(1, 2)
+        for t in range(4):
+            empty_action(0, 1, t)
+            action(1, 0, t)
+        for k in range(2):
+            interleave_u(0, 0, k, True)
+        for t in range(4):
+            clip(0, 1, t)
+        for k in range(2):
+            quantize_u(0, 0, k)
+        for k in range(2):
+            interleave_u(0, 1, k, k == 1)
+        steps = [(i, n) for i in range(8) for n in range(3)]
+        early = 6
+        for t in range(4):
+            empty_action(1, 0, t)
+        for k in range(2):
+            quantize_u(0, 1, k)
+        for t in range(4):
+            clip(1, 0, t)
+        for k in range(2):
+            interleave_u(1, 0, k, k == 1)
+        for t in range(4):
+            action(1, 1, t)
+            empty_action(1, 1, t)
+            if t < 3:
+                for i, n in steps[2 * t:2 * t + 2]:
+                    rate(i, n, "turn")
+                    add_drift(i, n)
+            if t < 2:
+                quantize_u(1, 0, 1 - t)
+            if t > 0:
+                clip(1, 1, t - 1)
+        for s, (i, n) in list(enumerate(steps))[early:]:
+            rate(i, n, "turn" if s % 2 == 0 else "acc")
+            add_drift(i, n)
+            if s == early:
+                clip(1, 1, 3)
+                interleave_u(1, 1, 0)
+                interleave_u(1, 1, 1)
+            if s in (early + 3, early + 5):
+                quantize_u(1, 1, (s - early - 3) // 2)

@@ -33,8 +33,6 @@ def tile_clipped_feedback_control_s3_kernel(
 
         ident = keep.tile([P, P], F32, name="ident")
         make_identity(nc, ident[:])
-        ident_bf = keep.tile([P, P], BF16, name="ident_bf")
-        nc.vector.tensor_copy(out=ident_bf[:], in_=ident[:])
         l_plane = keep.tile([P, A], U8, name="l_plane", align_bytes=64)
         b_plane = keep.tile([P, 2, S], U8, name="b_plane", align_bytes=64)
         nc.vector.memset(l_plane[:].bitcast(I32), 0)
@@ -82,12 +80,12 @@ def tile_clipped_feedback_control_s3_kernel(
             )
         nc.sync.dma_start(out=lim_bf[0][:], in_=hi.rearrange("(g p t) -> p g t", p=P, t=4))
         nc.sync.dma_start(out=lim_bf[1][:], in_=lo.rearrange("(g p t) -> p g t", p=P, t=4))
+        load_l(1)
         load_f(0, 1)
-        load_f(1, 1)
         load_x(2)
+        load_f(1, 1)
         load_f(2, 1)
         load_x(3)
-        load_l(1)
         load_e(2)
         load_e(3)
         nc.sync.dma_start(out=bw[:], in_=B_words.rearrange("g p n -> p g n"))
@@ -171,28 +169,6 @@ def tile_clipped_feedback_control_s3_kernel(
                 nc.vector.tensor_copy(out=dst, in_=src)
             else:
                 nc.scalar.copy(out=dst, in_=src)
-
-        def pair_f(c, g, k):
-            if k == 0:
-                live["fg", c, g] = stage.tile([P, 4 * W], BF16, name=f"fg{c}{g}", tag="fg", bufs=3, align_bytes=64)
-            bank = psum.tile([P, 2, W], BF16, name=f"fp{c}{g}{k}", tag="turn")
-            live["fp", c, g, k] = bank
-            for u in range(2):
-                nc.tensor.matmul(
-                    bank[:, u, :], lhsT=ident_bf[:],
-                    rhs=fr[c][g][:, 2 * u:2 * u + 2, 256 * k:256 * k + 256].rearrange("p e a -> p a e"),
-                    start=True, stop=True,
-                )
-
-        def empty_pairs(c, g, k):
-            dst = live["fg", c, g][:].bitcast(F32).rearrange("p (t m u) -> p t m u", t=4, u=2)
-            src = live["fp", c, g, k][:].bitcast(F32).rearrange("p u (m t) -> p t m u", t=4)
-            nc.scalar.copy(out=dst[:, :, 64 * k:64 * k + 64, :], in_=src)
-
-        def weave_f(c, g):
-            for k in range(2):
-                pair_f(c, g, k)
-                empty_pairs(c, g, k)
 
         def quantize_f(c, g):
             nc.vector.quantize_mx(out=fq[c][g][:].bitcast(FP8X4), scales=fs[c][g][:], in_=live["fg", c, g][:])
@@ -296,45 +272,45 @@ def tile_clipped_feedback_control_s3_kernel(
         for c in range(XP):
             spread_scales(c)
         permute_l_words(0)
-        weave_f(0, 0)
+        interleave_f(0, 0)
         samples_pass(0, 0)
-        weave_f(1, 0)
+        interleave_f(1, 0)
         samples_pass(0, 1)
         quantize_f(0, 0)
         quantize_x(0, 0)
+        turn_pass(0, EP)
         interleave_f(2, 0)
         scale_pass(0, 2)
-        turn_pass(0, EP)
         block_pass(0, 0, 0, order)
         turn_pass(0, 2)
         quantize_f(1, 0)
         quantize_x(0, 1)
-        weave_f(0, 1)
-        permute_l_scales(0)
         quantize_x(0, EP)
+        permute_l_scales(0)
         widen_limits()
         block_pass(0, 0, 1, order)
+        block_pass(0, 0, EP, order)
+        interleave_f(0, 1)
+        permute_l_words(1)
         quantize_f(2, 0)
         quantize_x(0, 2)
-        weave_f(1, 1)
-        block_pass(0, 0, EP, order)
-        interleave_f(2, 1)
         block_pass(0, 0, 2, order)
-        permute_l_words(1)
+        interleave_f(1, 1)
+        interleave_f(2, 1, True)
         permute_l_scales(1)
         quantize_f(0, 1)
-        quantize_f(1, 1)
-        scale_x(2, 0)
         quantize_f(2, 1)
-        scale_x(3, 0)
+        scale_x(2, 0)
+        quantize_f(1, 1)
         for j in (2, 3):
             turn(j, EP)
-        for t in range(4):
-            empty_action(0, 0, t)
+        empty_action(0, 0, 0)
         for j in (2, 3):
             empty_turn(j, EP)
+        scale_x(3, 0)
         action(0, 1, 0)
         for c in range(XP):
+            empty_action(0, 0, c + 1)
             turn_pass(1, c)
             if c + 1 < XP:
                 scale_pass(1, c + 1)

@@ -11,6 +11,7 @@ BF16 = mybir.dt.bfloat16
 U32 = mybir.dt.uint32
 I32 = mybir.dt.int32
 U8 = mybir.dt.uint8
+U16 = mybir.dt.uint16
 FP8 = mybir.dt.float8_e4m3fn
 FP8X4 = mybir.dt.float8_e4m3fn_x4
 FP4X4 = mybir.dt.float4_e2m1fn_x4
@@ -66,28 +67,28 @@ def tile_clipped_feedback_control_s3_kernel(
             )
 
         nc.sync.dma_start(out=scale_col[:], in_=x_scale.rearrange("o (c p j) -> p (o c) j", p=P, j=4))
-        load_l(0)
         load_x(0)
-        load_f(0, 0)
-        load_x(1)
-        load_f(1, 0)
         load_e(0)
         load_e(1)
-        load_f(2, 0)
+        load_l(0)
         for q in range(4):
             nc.sync.dma_start(
                 out=l_plane[32 * q:32 * q + 4, :].bitcast(I32), in_=L_scales[0, 4 * q:4 * q + 4, :].bitcast(I32)
             )
-        nc.sync.dma_start(out=lim_bf[0][:], in_=hi.rearrange("(g p t) -> p g t", p=P, t=4))
-        nc.sync.dma_start(out=lim_bf[1][:], in_=lo.rearrange("(g p t) -> p g t", p=P, t=4))
-        load_l(1)
-        load_f(0, 1)
-        load_x(2)
-        load_f(1, 1)
-        load_f(2, 1)
-        load_x(3)
+        load_f(0, 0)
+        load_x(1)
+        load_f(1, 0)
+        load_f(2, 0)
         load_e(2)
         load_e(3)
+        load_x(2)
+        nc.sync.dma_start(out=lim_bf[0][:], in_=hi.rearrange("(g p t) -> p g t", p=P, t=4))
+        nc.sync.dma_start(out=lim_bf[1][:], in_=lo.rearrange("(g p t) -> p g t", p=P, t=4))
+        load_x(3)
+        load_f(0, 1)
+        load_l(1)
+        load_f(1, 1)
+        load_f(2, 1)
         nc.sync.dma_start(out=bw[:], in_=B_words.rearrange("g p n -> p g n"))
         for q in range(4):
             nc.sync.dma_start(
@@ -116,8 +117,8 @@ def tile_clipped_feedback_control_s3_kernel(
 
         def permute_l_words(g):
             nc.vector.tensor_copy(
-                out=lw[:, g].rearrange("p t (m b) -> p m t b", b=2),
-                in_=l_raw[g][:].rearrange("p (m t b) -> p m t b", t=4, b=2),
+                out=lw[:, g].bitcast(U16).rearrange("p t m -> p m t"),
+                in_=l_raw[g][:].bitcast(U16).rearrange("p (m t) -> p m t", t=4),
             )
 
         def permute_l_scales(g):
@@ -170,12 +171,23 @@ def tile_clipped_feedback_control_s3_kernel(
             else:
                 nc.scalar.copy(out=dst, in_=src)
 
+        def interleave_f_half(c, g, k, on_vector=False):
+            if k == 0:
+                live["fg", c, g] = stage.tile([P, 4 * W], BF16, name=f"fg{c}{g}", tag="fg", bufs=3, align_bytes=64)
+            m = slice(64 * k, 64 * k + 64)
+            src = fr[c][g][:].rearrange("p j (m t) -> p m j t", t=4)
+            dst = live["fg", c, g][:].rearrange("p (t m j) -> p m j t", t=4, j=4)
+            if on_vector:
+                nc.vector.tensor_copy(out=dst[:, m], in_=src[:, m])
+            else:
+                nc.scalar.copy(out=dst[:, m], in_=src[:, m])
+
         def quantize_f(c, g):
             nc.vector.quantize_mx(out=fq[c][g][:].bitcast(FP8X4), scales=fs[c][g][:], in_=live["fg", c, g][:])
 
         def action_pass(h, g, t, c, order):
             if c == order[0]:
-                live["acc", h, g, t] = psum.tile([P, W], F32, name=f"acc{h}{g}{t}", tag="acc")
+                live["acc", h, g, t] = psum.tile([P, W], F32, name=f"acc{h}{g}{t}", tag="turn" if (h, g) == (0, 1) else "acc")
             cols = slice(P * t, P * t + P)
             if c < XP:
                 w, ws = fq[c][g][:, cols].bitcast(FP8X4), fs[c][g][:, cols]
@@ -236,14 +248,18 @@ def tile_clipped_feedback_control_s3_kernel(
                     start=(g == 0), stop=(g == 1),
                 )
 
-        def add_drift(i, n):
+        def add_drift(i, n, on_gpsimd=False):
             cols = slice(W * n, W * n + W)
             if n == 0:
                 live["ot", i] = stage.tile([P, S], F32, name=f"ot{i}", tag="ot", bufs=4)
             ot = live["ot", i]
-            nc.vector.tensor_tensor(out=ot[:, cols], in0=live["y", i, n][:], in1=dr[i // 2][:, i % 2, cols], op=ALU.add)
+            if on_gpsimd:
+                nc.scalar.copy(out=ot[:, cols], in_=live["y", i, n][:])
+                nc.gpsimd.tensor_tensor(out=ot[:, cols], in0=ot[:, cols], in1=dr[i // 2][:, i % 2, cols], op=ALU.add)
+            else:
+                nc.vector.tensor_tensor(out=ot[:, cols], in0=live["y", i, n][:], in1=dr[i // 2][:, i % 2, cols], op=ALU.add)
             rows = pair_rows(out, i // 2)[:, i % 2, :]
-            if i >= 6:
+            if True:
                 nc.sync.dma_start(out=rows[:, cols], in_=ot[:, cols])
             elif n == 2:
                 nc.sync.dma_start(out=rows, in_=ot[:])
@@ -268,95 +284,136 @@ def tile_clipped_feedback_control_s3_kernel(
             for j in (2 * h, 2 * h + 1):
                 scale_x(j, c)
 
-        order = (0, 1, EP, 2)
+        def pair_pass(h, g, k, c, order):
+            for t in (2 * k, 2 * k + 1):
+                action_pass(h, g, t, c, order)
+
+        order = (EP, 0, 1, 2)
         for c in range(XP):
             spread_scales(c)
-        permute_l_words(0)
-        interleave_f(0, 0)
-        samples_pass(0, 0)
-        interleave_f(1, 0)
-        samples_pass(0, 1)
-        quantize_f(0, 0)
-        quantize_x(0, 0)
+        scale_x(0, 0)
         turn_pass(0, EP)
-        interleave_f(2, 0)
-        scale_pass(0, 2)
-        block_pass(0, 0, 0, order)
-        turn_pass(0, 2)
-        quantize_f(1, 0)
-        quantize_x(0, 1)
+        permute_l_words(0)
+        scale_x(0, 1)
+        turn(0, 0)
+        turn(0, 1)
         quantize_x(0, EP)
         permute_l_scales(0)
+        interleave_f(0, 0)
+        empty_turn(0, 0)
+        scale_x(1, 0)
+        pair_pass(0, 0, 0, EP, order)
+        turn(1, 0)
+        empty_turn(1, 0)
+        interleave_f(1, 0)
+        scale_x(1, 1)
+        quantize_f(0, 0)
+        pair_pass(0, 0, 1, EP, order)
+        turn(1, 1)
+        empty_turn(0, 1)
+        empty_turn(1, 1)
+        quantize_x(0, 0)
+        scale_x(0, 2)
+        pair_pass(0, 0, 0, 0, order)
+        turn(0, 2)
+        interleave_f_half(2, 0, 0)
+        scale_x(1, 2)
+        turn(2, EP)
+        pair_pass(0, 0, 1, 0, order)
+        turn(1, 2)
+        turn(3, EP)
+        quantize_f(1, 0)
+        quantize_x(0, 1)
+        interleave_f_half(2, 0, 1, True)
+        empty_turn(0, 2)
+        empty_turn(1, 2)
         widen_limits()
         block_pass(0, 0, 1, order)
-        block_pass(0, 0, EP, order)
-        interleave_f(0, 1)
-        permute_l_words(1)
+        scale_x(2, 0)
         quantize_f(2, 0)
         quantize_x(0, 2)
-        block_pass(0, 0, 2, order)
-        interleave_f(1, 1)
-        interleave_f(2, 1, True)
-        permute_l_scales(1)
-        quantize_f(0, 1)
-        quantize_f(2, 1)
-        scale_x(2, 0)
-        quantize_f(1, 1)
-        for j in (2, 3):
-            turn(j, EP)
-        empty_action(0, 0, 0)
         for j in (2, 3):
             empty_turn(j, EP)
+        turn(2, 0)
+        block_pass(0, 0, 2, order)
+        interleave_f_half(0, 1, 0)
         scale_x(3, 0)
-        action(0, 1, 0)
-        for c in range(XP):
-            empty_action(0, 0, c + 1)
-            turn_pass(1, c)
-            if c + 1 < XP:
-                scale_pass(1, c + 1)
-            quantize_x(1, (EP, 0, 1)[c])
-            action(0, 1, c + 1)
+        quantize_x(1, EP)
+        for t in range(4):
+            empty_action(0, 0, t)
+        turn(3, 0)
+        for j in (2, 3):
+            empty_turn(j, 0)
+        block_pass(1, 0, EP, order)
+        interleave_f_half(0, 1, 1)
+        samples_pass(1, 1)
+        permute_l_words(1)
+        permute_l_scales(1)
+        quantize_x(1, 0)
+        interleave_f_half(1, 1, 0)
+        scale_x(2, 2)
+        pair_pass(1, 0, 0, 0, order)
+        turn(2, 2)
+        quantize_x(1, 1)
+        scale_x(3, 2)
+        pair_pass(1, 0, 1, 0, order)
+        pair_pass(1, 0, 0, 1, order)
+        turn(3, 2)
+        for j in (2, 3):
+            empty_turn(j, 2)
+        pair_pass(1, 0, 1, 1, order)
+        interleave_f_half(1, 1, 1)
+        quantize_f(0, 1)
+        interleave_f(2, 1, True)
+        quantize_x(1, 2)
+        late = (EP, 0, 2, 1)
+        pair_pass(0, 1, 0, EP, late)
+        pair_pass(0, 1, 0, 0, late)
+        block_pass(1, 0, 2, order)
+        pair_pass(0, 1, 1, EP, late)
+        pair_pass(0, 1, 1, 0, late)
+        quantize_f(2, 1)
+        quantize_f(1, 1)
+        for c in late[2:]:
+            block_pass(0, 1, c, late)
         for t in range(4):
             clip(0, 0, t)
-        quantize_x(1, 2)
-        for t in range(4):
-            empty_action(0, 1, t)
-            action(1, 0, t)
-        for k in range(2):
-            interleave_u(0, 0, k, True)
-        for t in range(4):
-            clip(0, 1, t)
-        for k in range(2):
-            quantize_u(0, 0, k)
-        for k in range(2):
-            interleave_u(0, 1, k, k == 1)
-        steps = [(i, n) for i in range(8) for n in range(3)]
-        early = 6
         for t in range(4):
             empty_action(1, 0, t)
-        for k in range(2):
-            quantize_u(0, 1, k)
+        interleave_u(0, 0, 0)
+        interleave_u(0, 0, 1, True)
         for t in range(4):
             clip(1, 0, t)
-        for k in range(2):
-            interleave_u(1, 0, k, k == 1)
-        for t in range(4):
+        quantize_u(0, 0, 1)
+        quantize_u(0, 0, 0)
+        for t in range(2):
             action(1, 1, t)
-            empty_action(1, 1, t)
-            if t < 3:
-                for i, n in steps[2 * t:2 * t + 2]:
-                    rate(i, n, "turn")
-                    add_drift(i, n)
-            if t < 2:
-                quantize_u(1, 0, 1 - t)
-            if t > 0:
-                clip(1, 1, t - 1)
-        for s, (i, n) in list(enumerate(steps))[early:]:
-            rate(i, n, "turn" if s % 2 == 0 else "acc")
+        for t in range(4):
+            empty_action(0, 1, t, t >= 2)
+        interleave_u(1, 0, 0)
+        for t in range(2):
+            clip(0, 1, t)
+        quantize_u(1, 0, 0)
+        interleave_u(0, 1, 0, True)
+        interleave_u(0, 1, 1)
+        interleave_u(1, 0, 1)
+        quantize_u(0, 1, 0)
+        quantize_u(0, 1, 1)
+        steps = [(i, n) for i in range(8) for n in range(3)]
+        for s, (i, n) in enumerate(steps):
+            if s in (0, 3):
+                action(1, 1, 2 + s // 3)
+                for t in ((0, 1, 2), (3,))[s // 3]:
+                    empty_action(1, 1, t)
+            rate(i, n, "turn" if s % 2 == 0 or s < 5 else "acc")
             add_drift(i, n)
-            if s == early:
+            if s == 1:
+                quantize_u(1, 0, 1)
+                for t in range(3):
+                    clip(1, 1, t)
+            if s == 3:
                 clip(1, 1, 3)
-                interleave_u(1, 1, 0)
-                interleave_u(1, 1, 1)
-            if s in (early + 3, early + 5):
-                quantize_u(1, 1, (s - early - 3) // 2)
+                for k in range(2):
+                    interleave_u(1, 1, k)
+            if s in (7, 9):
+                quantize_u(1, 1, (s - 7) // 2)

@@ -164,8 +164,8 @@ def tile_clipped_feedback_control_s3_kernel(
         def interleave_f(c, g, on_vector=False):
             fg = stage.tile([P, 4 * W], BF16, name=f"fg{c}{g}", tag="fg", bufs=3, align_bytes=64)
             live["fg", c, g] = fg
-            src = fr[c][g][:].rearrange("p j (m t) -> p m j t", t=4)
-            dst = fg[:].rearrange("p (t m j) -> p m j t", t=4, j=4)
+            src = fr[c][g][:].rearrange("p j (m r t) -> p m t j r", r=2, t=4)
+            dst = fg[:].rearrange("p (t m r j) -> p m t j r", t=4, r=2, j=4)
             if on_vector:
                 nc.vector.tensor_copy(out=dst, in_=src)
             else:
@@ -174,9 +174,9 @@ def tile_clipped_feedback_control_s3_kernel(
         def interleave_f_half(c, g, k, on_vector=False):
             if k == 0:
                 live["fg", c, g] = stage.tile([P, 4 * W], BF16, name=f"fg{c}{g}", tag="fg", bufs=3, align_bytes=64)
-            m = slice(64 * k, 64 * k + 64)
-            src = fr[c][g][:].rearrange("p j (m t) -> p m j t", t=4)
-            dst = live["fg", c, g][:].rearrange("p (t m j) -> p m j t", t=4, j=4)
+            m = slice(32 * k, 32 * k + 32)
+            src = fr[c][g][:].rearrange("p j (m r t) -> p m t j r", r=2, t=4)
+            dst = live["fg", c, g][:].rearrange("p (t m r j) -> p m t j r", t=4, r=2, j=4)
             if on_vector:
                 nc.vector.tensor_copy(out=dst[:, m], in_=src[:, m])
             else:
@@ -187,7 +187,7 @@ def tile_clipped_feedback_control_s3_kernel(
 
         def action_pass(h, g, t, c, order):
             if c == order[0]:
-                live["acc", h, g, t] = psum.tile([P, W], F32, name=f"acc{h}{g}{t}", tag="turn" if (h, g) == (0, 1) else "acc")
+                live["acc", h, g, t] = psum.tile([P, W], F32, name=f"acc{h}{g}{t}", tag="turn" if g == 1 else "acc")
             cols = slice(P * t, P * t + P)
             if c < XP:
                 w, ws = fq[c][g][:, cols].bitcast(FP8X4), fs[c][g][:, cols]
@@ -365,55 +365,58 @@ def tile_clipped_feedback_control_s3_kernel(
         interleave_f_half(1, 1, 1)
         quantize_f(0, 1)
         interleave_f(2, 1, True)
-        quantize_x(1, 2)
         late = (EP, 0, 2, 1)
-        pair_pass(0, 1, 0, EP, late)
-        pair_pass(0, 1, 0, 0, late)
-        block_pass(1, 0, 2, order)
-        pair_pass(0, 1, 1, EP, late)
-        pair_pass(0, 1, 1, 0, late)
-        quantize_f(2, 1)
-        quantize_f(1, 1)
-        for c in late[2:]:
-            block_pass(0, 1, c, late)
+        for c in late[:2]:
+            pair_pass(0, 1, 0, c, late)
         for t in range(4):
             clip(0, 0, t)
-        for t in range(4):
-            empty_action(1, 0, t)
-        interleave_u(0, 0, 0)
-        interleave_u(0, 0, 1, True)
-        for t in range(4):
-            clip(1, 0, t)
-        quantize_u(0, 0, 1)
-        quantize_u(0, 0, 0)
-        for t in range(2):
-            action(1, 1, t)
+        quantize_f(2, 1)
+        quantize_f(1, 1)
+        quantize_x(1, 2)
+        for k in range(2):
+            interleave_u(0, 0, k)
+        for c in late[:2]:
+            pair_pass(0, 1, 1, c, late)
+        for c in late[2:]:
+            block_pass(0, 1, c, late)
+        block_pass(1, 0, 2, order)
         for t in range(4):
             empty_action(0, 1, t, t >= 2)
-        interleave_u(1, 0, 0)
+        quantize_u(0, 0, 0)
         for t in range(2):
             clip(0, 1, t)
-        quantize_u(1, 0, 0)
+        quantize_u(0, 0, 1)
         interleave_u(0, 1, 0, True)
+        for t in range(4):
+            empty_action(1, 0, t)
         interleave_u(0, 1, 1)
-        interleave_u(1, 0, 1)
+        for t in range(2):
+            clip(1, 0, t)
         quantize_u(0, 1, 0)
-        quantize_u(0, 1, 1)
+        for t in range(2, 4):
+            clip(1, 0, t)
+        for t in range(2):
+            action(1, 1, t)
+        for k in range(2):
+            interleave_u(1, 0, k)
         steps = [(i, n) for i in range(8) for n in range(3)]
         for s, (i, n) in enumerate(steps):
-            if s in (0, 3):
-                action(1, 1, 2 + s // 3)
-                for t in ((0, 1, 2), (3,))[s // 3]:
+            if s in (2, 5):
+                action(1, 1, 2 + s // 5)
+                for t in ((0, 1, 2), (3,))[s // 5]:
                     empty_action(1, 1, t)
-            rate(i, n, "turn" if s % 2 == 0 or s < 5 else "acc")
-            add_drift(i, n)
+            rate(i, n, "acc" if s % 2 == 0 or s < 7 else "turn")
+            add_drift(i, n, False)
             if s == 1:
-                quantize_u(1, 0, 1)
+                quantize_u(0, 1, 1)
+            if s in (1, 4):
+                quantize_u(1, 0, s // 4)
+            if s == 4:
                 for t in range(3):
                     clip(1, 1, t)
-            if s == 3:
+            if s == 5:
                 clip(1, 1, 3)
                 for k in range(2):
                     interleave_u(1, 1, k)
-            if s in (7, 9):
-                quantize_u(1, 1, (s - 7) // 2)
+            if s in (8, 10):
+                quantize_u(1, 1, (s - 8) // 2)

@@ -115,6 +115,21 @@ def tile_clipped_feedback_control_s3_kernel(
                 nc.tensor.transpose(bank[:, j, :], scale_col[:, c, j:j + 1].to_broadcast([P, P]), ident[:])
             nc.scalar.copy(out=scale_row[c][:].rearrange("p (m j) -> p m j", j=4), in_=bank[:].rearrange("p j m -> p m j"))
 
+        def spread_by_matmul(c, k):
+            if k == 0:
+                live["sb", c] = psum.tile([P, 4, P], F32, name=f"sb{c}", tag="acc")
+            bank = live["sb", c]
+            for j in (2 * k, 2 * k + 1):
+                nc.tensor.matmul(
+                    bank[:, j, :], lhsT=scale_col[:, c, j:j + 1].to_broadcast([P, P]), rhs=ident[:],
+                    start=True, stop=True,
+                )
+
+        def empty_scales(c):
+            nc.scalar.copy(
+                out=scale_row[c][:].rearrange("p (m j) -> p m j", j=4), in_=live["sb", c][:].rearrange("p j m -> p m j")
+            )
+
         def permute_l_words(g):
             nc.vector.tensor_copy(
                 out=lw[:, g].bitcast(U16).rearrange("p t m -> p m t"),
@@ -289,12 +304,15 @@ def tile_clipped_feedback_control_s3_kernel(
                 action_pass(h, g, t, c, order)
 
         order = (EP, 0, 1, 2)
-        for c in range(XP):
+        for c in range(2):
             spread_scales(c)
+        spread_by_matmul(2, 0)
         scale_x(0, 0)
         turn_pass(0, EP)
         permute_l_words(0)
         scale_x(0, 1)
+        spread_by_matmul(2, 1)
+        empty_scales(2)
         turn(0, 0)
         turn(0, 1)
         quantize_x(0, EP)
@@ -318,50 +336,54 @@ def tile_clipped_feedback_control_s3_kernel(
         turn(0, 2)
         interleave_f_half(2, 0, 0)
         scale_x(1, 2)
-        turn(2, EP)
         pair_pass(0, 0, 1, 0, order)
+        turn(2, EP)
         turn(1, 2)
-        turn(3, EP)
         quantize_f(1, 0)
         quantize_x(0, 1)
         interleave_f_half(2, 0, 1, True)
         empty_turn(0, 2)
         empty_turn(1, 2)
         widen_limits()
-        block_pass(0, 0, 1, order)
+        pair_pass(0, 0, 0, 1, order)
+        turn(3, EP)
+        pair_pass(0, 0, 1, 1, order)
         scale_x(2, 0)
         quantize_f(2, 0)
         quantize_x(0, 2)
         for j in (2, 3):
             empty_turn(j, EP)
         turn(2, 0)
+        empty_turn(2, 0)
         block_pass(0, 0, 2, order)
-        interleave_f_half(0, 1, 0)
         scale_x(3, 0)
         quantize_x(1, EP)
-        for t in range(4):
-            empty_action(0, 0, t)
         turn(3, 0)
-        for j in (2, 3):
-            empty_turn(j, 0)
-        block_pass(1, 0, EP, order)
+        for t in range(3):
+            empty_action(0, 0, t)
+        empty_turn(3, 0)
+        empty_action(0, 0, 3)
+        interleave_f_half(0, 1, 0)
+        scale_pass(1, 1)
+        for k in range(2):
+            pair_pass(1, 0, k, EP, order)
+            turn(2 + k, 1)
+            empty_turn(2 + k, 1)
         interleave_f_half(0, 1, 1)
-        samples_pass(1, 1)
-        permute_l_words(1)
-        permute_l_scales(1)
         quantize_x(1, 0)
-        interleave_f_half(1, 1, 0)
         scale_x(2, 2)
         pair_pass(1, 0, 0, 0, order)
         turn(2, 2)
+        empty_turn(2, 2)
+        interleave_f_half(1, 1, 0)
+        permute_l_words(1)
+        permute_l_scales(1)
         quantize_x(1, 1)
         scale_x(3, 2)
         pair_pass(1, 0, 1, 0, order)
-        pair_pass(1, 0, 0, 1, order)
+        block_pass(1, 0, 1, order)
         turn(3, 2)
-        for j in (2, 3):
-            empty_turn(j, 2)
-        pair_pass(1, 0, 1, 1, order)
+        empty_turn(3, 2)
         interleave_f_half(1, 1, 1)
         quantize_f(0, 1)
         interleave_f(2, 1, True)

@@ -34,8 +34,8 @@ def tile_clipped_feedback_control_s3_kernel(
 
         ident = keep.tile([P, P], F32, name="ident")
         make_identity(nc, ident[:])
-        l_plane = keep.tile([P, A], U8, name="l_plane", align_bytes=64)
-        b_plane = keep.tile([P, 2, S], U8, name="b_plane", align_bytes=64)
+        l_plane = keep.tile([P, A], U8, name="l_plane", align_bytes=256)
+        b_plane = keep.tile([P, 2, S], U8, name="b_plane", align_bytes=256)
         nc.vector.memset(l_plane[:].bitcast(I32), 0)
         nc.vector.memset(b_plane[:].rearrange("p g n -> p (g n)").bitcast(I32), 0)
 
@@ -46,7 +46,7 @@ def tile_clipped_feedback_control_s3_kernel(
         xb = [keep.tile([P, 2, S], U8, name=f"xb{j}") for j in range(4)]
         eb = [keep.tile([P, 2 * E], BF16, name=f"eb{j}") for j in range(4)]
         fr = [[keep.tile([P, 4, W], BF16, name=f"fr{c}{g}") for g in range(2)] for c in range(XP)]
-        bw = keep.tile([P, 2, 2 * S], U8, name="bw", align_bytes=64)
+        bw = keep.tile([P, 2, 2 * S], U8, name="bw", align_bytes=256)
         dr = [keep.tile([P, 2, S], BF16, name=f"dr{j}") for j in range(4)]
 
         def pair_rows(t, j):
@@ -99,14 +99,14 @@ def tile_clipped_feedback_control_s3_kernel(
             nc.sync.dma_start(out=dr[j][:], in_=pair_rows(drift, j))
 
         lim = keep.tile([P, 2, 2, 4], F32, name="lim")
-        lw = keep.tile([P, 2, 4, 256], U8, name="lw", align_bytes=64)
-        ls = keep.tile([P, 2, 4, P], U8, name="ls", align_bytes=64)
-        fq = [[keep.tile([P, W], U32, name=f"fq{c}{g}", align_bytes=64) for g in range(2)] for c in range(XP)]
-        fs = [[keep.tile([P, W], U8, name=f"fs{c}{g}", align_bytes=64) for g in range(2)] for c in range(XP)]
-        xq = [[keep.tile([P, W], U32, name=f"xq{h}{c}", align_bytes=64) for c in range(XP + 1)] for h in range(2)]
-        xs = [[keep.tile([P, W], U8, name=f"xs{h}{c}", align_bytes=64) for c in range(XP + 1)] for h in range(2)]
-        uq = [[keep.tile([P, W], U32, name=f"uq{h}{g}", align_bytes=64) for g in range(2)] for h in range(2)]
-        us = [[keep.tile([P, W], U8, name=f"us{h}{g}", align_bytes=64) for g in range(2)] for h in range(2)]
+        lw = keep.tile([P, 2, 4, 256], U8, name="lw", align_bytes=256)
+        ls = keep.tile([P, 2, 4, P], U8, name="ls", align_bytes=256)
+        fq = [[keep.tile([P, W], U32, name=f"fq{c}{g}", align_bytes=256) for g in range(2)] for c in range(XP)]
+        fs = [[keep.tile([P, W], U8, name=f"fs{c}{g}", align_bytes=256) for g in range(2)] for c in range(XP)]
+        xq = [[keep.tile([P, W], U32, name=f"xq{h}{c}", align_bytes=256) for c in range(XP + 1)] for h in range(2)]
+        xs = [[keep.tile([P, W], U8, name=f"xs{h}{c}", align_bytes=256) for c in range(XP + 1)] for h in range(2)]
+        uq = [[keep.tile([P, W], U32, name=f"uq{h}{g}", align_bytes=256) for g in range(2)] for h in range(2)]
+        us = [[keep.tile([P, W], U8, name=f"us{h}{g}", align_bytes=256) for g in range(2)] for h in range(2)]
         live = {}
 
         def spread_scales(c):
@@ -166,7 +166,7 @@ def tile_clipped_feedback_control_s3_kernel(
         def empty_turn(j, c):
             h, half = divmod(j, 2)
             if half == 0:
-                live["xg", h, c] = stage.tile([P, 4 * W], BF16, name=f"xg{h}{c}", tag="xg", bufs=4, align_bytes=64)
+                live["xg", h, c] = stage.tile([P, 4 * W], BF16, name=f"xg{h}{c}", tag="xg", bufs=4, align_bytes=256)
             dst = live["xg", h, c][:, 2 * W * half:2 * W * half + 2 * W]
             nc.scalar.copy(
                 out=dst.bitcast(F32).rearrange("p (i r u) -> p i r u", i=2, u=2),
@@ -177,7 +177,7 @@ def tile_clipped_feedback_control_s3_kernel(
             nc.vector.quantize_mx(out=xq[h][c][:].bitcast(FP8X4), scales=xs[h][c][:], in_=live["xg", h, c][:])
 
         def interleave_f(c, g, on_vector=False):
-            fg = stage.tile([P, 4 * W], BF16, name=f"fg{c}{g}", tag="fg", bufs=3, align_bytes=64)
+            fg = stage.tile([P, 4 * W], BF16, name=f"fg{c}{g}", tag="fg", bufs=3, align_bytes=256)
             live["fg", c, g] = fg
             src = fr[c][g][:].rearrange("p j (m r t) -> p m t j r", r=2, t=4)
             dst = fg[:].rearrange("p (t m r j) -> p m t j r", t=4, r=2, j=4)
@@ -188,7 +188,7 @@ def tile_clipped_feedback_control_s3_kernel(
 
         def interleave_f_half(c, g, k, on_vector=False):
             if k == 0:
-                live["fg", c, g] = stage.tile([P, 4 * W], BF16, name=f"fg{c}{g}", tag="fg", bufs=3, align_bytes=64)
+                live["fg", c, g] = stage.tile([P, 4 * W], BF16, name=f"fg{c}{g}", tag="fg", bufs=3, align_bytes=256)
             m = slice(32 * k, 32 * k + 32)
             src = fr[c][g][:].rearrange("p j (m r t) -> p m t j r", r=2, t=4)
             dst = live["fg", c, g][:].rearrange("p (t m r j) -> p m t j r", t=4, r=2, j=4)
@@ -237,7 +237,7 @@ def tile_clipped_feedback_control_s3_kernel(
             )
 
         def interleave_u(h, g, k, on_vector=False):
-            ug = stage.tile([P, 2 * W], BF16, name=f"ug{h}{g}{k}", tag="ug", bufs=4, align_bytes=64)
+            ug = stage.tile([P, 2 * W], BF16, name=f"ug{h}{g}{k}", tag="ug", bufs=4, align_bytes=256)
             live["ug", h, g, k] = ug
             src = live["up", h, g][:, :, 256 * k:256 * k + 256].rearrange("p t (c i) -> p c t i", i=4)
             dst = ug[:].rearrange("p (c i t) -> p c t i", i=4, t=4)

@@ -299,6 +299,14 @@ def tile_clipped_feedback_control_s3_kernel(
             for j in (2 * h, 2 * h + 1):
                 scale_x(j, c)
 
+        def turn_only(h, c):
+            for j in (2 * h, 2 * h + 1):
+                turn(j, c)
+
+        def empty_pass(h, c):
+            for j in (2 * h, 2 * h + 1):
+                empty_turn(j, c)
+
         def pair_pass(h, g, k, c, order):
             for t in (2 * k, 2 * k + 1):
                 action_pass(h, g, t, c, order)
@@ -331,59 +339,47 @@ def tile_clipped_feedback_control_s3_kernel(
         empty_turn(0, 1)
         empty_turn(1, 1)
         quantize_x(0, 0)
-        scale_x(0, 2)
+        interleave_f_half(2, 0, 0)
+        scale_pass(0, 2)
         pair_pass(0, 0, 0, 0, order)
         turn(0, 2)
-        interleave_f_half(2, 0, 0)
-        scale_x(1, 2)
         pair_pass(0, 0, 1, 0, order)
-        turn(2, EP)
         turn(1, 2)
+        turn(2, EP)
         quantize_f(1, 0)
         quantize_x(0, 1)
         interleave_f_half(2, 0, 1, True)
-        empty_turn(0, 2)
-        empty_turn(1, 2)
+        empty_pass(0, 2)
         widen_limits()
-        pair_pass(0, 0, 0, 1, order)
+        block_pass(0, 0, 1, order)
         turn(3, EP)
-        pair_pass(0, 0, 1, 1, order)
+        empty_pass(1, EP)
         scale_x(2, 0)
-        quantize_f(2, 0)
-        quantize_x(0, 2)
-        for j in (2, 3):
-            empty_turn(j, EP)
         turn(2, 0)
         empty_turn(2, 0)
+        quantize_f(2, 0)
+        quantize_x(0, 2)
         block_pass(0, 0, 2, order)
         scale_x(3, 0)
         quantize_x(1, EP)
         turn(3, 0)
-        for t in range(3):
+        for t in range(4):
             empty_action(0, 0, t)
         empty_turn(3, 0)
-        empty_action(0, 0, 3)
         interleave_f_half(0, 1, 0)
         scale_pass(1, 1)
-        for k in range(2):
-            pair_pass(1, 0, k, EP, order)
-            turn(2 + k, 1)
-            empty_turn(2 + k, 1)
-        interleave_f_half(0, 1, 1)
+        block_pass(1, 0, EP, order)
+        turn_pass(1, 1)
         quantize_x(1, 0)
-        scale_x(2, 2)
-        pair_pass(1, 0, 0, 0, order)
-        turn(2, 2)
-        empty_turn(2, 2)
+        scale_pass(1, 2)
+        interleave_f_half(0, 1, 1)
+        block_pass(1, 0, 0, order)
+        turn_pass(1, 2)
         interleave_f_half(1, 1, 0)
+        quantize_x(1, 1)
         permute_l_words(1)
         permute_l_scales(1)
-        quantize_x(1, 1)
-        scale_x(3, 2)
-        pair_pass(1, 0, 1, 0, order)
         block_pass(1, 0, 1, order)
-        turn(3, 2)
-        empty_turn(3, 2)
         interleave_f_half(1, 1, 1)
         quantize_f(0, 1)
         interleave_f(2, 1, True)
@@ -423,22 +419,27 @@ def tile_clipped_feedback_control_s3_kernel(
             interleave_u(1, 0, k)
         steps = [(i, n) for i in range(8) for n in range(3)]
         for s, (i, n) in enumerate(steps):
-            if s in (2, 5):
-                action(1, 1, 2 + s // 5)
-                for t in ((0, 1, 2), (3,))[s // 5]:
+            if s == 3:
+                action(1, 1, 2)
+                for t in range(3):
                     empty_action(1, 1, t)
-            rate(i, n, "acc" if s % 2 == 0 or s < 7 else "turn")
-            add_drift(i, n, False)
+            if s == 6:
+                action(1, 1, 3)
+                empty_action(1, 1, 3)
+            rate(i, n, "acc" if s % 2 == 0 or s < 8 else "turn")
+            add_drift(i, n)
             if s == 1:
                 quantize_u(0, 1, 1)
-            if s in (1, 4):
-                quantize_u(1, 0, s // 4)
-            if s == 4:
+                quantize_u(1, 0, 0)
+            if s == 5:
+                quantize_u(1, 0, 1)
                 for t in range(3):
                     clip(1, 1, t)
-            if s == 5:
+            if s == 6:
                 clip(1, 1, 3)
-                for k in range(2):
-                    interleave_u(1, 1, k)
-            if s in (8, 10):
-                quantize_u(1, 1, (s - 8) // 2)
+                interleave_u(1, 1, 0)
+                interleave_u(1, 1, 1)
+            if s == 9:
+                quantize_u(1, 1, 0)
+            if s == 11:
+                quantize_u(1, 1, 1)

@@ -220,7 +220,7 @@ def tile_clipped_feedback_control_s3_kernel(
 
         def empty_action(h, g, t, on_vector=False):
             if t == 0:
-                live["up", h, g] = stage.tile([P, 4, W], BF16, name=f"up{h}{g}", tag="up", bufs=4)
+                live["up", h, g] = stage.tile([P, 4, W], BF16, name=f"up{h}{g}", tag="up", bufs=3)
             u = live["up", h, g][:, t, :]
             if on_vector:
                 nc.vector.tensor_scalar(
@@ -263,21 +263,21 @@ def tile_clipped_feedback_control_s3_kernel(
                     start=(g == 0), stop=(g == 1),
                 )
 
-        def add_drift(i, n, on_gpsimd=False):
-            cols = slice(W * n, W * n + W)
-            if n == 0:
-                live["ot", i] = stage.tile([P, S], F32, name=f"ot{i}", tag="ot", bufs=4)
-            ot = live["ot", i]
-            if on_gpsimd:
-                nc.scalar.copy(out=ot[:, cols], in_=live["y", i, n][:])
-                nc.gpsimd.tensor_tensor(out=ot[:, cols], in0=ot[:, cols], in1=dr[i // 2][:, i % 2, cols], op=ALU.add)
-            else:
-                nc.vector.tensor_tensor(out=ot[:, cols], in0=live["y", i, n][:], in1=dr[i // 2][:, i % 2, cols], op=ALU.add)
-            rows = pair_rows(out, i // 2)[:, i % 2, :]
-            if True:
-                nc.sync.dma_start(out=rows[:, cols], in_=ot[:, cols])
-            elif n == 2:
-                nc.sync.dma_start(out=rows, in_=ot[:])
+        def add_drift(i, n):
+            j, chunk = i // 2, XP * (i % 2) + n
+            if chunk == 0:
+                live["ot", j] = stage.tile([P, 2 * S], F32, name=f"ot{j}", tag="ot", bufs=3)
+            cols = slice(W * chunk, W * chunk + W)
+            nc.vector.tensor_tensor(
+                out=live["ot", j][:, cols], in0=live["y", i, n][:],
+                in1=dr[j][:].rearrange("p i k -> p (i k)")[:, cols], op=ALU.add,
+            )
+
+        def store(first, count):
+            j, chunk = divmod(first, 2 * XP)
+            cols = slice(W * chunk, W * (chunk + count))
+            rows = pair_rows(out, j).rearrange("p i k -> p (i k)")
+            nc.sync.dma_start(out=rows[:, cols], in_=live["ot", j][:, cols])
 
         def samples_pass(h, c):
             for j in (2 * h, 2 * h + 1):
@@ -428,6 +428,10 @@ def tile_clipped_feedback_control_s3_kernel(
                 empty_action(1, 1, 3)
             rate(i, n, "acc" if s % 2 == 0 or s < 8 else "turn")
             add_drift(i, n)
+            if s < 6 or s >= 22:
+                store(s, 1)
+            elif s % 2 == 1:
+                store(s - 1, 2)
             if s == 1:
                 quantize_u(0, 1, 1)
                 quantize_u(1, 0, 0)

@@ -273,11 +273,11 @@ def tile_clipped_feedback_control_s3_kernel(
                 in1=dr[j][:].rearrange("p i k -> p (i k)")[:, cols], op=ALU.add,
             )
 
-        def store(first, count):
+        def store(first, count, queue=nc.sync):
             j, chunk = divmod(first, 2 * XP)
             cols = slice(W * chunk, W * (chunk + count))
             rows = pair_rows(out, j).rearrange("p i k -> p (i k)")
-            nc.sync.dma_start(out=rows[:, cols], in_=live["ot", j][:, cols])
+            queue.dma_start(out=rows[:, cols], in_=live["ot", j][:, cols])
 
         def samples_pass(h, c):
             for j in (2 * h, 2 * h + 1):
@@ -429,9 +429,9 @@ def tile_clipped_feedback_control_s3_kernel(
             rate(i, n, "acc" if s % 2 == 0 or s < 8 else "turn")
             add_drift(i, n)
             if s < 6 or s >= 22:
-                store(s, 1)
+                store(s, 1, nc.scalar if s == 22 else nc.sync)
             elif s % 2 == 1:
-                store(s - 1, 2)
+                store(s - 1, 2, nc.scalar if s >= 10 and s % 4 == 3 else nc.sync)
             if s == 1:
                 quantize_u(0, 1, 1)
                 quantize_u(1, 0, 0)

@@ -70,22 +70,22 @@ def tile_clipped_feedback_control_s3_kernel(
         load_x(0)
         load_e(0)
         load_e(1)
+        load_f(0, 0)
         load_l(0)
         for q in range(4):
             nc.sync.dma_start(
                 out=l_plane[32 * q:32 * q + 4, :].bitcast(I32), in_=L_scales[0, 4 * q:4 * q + 4, :].bitcast(I32)
             )
-        load_f(0, 0)
         load_x(1)
         load_f(1, 0)
         load_f(2, 0)
+        load_x(2)
         load_e(2)
         load_e(3)
-        load_x(2)
-        nc.sync.dma_start(out=lim_bf[0][:], in_=hi.rearrange("(g p t) -> p g t", p=P, t=4))
-        nc.sync.dma_start(out=lim_bf[1][:], in_=lo.rearrange("(g p t) -> p g t", p=P, t=4))
         load_x(3)
         load_f(0, 1)
+        nc.sync.dma_start(out=lim_bf[0][:], in_=hi.rearrange("(g p t) -> p g t", p=P, t=4))
+        nc.sync.dma_start(out=lim_bf[1][:], in_=lo.rearrange("(g p t) -> p g t", p=P, t=4))
         load_l(1)
         load_f(1, 1)
         load_f(2, 1)
@@ -98,7 +98,6 @@ def tile_clipped_feedback_control_s3_kernel(
         for j in range(4):
             nc.sync.dma_start(out=dr[j][:], in_=pair_rows(drift, j))
 
-        lim = keep.tile([P, 2, 2, 4], F32, name="lim")
         lw = keep.tile([P, 2, 4, 256], U8, name="lw", align_bytes=256)
         ls = keep.tile([P, 2, 4, P], U8, name="ls", align_bytes=256)
         fq = [[keep.tile([P, W], U32, name=f"fq{c}{g}", align_bytes=256) for g in range(2)] for c in range(XP)]
@@ -115,21 +114,6 @@ def tile_clipped_feedback_control_s3_kernel(
                 nc.tensor.transpose(bank[:, j, :], scale_col[:, c, j:j + 1].to_broadcast([P, P]), ident[:])
             nc.scalar.copy(out=scale_row[c][:].rearrange("p (m j) -> p m j", j=4), in_=bank[:].rearrange("p j m -> p m j"))
 
-        def spread_by_matmul(c, k):
-            if k == 0:
-                live["sb", c] = psum.tile([P, 4, P], F32, name=f"sb{c}", tag="acc")
-            bank = live["sb", c]
-            for j in (2 * k, 2 * k + 1):
-                nc.tensor.matmul(
-                    bank[:, j, :], lhsT=scale_col[:, c, j:j + 1].to_broadcast([P, P]), rhs=ident[:],
-                    start=True, stop=True,
-                )
-
-        def empty_scales(c):
-            nc.scalar.copy(
-                out=scale_row[c][:].rearrange("p (m j) -> p m j", j=4), in_=live["sb", c][:].rearrange("p j m -> p m j")
-            )
-
         def permute_l_words(g):
             nc.vector.tensor_copy(
                 out=lw[:, g].bitcast(U16).rearrange("p t m -> p m t"),
@@ -142,10 +126,6 @@ def tile_clipped_feedback_control_s3_kernel(
                 in_=l_plane[:, W * g:W * g + W].rearrange("p (m t) -> p m t", t=4),
             )
 
-        def widen_limits():
-            for k in range(2):
-                nc.vector.tensor_copy(out=lim[:, k], in_=lim_bf[k][:])
-
         def scale_x(j, c):
             for i in range(2):
                 xv = stage.tile([P, W], BF16, name=f"xv{j}{c}{i}", tag="xv", bufs=8)
@@ -154,8 +134,8 @@ def tile_clipped_feedback_control_s3_kernel(
                     out=xv[:], in0=xb[j][:, i, W * c:W * c + W].bitcast(FP8), in1=scale_row[c][:], op=ALU.mult
                 )
 
-        def turn(j, c):
-            bank = psum.tile([P, 2, 2, P], F32, name=f"xt{j}{c}", tag="turn")
+        def turn(j, c, tag="turn"):
+            bank = psum.tile([P, 2, 2, P], F32, name=f"xt{j}{c}", tag=tag)
             live["xt", j, c] = bank
             for i in range(2):
                 src = live["xv", j, c, i][:] if c < XP else eb[j][:, E * i:E * i + E]
@@ -186,10 +166,10 @@ def tile_clipped_feedback_control_s3_kernel(
             else:
                 nc.scalar.copy(out=dst, in_=src)
 
-        def interleave_f_half(c, g, k, on_vector=False):
+        def interleave_f_half(c, g, k, on_vector=False, cut=32):
             if k == 0:
                 live["fg", c, g] = stage.tile([P, 4 * W], BF16, name=f"fg{c}{g}", tag="fg", bufs=3, align_bytes=256)
-            m = slice(32 * k, 32 * k + 32)
+            m = slice(cut, 64) if k else slice(0, cut)
             src = fr[c][g][:].rearrange("p j (m r t) -> p m t j r", r=2, t=4)
             dst = live["fg", c, g][:].rearrange("p (t m r j) -> p m t j r", t=4, r=2, j=4)
             if on_vector:
@@ -224,7 +204,7 @@ def tile_clipped_feedback_control_s3_kernel(
             u = live["up", h, g][:, t, :]
             if on_vector:
                 nc.vector.tensor_scalar(
-                    out=u, in0=live["acc", h, g, t][:], scalar1=lim[:, 0, g, t:t + 1], scalar2=lim[:, 1, g, t:t + 1],
+                    out=u, in0=live["acc", h, g, t][:], scalar1=lim_bf[0][:, g, t:t + 1], scalar2=lim_bf[1][:, g, t:t + 1],
                     op0=ALU.min, op1=ALU.max,
                 )
             else:
@@ -233,7 +213,7 @@ def tile_clipped_feedback_control_s3_kernel(
         def clip(h, g, t):
             u = live["up", h, g][:, t, :]
             nc.vector.tensor_scalar(
-                out=u, in0=u, scalar1=lim[:, 0, g, t:t + 1], scalar2=lim[:, 1, g, t:t + 1], op0=ALU.min, op1=ALU.max
+                out=u, in0=u, scalar1=lim_bf[0][:, g, t:t + 1], scalar2=lim_bf[1][:, g, t:t + 1], op0=ALU.min, op1=ALU.max
             )
 
         def interleave_u(h, g, k, on_vector=False):
@@ -312,53 +292,51 @@ def tile_clipped_feedback_control_s3_kernel(
                 action_pass(h, g, t, c, order)
 
         order = (EP, 0, 1, 2)
-        for c in range(2):
+        for c in range(XP):
             spread_scales(c)
-        spread_by_matmul(2, 0)
         scale_x(0, 0)
-        turn_pass(0, EP)
-        permute_l_words(0)
-        scale_x(0, 1)
-        spread_by_matmul(2, 1)
-        empty_scales(2)
+        turn(0, EP, "acc")
+        turn(1, EP, "acc")
+        empty_pass(0, EP)
         turn(0, 0)
+        interleave_f(0, 0)
+        scale_x(0, 1)
         turn(0, 1)
         quantize_x(0, EP)
+        permute_l_words(0)
         permute_l_scales(0)
-        interleave_f(0, 0)
-        empty_turn(0, 0)
         scale_x(1, 0)
         pair_pass(0, 0, 0, EP, order)
         turn(1, 0)
+        empty_turn(0, 0)
+        empty_turn(0, 1)
         empty_turn(1, 0)
-        interleave_f(1, 0)
-        scale_x(1, 1)
         quantize_f(0, 0)
+        scale_x(1, 1)
         pair_pass(0, 0, 1, EP, order)
         turn(1, 1)
-        empty_turn(0, 1)
-        empty_turn(1, 1)
+        interleave_f(1, 0)
         quantize_x(0, 0)
-        interleave_f_half(2, 0, 0)
         scale_pass(0, 2)
         pair_pass(0, 0, 0, 0, order)
         turn(0, 2)
         pair_pass(0, 0, 1, 0, order)
+        empty_turn(1, 1)
         turn(1, 2)
         turn(2, EP)
+        interleave_f_half(2, 0, 0, False, 44)
         quantize_f(1, 0)
         quantize_x(0, 1)
-        interleave_f_half(2, 0, 1, True)
+        interleave_f_half(2, 0, 1, True, 44)
         empty_pass(0, 2)
-        widen_limits()
         block_pass(0, 0, 1, order)
         turn(3, EP)
         empty_pass(1, EP)
         scale_x(2, 0)
-        turn(2, 0)
-        empty_turn(2, 0)
         quantize_f(2, 0)
         quantize_x(0, 2)
+        turn(2, 0)
+        empty_turn(2, 0)
         block_pass(0, 0, 2, order)
         scale_x(3, 0)
         quantize_x(1, EP)
@@ -386,13 +364,13 @@ def tile_clipped_feedback_control_s3_kernel(
         late = (EP, 0, 2, 1)
         for c in late[:2]:
             pair_pass(0, 1, 0, c, late)
+        quantize_f(2, 1)
         for t in range(4):
             clip(0, 0, t)
-        quantize_f(2, 1)
         quantize_f(1, 1)
         quantize_x(1, 2)
         for k in range(2):
-            interleave_u(0, 0, k)
+            interleave_u(0, 0, k, k == 1)
         for c in late[:2]:
             pair_pass(0, 1, 1, c, late)
         for c in late[2:]:

@@ -40,7 +40,6 @@ def tile_clipped_feedback_control_s3_kernel(
         nc.vector.memset(b_plane[:].rearrange("p g n -> p (g n)").bitcast(I32), 0)
 
         scale_col = keep.tile([P, XP, 4], F32, name="scale_col")
-        scale_row = [keep.tile([P, W], F32, name=f"scale_row{c}") for c in range(XP)]
         l_raw = [keep.tile([P, A], U8, name=f"l_raw{g}") for g in range(2)]
         lim_bf = [keep.tile([P, 2, 4], BF16, name=f"lim_bf{k}") for k in range(2)]
         xb = [keep.tile([P, 2, S], U8, name=f"xb{j}") for j in range(4)]
@@ -66,26 +65,26 @@ def tile_clipped_feedback_control_s3_kernel(
                 out=fr[c][g][:], in_=F[W * c:W * c + W, W * g:W * g + W].rearrange("(p j) a -> p j a", j=4)
             )
 
-        nc.sync.dma_start(out=scale_col[:], in_=x_scale.rearrange("o (c p j) -> p (o c) j", p=P, j=4))
         load_x(0)
-        load_e(0)
-        load_e(1)
-        load_f(0, 0)
+        nc.sync.dma_start(out=scale_col[:], in_=x_scale.rearrange("o (c p j) -> p (o c) j", p=P, j=4))
+        load_x(1)
         load_l(0)
         for q in range(4):
             nc.sync.dma_start(
                 out=l_plane[32 * q:32 * q + 4, :].bitcast(I32), in_=L_scales[0, 4 * q:4 * q + 4, :].bitcast(I32)
             )
-        load_x(1)
+        load_f(0, 0)
+        load_e(0)
+        load_e(1)
         load_f(1, 0)
         load_f(2, 0)
-        load_x(2)
         load_e(2)
         load_e(3)
-        load_x(3)
-        load_f(0, 1)
+        load_x(2)
         nc.sync.dma_start(out=lim_bf[0][:], in_=hi.rearrange("(g p t) -> p g t", p=P, t=4))
         nc.sync.dma_start(out=lim_bf[1][:], in_=lo.rearrange("(g p t) -> p g t", p=P, t=4))
+        load_x(3)
+        load_f(0, 1)
         load_l(1)
         load_f(1, 1)
         load_f(2, 1)
@@ -98,6 +97,7 @@ def tile_clipped_feedback_control_s3_kernel(
         for j in range(4):
             nc.sync.dma_start(out=dr[j][:], in_=pair_rows(drift, j))
 
+        lim = keep.tile([P, 2, 2, 4], F32, name="lim")
         lw = keep.tile([P, 2, 4, 256], U8, name="lw", align_bytes=256)
         ls = keep.tile([P, 2, 4, P], U8, name="ls", align_bytes=256)
         fq = [[keep.tile([P, W], U32, name=f"fq{c}{g}", align_bytes=256) for g in range(2)] for c in range(XP)]
@@ -107,12 +107,6 @@ def tile_clipped_feedback_control_s3_kernel(
         uq = [[keep.tile([P, W], U32, name=f"uq{h}{g}", align_bytes=256) for g in range(2)] for h in range(2)]
         us = [[keep.tile([P, W], U8, name=f"us{h}{g}", align_bytes=256) for g in range(2)] for h in range(2)]
         live = {}
-
-        def spread_scales(c):
-            bank = psum.tile([P, 4, P], F32, name=f"sb{c}", tag="turn")
-            for j in range(4):
-                nc.tensor.transpose(bank[:, j, :], scale_col[:, c, j:j + 1].to_broadcast([P, P]), ident[:])
-            nc.scalar.copy(out=scale_row[c][:].rearrange("p (m j) -> p m j", j=4), in_=bank[:].rearrange("p j m -> p m j"))
 
         def permute_l_words(g):
             nc.vector.tensor_copy(
@@ -126,32 +120,39 @@ def tile_clipped_feedback_control_s3_kernel(
                 in_=l_plane[:, W * g:W * g + W].rearrange("p (m t) -> p m t", t=4),
             )
 
-        def scale_x(j, c):
+        def widen_limits():
+            for k in range(2):
+                nc.vector.tensor_copy(out=lim[:, k], in_=lim_bf[k][:])
+
+        def widen_x(j, c):
             for i in range(2):
-                xv = stage.tile([P, W], BF16, name=f"xv{j}{c}{i}", tag="xv", bufs=8)
+                xv = stage.tile([P, W], BF16, name=f"xv{j}{c}{i}", tag="xv", bufs=12)
                 live["xv", j, c, i] = xv
-                nc.vector.tensor_tensor(
-                    out=xv[:], in0=xb[j][:, i, W * c:W * c + W].bitcast(FP8), in1=scale_row[c][:], op=ALU.mult
-                )
+                nc.scalar.copy(out=xv[:], in_=xb[j][:, i, W * c:W * c + W].bitcast(FP8))
 
         def turn(j, c, tag="turn"):
-            bank = psum.tile([P, 2, 2, P], F32, name=f"xt{j}{c}", tag=tag)
+            bank = psum.tile([P, 2, P, 2], F32, name=f"xt{j}{c}", tag=tag)
             live["xt", j, c] = bank
             for i in range(2):
                 src = live["xv", j, c, i][:] if c < XP else eb[j][:, E * i:E * i + E]
                 words = src.bitcast(F32)
                 for u in range(2):
-                    nc.tensor.transpose(bank[:, i, u, :], words[:, u::2], ident[:])
+                    nc.tensor.transpose(bank[:, i, :, u], words[:, u::2], ident[:])
 
         def empty_turn(j, c):
             h, half = divmod(j, 2)
             if half == 0:
                 live["xg", h, c] = stage.tile([P, 4 * W], BF16, name=f"xg{h}{c}", tag="xg", bufs=4, align_bytes=256)
             dst = live["xg", h, c][:, 2 * W * half:2 * W * half + 2 * W]
-            nc.scalar.copy(
-                out=dst.bitcast(F32).rearrange("p (i r u) -> p i r u", i=2, u=2),
-                in_=live["xt", j, c][:].rearrange("p i u r -> p i r u"),
-            )
+            words = live["xt", j, c][:].rearrange("p i r u -> p (i r u)")
+            if c == EP:
+                nc.scalar.copy(out=dst.bitcast(F32), in_=words)
+            else:
+                nc.vector.tensor_tensor(
+                    out=dst.rearrange("p (s t) -> p s t", t=4),
+                    in0=words.bitcast(BF16).rearrange("p (s t) -> p s t", t=4),
+                    in1=scale_col[:, c:c + 1, :].to_broadcast([P, 2 * P, 4]), op=ALU.mult,
+                )
 
         def quantize_x(h, c):
             nc.vector.quantize_mx(out=xq[h][c][:].bitcast(FP8X4), scales=xs[h][c][:], in_=live["xg", h, c][:])
@@ -167,7 +168,7 @@ def tile_clipped_feedback_control_s3_kernel(
                 nc.scalar.copy(out=dst, in_=src)
 
         def interleave_f_half(c, g, k, on_vector=False, cut=32):
-            if k == 0:
+            if ("fg", c, g) not in live:
                 live["fg", c, g] = stage.tile([P, 4 * W], BF16, name=f"fg{c}{g}", tag="fg", bufs=3, align_bytes=256)
             m = slice(cut, 64) if k else slice(0, cut)
             src = fr[c][g][:].rearrange("p j (m r t) -> p m t j r", r=2, t=4)
@@ -182,7 +183,7 @@ def tile_clipped_feedback_control_s3_kernel(
 
         def action_pass(h, g, t, c, order):
             if c == order[0]:
-                live["acc", h, g, t] = psum.tile([P, W], F32, name=f"acc{h}{g}{t}", tag="turn" if g == 1 else "acc")
+                live["acc", h, g, t] = psum.tile([P, W], F32, name=f"acc{h}{g}{t}", tag="turn" if (h, g) == (0, 1) else "acc")
             cols = slice(P * t, P * t + P)
             if c < XP:
                 w, ws = fq[c][g][:, cols].bitcast(FP8X4), fs[c][g][:, cols]
@@ -200,11 +201,11 @@ def tile_clipped_feedback_control_s3_kernel(
 
         def empty_action(h, g, t, on_vector=False):
             if t == 0:
-                live["up", h, g] = stage.tile([P, 4, W], BF16, name=f"up{h}{g}", tag="up", bufs=3)
+                live["up", h, g] = stage.tile([P, 4, W], BF16, name=f"up{h}{g}", tag="up", bufs=4)
             u = live["up", h, g][:, t, :]
             if on_vector:
                 nc.vector.tensor_scalar(
-                    out=u, in0=live["acc", h, g, t][:], scalar1=lim_bf[0][:, g, t:t + 1], scalar2=lim_bf[1][:, g, t:t + 1],
+                    out=u, in0=live["acc", h, g, t][:], scalar1=lim[:, 0, g, t:t + 1], scalar2=lim[:, 1, g, t:t + 1],
                     op0=ALU.min, op1=ALU.max,
                 )
             else:
@@ -213,7 +214,7 @@ def tile_clipped_feedback_control_s3_kernel(
         def clip(h, g, t):
             u = live["up", h, g][:, t, :]
             nc.vector.tensor_scalar(
-                out=u, in0=u, scalar1=lim_bf[0][:, g, t:t + 1], scalar2=lim_bf[1][:, g, t:t + 1], op0=ALU.min, op1=ALU.max
+                out=u, in0=u, scalar1=lim[:, 0, g, t:t + 1], scalar2=lim[:, 1, g, t:t + 1], op0=ALU.min, op1=ALU.max
             )
 
         def interleave_u(h, g, k, on_vector=False):
@@ -259,13 +260,6 @@ def tile_clipped_feedback_control_s3_kernel(
             rows = pair_rows(out, j).rearrange("p i k -> p (i k)")
             queue.dma_start(out=rows[:, cols], in_=live["ot", j][:, cols])
 
-        def samples_pass(h, c):
-            for j in (2 * h, 2 * h + 1):
-                if c < XP:
-                    scale_x(j, c)
-                turn(j, c)
-                empty_turn(j, c)
-
         def block_pass(h, g, c, order):
             for t in range(4):
                 action_pass(h, g, t, c, order)
@@ -275,14 +269,6 @@ def tile_clipped_feedback_control_s3_kernel(
                 turn(j, c)
                 empty_turn(j, c)
 
-        def scale_pass(h, c):
-            for j in (2 * h, 2 * h + 1):
-                scale_x(j, c)
-
-        def turn_only(h, c):
-            for j in (2 * h, 2 * h + 1):
-                turn(j, c)
-
         def empty_pass(h, c):
             for j in (2 * h, 2 * h + 1):
                 empty_turn(j, c)
@@ -291,120 +277,115 @@ def tile_clipped_feedback_control_s3_kernel(
             for t in (2 * k, 2 * k + 1):
                 action_pass(h, g, t, c, order)
 
-        order = (EP, 0, 1, 2)
-        for c in range(XP):
-            spread_scales(c)
-        scale_x(0, 0)
+        order = (0, EP, 1, 2)
+        for j in range(2):
+            for c in range(2):
+                widen_x(j, c)
+                turn(j, c)
+        for j in range(2):
+            widen_x(j, 2)
+        empty_turn(0, 0)
+        turn(0, 2)
+        empty_turn(0, 1)
+        turn(1, 2)
+        empty_turn(1, 0)
+        interleave_f(0, 0)
         turn(0, EP, "acc")
         turn(1, EP, "acc")
         empty_pass(0, EP)
-        turn(0, 0)
-        interleave_f(0, 0)
-        scale_x(0, 1)
-        turn(0, 1)
-        quantize_x(0, EP)
         permute_l_words(0)
-        permute_l_scales(0)
-        scale_x(1, 0)
-        pair_pass(0, 0, 0, EP, order)
-        turn(1, 0)
-        empty_turn(0, 0)
-        empty_turn(0, 1)
-        empty_turn(1, 0)
-        quantize_f(0, 0)
-        scale_x(1, 1)
-        pair_pass(0, 0, 1, EP, order)
-        turn(1, 1)
-        interleave_f(1, 0)
         quantize_x(0, 0)
-        scale_pass(0, 2)
-        pair_pass(0, 0, 0, 0, order)
-        turn(0, 2)
-        pair_pass(0, 0, 1, 0, order)
+        permute_l_scales(0)
+        quantize_f(0, 0)
+        block_pass(0, 0, 0, order)
         empty_turn(1, 1)
-        turn(1, 2)
-        turn(2, EP)
-        interleave_f_half(2, 0, 0, False, 44)
-        quantize_f(1, 0)
+        quantize_x(0, EP)
+        interleave_f(1, 0)
         quantize_x(0, 1)
-        interleave_f_half(2, 0, 1, True, 44)
-        empty_pass(0, 2)
-        block_pass(0, 0, 1, order)
+        block_pass(0, 0, EP, order)
+        empty_turn(0, 2)
+        turn(2, EP)
         turn(3, EP)
-        empty_pass(1, EP)
-        scale_x(2, 0)
-        quantize_f(2, 0)
+        quantize_f(1, 0)
+        interleave_f_half(2, 0, 0, False, 40)
+        widen_x(2, 0)
+        widen_x(3, 0)
+        empty_turn(1, 2)
+        block_pass(0, 0, 1, order)
+        interleave_f_half(2, 0, 1, True, 40)
         quantize_x(0, 2)
         turn(2, 0)
-        empty_turn(2, 0)
-        block_pass(0, 0, 2, order)
-        scale_x(3, 0)
-        quantize_x(1, EP)
         turn(3, 0)
+        empty_pass(1, EP)
+        quantize_f(2, 0)
+        for c in range(1, XP):
+            widen_x(2, c)
+            widen_x(3, c)
+        block_pass(0, 0, 2, order)
+        turn(2, 1)
+        turn(3, 1)
+        empty_pass(1, 0)
+        quantize_x(1, EP)
         for t in range(4):
             empty_action(0, 0, t)
-        empty_turn(3, 0)
-        interleave_f_half(0, 1, 0)
-        scale_pass(1, 1)
-        block_pass(1, 0, EP, order)
-        turn_pass(1, 1)
         quantize_x(1, 0)
-        scale_pass(1, 2)
-        interleave_f_half(0, 1, 1)
+        order = (EP, 0, 1, 2)
+        block_pass(1, 0, EP, order)
+        interleave_f(0, 1)
+        turn(2, 2)
+        turn(3, 2)
+        empty_pass(1, 1)
         block_pass(1, 0, 0, order)
-        turn_pass(1, 2)
-        interleave_f_half(1, 1, 0)
-        quantize_x(1, 1)
         permute_l_words(1)
+        quantize_x(1, 1)
         permute_l_scales(1)
+        interleave_f(2, 1)
         block_pass(1, 0, 1, order)
-        interleave_f_half(1, 1, 1)
+        empty_turn(2, 2)
         quantize_f(0, 1)
-        interleave_f(2, 1, True)
+        empty_turn(3, 2)
         late = (EP, 0, 2, 1)
         for c in late[:2]:
             pair_pass(0, 1, 0, c, late)
+        widen_limits()
+        interleave_f(1, 1)
+        quantize_x(1, 2)
         quantize_f(2, 1)
+        for c in late[:2]:
+            pair_pass(0, 1, 1, c, late)
         for t in range(4):
             clip(0, 0, t)
         quantize_f(1, 1)
-        quantize_x(1, 2)
-        for k in range(2):
-            interleave_u(0, 0, k, k == 1)
-        for c in late[:2]:
-            pair_pass(0, 1, 1, c, late)
+        block_pass(1, 0, 2, order)
         for c in late[2:]:
             block_pass(0, 1, c, late)
-        block_pass(1, 0, 2, order)
+        for t in range(4):
+            empty_action(1, 0, t, t >= 2)
+        interleave_u(0, 0, 0)
+        for t in range(2):
+            clip(1, 0, t)
         for t in range(4):
             empty_action(0, 1, t, t >= 2)
-        quantize_u(0, 0, 0)
+        for t in range(3):
+            action(1, 1, t)
+        interleave_u(0, 0, 1)
         for t in range(2):
             clip(0, 1, t)
-        quantize_u(0, 0, 1)
+        quantize_u(0, 0, 0)
         interleave_u(0, 1, 0, True)
-        for t in range(4):
-            empty_action(1, 0, t)
         interleave_u(0, 1, 1)
-        for t in range(2):
-            clip(1, 0, t)
+        quantize_u(0, 0, 1)
         quantize_u(0, 1, 0)
-        for t in range(2, 4):
-            clip(1, 0, t)
-        for t in range(2):
-            action(1, 1, t)
-        for k in range(2):
-            interleave_u(1, 0, k)
+        for t in range(3):
+            empty_action(1, 1, t)
+        interleave_u(1, 0, 0)
         steps = [(i, n) for i in range(8) for n in range(3)]
         for s, (i, n) in enumerate(steps):
             if s == 3:
-                action(1, 1, 2)
-                for t in range(3):
-                    empty_action(1, 1, t)
-            if s == 6:
                 action(1, 1, 3)
                 empty_action(1, 1, 3)
-            rate(i, n, "acc" if s % 2 == 0 or s < 8 else "turn")
+                interleave_u(1, 0, 1)
+            rate(i, n, "turn" if s % 2 == 0 or s < 8 else "acc")
             add_drift(i, n)
             if s < 6 or s >= 22:
                 store(s, 1, nc.scalar if s == 22 else nc.sync)
@@ -412,16 +393,17 @@ def tile_clipped_feedback_control_s3_kernel(
                 store(s - 1, 2, nc.scalar if s >= 10 and s % 4 == 3 else nc.sync)
             if s == 1:
                 quantize_u(0, 1, 1)
-                quantize_u(1, 0, 0)
-            if s == 5:
-                quantize_u(1, 0, 1)
+            if s == 2:
                 for t in range(3):
                     clip(1, 1, t)
-            if s == 6:
+                quantize_u(1, 0, 0)
+            if s == 3:
                 clip(1, 1, 3)
                 interleave_u(1, 1, 0)
                 interleave_u(1, 1, 1)
-            if s == 9:
+            if s == 5:
+                quantize_u(1, 0, 1)
+            if s == 8:
                 quantize_u(1, 1, 0)
             if s == 11:
                 quantize_u(1, 1, 1)

@@ -40,7 +40,7 @@ def tile_clipped_feedback_control_s3_kernel(
         nc.vector.memset(b_plane[:].rearrange("p g n -> p (g n)").bitcast(I32), 0)
 
         scale_col = keep.tile([P, XP, 4], F32, name="scale_col")
-        l_raw = [keep.tile([P, A], U8, name=f"l_raw{g}") for g in range(2)]
+        l_raw = keep.tile([P, 2 * A], U8, name="l_raw")
         lim_bf = [keep.tile([P, 2, 4], BF16, name=f"lim_bf{k}") for k in range(2)]
         xb = [keep.tile([P, 2, S], U8, name=f"xb{j}") for j in range(4)]
         eb = [keep.tile([P, 2 * E], BF16, name=f"eb{j}") for j in range(4)]
@@ -57,9 +57,6 @@ def tile_clipped_feedback_control_s3_kernel(
         def load_e(j):
             nc.sync.dma_start(out=eb[j][:], in_=pair_rows(e, j).rearrange("p i k -> p (i k)"))
 
-        def load_l(g):
-            nc.sync.dma_start(out=l_raw[g][:], in_=L_words[0, :, A * g:A * g + A])
-
         def load_f(c, g):
             nc.sync.dma_start(
                 out=fr[c][g][:], in_=F[W * c:W * c + W, W * g:W * g + W].rearrange("(p j) a -> p j a", j=4)
@@ -68,26 +65,25 @@ def tile_clipped_feedback_control_s3_kernel(
         load_x(0)
         nc.sync.dma_start(out=scale_col[:], in_=x_scale.rearrange("o (c p j) -> p (o c) j", p=P, j=4))
         load_x(1)
-        load_l(0)
         for q in range(4):
             nc.sync.dma_start(
                 out=l_plane[32 * q:32 * q + 4, :].bitcast(I32), in_=L_scales[0, 4 * q:4 * q + 4, :].bitcast(I32)
             )
         load_f(0, 0)
+        nc.sync.dma_start(out=l_raw[:], in_=L_words[0])
         load_e(0)
         load_e(1)
         load_f(1, 0)
         load_f(2, 0)
+        load_x(2)
         load_e(2)
         load_e(3)
-        load_x(2)
-        nc.sync.dma_start(out=lim_bf[0][:], in_=hi.rearrange("(g p t) -> p g t", p=P, t=4))
-        nc.sync.dma_start(out=lim_bf[1][:], in_=lo.rearrange("(g p t) -> p g t", p=P, t=4))
         load_x(3)
         load_f(0, 1)
-        load_l(1)
-        load_f(1, 1)
+        nc.sync.dma_start(out=lim_bf[0][:], in_=hi.rearrange("(g p t) -> p g t", p=P, t=4))
+        nc.sync.dma_start(out=lim_bf[1][:], in_=lo.rearrange("(g p t) -> p g t", p=P, t=4))
         load_f(2, 1)
+        load_f(1, 1)
         nc.sync.dma_start(out=bw[:], in_=B_words.rearrange("g p n -> p g n"))
         for q in range(4):
             nc.sync.dma_start(
@@ -106,12 +102,19 @@ def tile_clipped_feedback_control_s3_kernel(
         xs = [[keep.tile([P, W], U8, name=f"xs{h}{c}", align_bytes=256) for c in range(XP + 1)] for h in range(2)]
         uq = [[keep.tile([P, W], U32, name=f"uq{h}{g}", align_bytes=256) for g in range(2)] for h in range(2)]
         us = [[keep.tile([P, W], U8, name=f"us{h}{g}", align_bytes=256) for g in range(2)] for h in range(2)]
+        xv = [stage.tile([P, 2, S], BF16, name=f"xv{j}", tag="xv", bufs=2) for j in range(4)]
         live = {}
+
+        follows = {"fg20": "fg00", "fg01": "fg00", "xg10": "xg02", "xg12": "xg02", "xg11": "xg03", "fg11": "xg03",
+                   "xg13": "xg00", "fg21": "xg01"}
+
+        def grouped(name):
+            return stage.tile([P, 4 * W], BF16, name=name, tag=follows.get(name, name), bufs=1, align_bytes=256)
 
         def permute_l_words(g):
             nc.vector.tensor_copy(
                 out=lw[:, g].bitcast(U16).rearrange("p t m -> p m t"),
-                in_=l_raw[g][:].bitcast(U16).rearrange("p (m t) -> p m t", t=4),
+                in_=l_raw[:, A * g:A * g + A].bitcast(U16).rearrange("p (m t) -> p m t", t=4),
             )
 
         def permute_l_scales(g):
@@ -124,59 +127,64 @@ def tile_clipped_feedback_control_s3_kernel(
             for k in range(2):
                 nc.vector.tensor_copy(out=lim[:, k], in_=lim_bf[k][:])
 
-        def widen_x(j, c):
+        def widen_x(j, first=0, last=XP):
             for i in range(2):
-                xv = stage.tile([P, W], BF16, name=f"xv{j}{c}{i}", tag="xv", bufs=12)
-                live["xv", j, c, i] = xv
-                nc.scalar.copy(out=xv[:], in_=xb[j][:, i, W * c:W * c + W].bitcast(FP8))
+                cols = slice(W * first, W * last)
+                nc.scalar.copy(out=xv[j][:, i, cols], in_=xb[j][:, i, cols].bitcast(FP8))
 
         def turn(j, c, tag="turn"):
             bank = psum.tile([P, 2, P, 2], F32, name=f"xt{j}{c}", tag=tag)
             live["xt", j, c] = bank
             for i in range(2):
-                src = live["xv", j, c, i][:] if c < XP else eb[j][:, E * i:E * i + E]
+                src = xv[j][:, i, W * c:W * c + W] if c < XP else eb[j][:, E * i:E * i + E]
                 words = src.bitcast(F32)
                 for u in range(2):
                     nc.tensor.transpose(bank[:, i, :, u], words[:, u::2], ident[:])
 
-        def empty_turn(j, c):
+        def grouped_half(j, c):
             h, half = divmod(j, 2)
-            if half == 0:
-                live["xg", h, c] = stage.tile([P, 4 * W], BF16, name=f"xg{h}{c}", tag="xg", bufs=4, align_bytes=256)
-            dst = live["xg", h, c][:, 2 * W * half:2 * W * half + 2 * W]
+            if ("xg", h, c) not in live:
+                live["xg", h, c] = grouped(f"xg{h}{c}")
+            return live["xg", h, c][:, 2 * W * half:2 * W * half + 2 * W]
+
+        def scaled(engine, j, c, values):
+            engine.tensor_tensor(
+                out=grouped_half(j, c).rearrange("p (s t) -> p s t", t=4), in0=values.rearrange("p (s t) -> p s t", t=4),
+                in1=scale_col[:, c:c + 1, :].to_broadcast([P, 2 * P, 4]), op=ALU.mult,
+            )
+
+        def empty_turn(j, c):
             words = live["xt", j, c][:].rearrange("p i r u -> p (i r u)")
             if c == EP:
-                nc.scalar.copy(out=dst.bitcast(F32), in_=words)
+                nc.scalar.copy(out=grouped_half(j, c).bitcast(F32), in_=words)
             else:
-                nc.vector.tensor_tensor(
-                    out=dst.rearrange("p (s t) -> p s t", t=4),
-                    in0=words.bitcast(BF16).rearrange("p (s t) -> p s t", t=4),
-                    in1=scale_col[:, c:c + 1, :].to_broadcast([P, 2 * P, 4]), op=ALU.mult,
-                )
+                scaled(nc.vector, j, c, words.bitcast(BF16))
+
+        def park_turn(j, c):
+            live["xp", j, c] = stage.tile([P, W], F32, name=f"xp{j}{c}", tag="xp", bufs=2)
+            nc.scalar.copy(out=live["xp", j, c][:], in_=live["xt", j, c][:].rearrange("p i r u -> p (i r u)"))
+
+        def scale_parked(j, c):
+            scaled(nc.gpsimd, j, c, live["xp", j, c][:].bitcast(BF16))
 
         def quantize_x(h, c):
             nc.vector.quantize_mx(out=xq[h][c][:].bitcast(FP8X4), scales=xs[h][c][:], in_=live["xg", h, c][:])
 
-        def interleave_f(c, g, on_vector=False):
-            fg = stage.tile([P, 4 * W], BF16, name=f"fg{c}{g}", tag="fg", bufs=3, align_bytes=256)
-            live["fg", c, g] = fg
-            src = fr[c][g][:].rearrange("p j (m r t) -> p m t j r", r=2, t=4)
-            dst = fg[:].rearrange("p (t m r j) -> p m t j r", t=4, r=2, j=4)
-            if on_vector:
+        def interleave_f(c, g, first=0, last=128, engine=nc.scalar):
+            if ("fg", c, g) not in live:
+                live["fg", c, g] = grouped(f"fg{c}{g}")
+            if engine is nc.gpsimd:
+                src = fr[c][g][:].rearrange("p j (m t) -> p m t j", t=4)[:, first:last]
+                dst = live["fg", c, g][:].rearrange("p (t m j) -> p m t j", t=4, j=4)[:, first:last]
+                nc.gpsimd.tensor_scalar(out=dst, in0=src, scalar1=1.0, scalar2=0.0, op0=ALU.mult, op1=ALU.add)
+                return
+            m = slice(first // 2, last // 2)
+            src = fr[c][g][:].rearrange("p j (m r t) -> p m t j r", r=2, t=4)[:, m]
+            dst = live["fg", c, g][:].rearrange("p (t m r j) -> p m t j r", t=4, r=2, j=4)[:, m]
+            if engine is nc.vector:
                 nc.vector.tensor_copy(out=dst, in_=src)
             else:
                 nc.scalar.copy(out=dst, in_=src)
-
-        def interleave_f_half(c, g, k, on_vector=False, cut=32):
-            if ("fg", c, g) not in live:
-                live["fg", c, g] = stage.tile([P, 4 * W], BF16, name=f"fg{c}{g}", tag="fg", bufs=3, align_bytes=256)
-            m = slice(cut, 64) if k else slice(0, cut)
-            src = fr[c][g][:].rearrange("p j (m r t) -> p m t j r", r=2, t=4)
-            dst = live["fg", c, g][:].rearrange("p (t m r j) -> p m t j r", t=4, r=2, j=4)
-            if on_vector:
-                nc.vector.tensor_copy(out=dst[:, m], in_=src[:, m])
-            else:
-                nc.scalar.copy(out=dst[:, m], in_=src[:, m])
 
         def quantize_f(c, g):
             nc.vector.quantize_mx(out=fq[c][g][:].bitcast(FP8X4), scales=fs[c][g][:], in_=live["fg", c, g][:])
@@ -278,81 +286,84 @@ def tile_clipped_feedback_control_s3_kernel(
                 action_pass(h, g, t, c, order)
 
         order = (0, EP, 1, 2)
-        for j in range(2):
-            for c in range(2):
-                widen_x(j, c)
-                turn(j, c)
-        for j in range(2):
-            widen_x(j, 2)
+        for c in range(XP):
+            widen_x(0, c, c + 1)
+            turn(0, c)
+        widen_x(1, 0, 2)
+        turn(1, 0)
+        park_turn(0, 2)
+        scale_parked(0, 2)
+        widen_x(1, 2, 3)
         empty_turn(0, 0)
-        turn(0, 2)
+        turn(1, 1)
         empty_turn(0, 1)
         turn(1, 2)
         empty_turn(1, 0)
+        empty_turn(1, 1)
         interleave_f(0, 0)
         turn(0, EP, "acc")
         turn(1, EP, "acc")
         empty_pass(0, EP)
-        permute_l_words(0)
         quantize_x(0, 0)
-        permute_l_scales(0)
         quantize_f(0, 0)
         block_pass(0, 0, 0, order)
-        empty_turn(1, 1)
+        permute_l_words(0)
         quantize_x(0, EP)
+        permute_l_scales(0)
         interleave_f(1, 0)
-        quantize_x(0, 1)
         block_pass(0, 0, EP, order)
-        empty_turn(0, 2)
+        empty_turn(1, 2)
+        quantize_x(0, 1)
         turn(2, EP)
         turn(3, EP)
         quantize_f(1, 0)
-        interleave_f_half(2, 0, 0, False, 40)
-        widen_x(2, 0)
-        widen_x(3, 0)
-        empty_turn(1, 2)
+        interleave_f(2, 0, 0, 64)
+        widen_x(2, 0, 1)
+        widen_x(3, 0, 1)
         block_pass(0, 0, 1, order)
-        interleave_f_half(2, 0, 1, True, 40)
+        interleave_f(2, 0, 64, 128, nc.vector)
         quantize_x(0, 2)
         turn(2, 0)
         turn(3, 0)
         empty_pass(1, EP)
+        permute_l_words(1)
+        permute_l_scales(1)
         quantize_f(2, 0)
-        for c in range(1, XP):
-            widen_x(2, c)
-            widen_x(3, c)
-        block_pass(0, 0, 2, order)
+        widen_x(2, 1, 3)
+        widen_x(3, 1, 3)
+        pair_pass(0, 0, 0, 2, order)
         turn(2, 1)
+        pair_pass(0, 0, 1, 2, order)
         turn(3, 1)
+        interleave_f(0, 1, 64, 128, nc.gpsimd)
         empty_pass(1, 0)
         quantize_x(1, EP)
-        for t in range(4):
+        for t in range(3):
             empty_action(0, 0, t)
-        quantize_x(1, 0)
-        order = (EP, 0, 1, 2)
-        block_pass(1, 0, EP, order)
-        interleave_f(0, 1)
-        turn(2, 2)
         turn(3, 2)
+        park_turn(3, 2)
+        empty_action(0, 0, 3)
+        quantize_x(1, 0)
+        scale_parked(3, 2)
+        order = (EP, 0, 1, 2)
+        pair_pass(1, 0, 0, EP, order)
+        turn(2, 2)
+        pair_pass(1, 0, 1, EP, order)
+        interleave_f(0, 1, 0, 64)
         empty_pass(1, 1)
-        block_pass(1, 0, 0, order)
-        permute_l_words(1)
-        quantize_x(1, 1)
-        permute_l_scales(1)
-        interleave_f(2, 1)
-        block_pass(1, 0, 1, order)
         empty_turn(2, 2)
+        block_pass(1, 0, 0, order)
+        interleave_f(2, 1)
+        quantize_x(1, 1)
         quantize_f(0, 1)
-        empty_turn(3, 2)
         late = (EP, 0, 2, 1)
-        for c in late[:2]:
-            pair_pass(0, 1, 0, c, late)
-        widen_limits()
+        block_pass(0, 1, EP, late)
+        block_pass(1, 0, 1, order)
+        block_pass(0, 1, 0, late)
         interleave_f(1, 1)
         quantize_x(1, 2)
+        widen_limits()
         quantize_f(2, 1)
-        for c in late[:2]:
-            pair_pass(0, 1, 1, c, late)
         for t in range(4):
             clip(0, 0, t)
         quantize_f(1, 1)

@@ -207,20 +207,20 @@ def tile_clipped_feedback_control_s3_kernel(
             for c in range(XP + 1):
                 action_pass(h, g, t, c, range(XP + 1))
 
-        def empty_action(h, g, t, on_vector=False):
-            if t == 0:
+        def empty_action(h, g, t, on_vector=False, cols=slice(0, W)):
+            if ("up", h, g) not in live:
                 live["up", h, g] = stage.tile([P, 4, W], BF16, name=f"up{h}{g}", tag="up", bufs=4)
-            u = live["up", h, g][:, t, :]
+            u = live["up", h, g][:, t, cols]
             if on_vector:
                 nc.vector.tensor_scalar(
-                    out=u, in0=live["acc", h, g, t][:], scalar1=lim[:, 0, g, t:t + 1], scalar2=lim[:, 1, g, t:t + 1],
+                    out=u, in0=live["acc", h, g, t][:, cols], scalar1=lim[:, 0, g, t:t + 1], scalar2=lim[:, 1, g, t:t + 1],
                     op0=ALU.min, op1=ALU.max,
                 )
             else:
-                nc.scalar.copy(out=u, in_=live["acc", h, g, t][:])
+                nc.scalar.copy(out=u, in_=live["acc", h, g, t][:, cols])
 
-        def clip(h, g, t):
-            u = live["up", h, g][:, t, :]
+        def clip(h, g, t, cols=slice(0, W)):
+            u = live["up", h, g][:, t, cols]
             nc.vector.tensor_scalar(
                 out=u, in0=u, scalar1=lim[:, 0, g, t:t + 1], scalar2=lim[:, 1, g, t:t + 1], op0=ALU.min, op1=ALU.max
             )
@@ -257,10 +257,12 @@ def tile_clipped_feedback_control_s3_kernel(
             if chunk == 0:
                 live["ot", j] = stage.tile([P, 2 * S], F32, name=f"ot{j}", tag="ot", bufs=3)
             cols = slice(W * chunk, W * chunk + W)
-            nc.vector.tensor_tensor(
-                out=live["ot", j][:, cols], in0=live["y", i, n][:],
-                in1=dr[j][:].rearrange("p i k -> p (i k)")[:, cols], op=ALU.add,
-            )
+            dst, given = live["ot", j][:, cols], dr[j][:].rearrange("p i k -> p (i k)")[:, cols]
+            if XP * i + n in by_gpsimd:
+                nc.scalar.copy(out=dst, in_=live["y", i, n][:])
+                nc.gpsimd.tensor_tensor(out=dst, in0=dst, in1=given, op=ALU.add)
+            else:
+                nc.vector.tensor_tensor(out=dst, in0=live["y", i, n][:], in1=given, op=ALU.add)
 
         def store(first, count, queue=nc.sync):
             j, chunk = divmod(first, 2 * XP)
@@ -286,14 +288,14 @@ def tile_clipped_feedback_control_s3_kernel(
                 action_pass(h, g, t, c, order)
 
         order = (0, EP, 1, 2)
-        for c in range(XP):
+        for c in (0, 2, 1):
             widen_x(0, c, c + 1)
             turn(0, c)
-        widen_x(1, 0, 2)
+        widen_x(1, 0, 1)
         turn(1, 0)
         park_turn(0, 2)
         scale_parked(0, 2)
-        widen_x(1, 2, 3)
+        widen_x(1, 1, 3)
         empty_turn(0, 0)
         turn(1, 1)
         empty_turn(0, 1)
@@ -375,46 +377,53 @@ def tile_clipped_feedback_control_s3_kernel(
         interleave_u(0, 0, 0)
         for t in range(2):
             clip(1, 0, t)
+        halves = (slice(0, W // 2), slice(W // 2, W))
         for t in range(4):
-            empty_action(0, 1, t, t >= 2)
-        for t in range(3):
-            action(1, 1, t)
+            empty_action(0, 1, t, True, halves[0])
         interleave_u(0, 0, 1)
+        for t in range(4):
+            empty_action(0, 1, t, False, halves[1])
         for t in range(2):
-            clip(0, 1, t)
+            action(1, 1, t)
         quantize_u(0, 0, 0)
         interleave_u(0, 1, 0, True)
-        interleave_u(0, 1, 1)
         quantize_u(0, 0, 1)
         quantize_u(0, 1, 0)
-        for t in range(3):
-            empty_action(1, 1, t)
+        for t in range(4):
+            clip(0, 1, t, halves[1])
         interleave_u(1, 0, 0)
+        interleave_u(0, 1, 1)
+        for t in range(2):
+            empty_action(1, 1, t)
+        by_gpsimd = ()
         steps = [(i, n) for i in range(8) for n in range(3)]
         for s, (i, n) in enumerate(steps):
             if s == 3:
+                action(1, 1, 2)
+                empty_action(1, 1, 2)
+                interleave_u(1, 0, 1)
+            if s == 5:
                 action(1, 1, 3)
                 empty_action(1, 1, 3)
-                interleave_u(1, 0, 1)
             rate(i, n, "turn" if s % 2 == 0 or s < 8 else "acc")
             add_drift(i, n)
             if s < 6 or s >= 22:
                 store(s, 1, nc.scalar if s == 22 else nc.sync)
             elif s % 2 == 1:
                 store(s - 1, 2, nc.scalar if s >= 10 and s % 4 == 3 else nc.sync)
-            if s == 1:
-                quantize_u(0, 1, 1)
             if s == 2:
+                quantize_u(0, 1, 1)
+                quantize_u(1, 0, 0)
+            if s == 5 - 1:
                 for t in range(3):
                     clip(1, 1, t)
-                quantize_u(1, 0, 0)
-            if s == 3:
+            if s == 5:
                 clip(1, 1, 3)
                 interleave_u(1, 1, 0)
                 interleave_u(1, 1, 1)
-            if s == 5:
-                quantize_u(1, 0, 1)
-            if s == 8:
+            if s == 9:
                 quantize_u(1, 1, 0)
-            if s == 11:
+            if s == 13:
+                quantize_u(1, 0, 1)
+            if s == 15:
                 quantize_u(1, 1, 1)

@@ -93,7 +93,6 @@ def tile_clipped_feedback_control_s3_kernel(
         for j in range(4):
             nc.sync.dma_start(out=dr[j][:], in_=pair_rows(drift, j))
 
-        lim = keep.tile([P, 2, 2, 4], F32, name="lim")
         lw = keep.tile([P, 2, 4, 256], U8, name="lw", align_bytes=256)
         ls = keep.tile([P, 2, 4, P], U8, name="ls", align_bytes=256)
         fq = [[keep.tile([P, W], U32, name=f"fq{c}{g}", align_bytes=256) for g in range(2)] for c in range(XP)]
@@ -122,10 +121,6 @@ def tile_clipped_feedback_control_s3_kernel(
                 out=ls[:, g].rearrange("p t m -> p m t"),
                 in_=l_plane[:, W * g:W * g + W].rearrange("p (m t) -> p m t", t=4),
             )
-
-        def widen_limits():
-            for k in range(2):
-                nc.vector.tensor_copy(out=lim[:, k], in_=lim_bf[k][:])
 
         def widen_x(j, first=0, last=XP):
             for i in range(2):
@@ -213,7 +208,7 @@ def tile_clipped_feedback_control_s3_kernel(
             u = live["up", h, g][:, t, cols]
             if on_vector:
                 nc.vector.tensor_scalar(
-                    out=u, in0=live["acc", h, g, t][:, cols], scalar1=lim[:, 0, g, t:t + 1], scalar2=lim[:, 1, g, t:t + 1],
+                    out=u, in0=live["acc", h, g, t][:, cols], scalar1=lim_bf[0][:, g, t:t + 1], scalar2=lim_bf[1][:, g, t:t + 1],
                     op0=ALU.min, op1=ALU.max,
                 )
             else:
@@ -222,7 +217,7 @@ def tile_clipped_feedback_control_s3_kernel(
         def clip(h, g, t, cols=slice(0, W)):
             u = live["up", h, g][:, t, cols]
             nc.vector.tensor_scalar(
-                out=u, in0=u, scalar1=lim[:, 0, g, t:t + 1], scalar2=lim[:, 1, g, t:t + 1], op0=ALU.min, op1=ALU.max
+                out=u, in0=u, scalar1=lim_bf[0][:, g, t:t + 1], scalar2=lim_bf[1][:, g, t:t + 1], op0=ALU.min, op1=ALU.max
             )
 
         def interleave_u(h, g, k, on_vector=False):
@@ -331,27 +326,28 @@ def tile_clipped_feedback_control_s3_kernel(
         permute_l_words(1)
         permute_l_scales(1)
         quantize_f(2, 0)
-        widen_x(2, 1, 3)
         widen_x(3, 1, 3)
+        widen_x(2, 1, 3)
         pair_pass(0, 0, 0, 2, order)
-        turn(2, 1)
-        pair_pass(0, 0, 1, 2, order)
-        turn(3, 1)
-        interleave_f(0, 1, 64, 128, nc.gpsimd)
+        interleave_f(0, 1, 80, 128, nc.gpsimd)
         empty_pass(1, 0)
-        quantize_x(1, EP)
-        for t in range(3):
-            empty_action(0, 0, t)
         turn(3, 2)
+        pair_pass(0, 0, 1, 2, order)
+        turn(2, 1)
+        quantize_x(1, EP)
+        for t in range(2):
+            empty_action(0, 0, t)
         park_turn(3, 2)
-        empty_action(0, 0, 3)
+        for t in range(2, 4):
+            empty_action(0, 0, t)
         quantize_x(1, 0)
         scale_parked(3, 2)
         order = (EP, 0, 1, 2)
+        turn(3, 1)
         pair_pass(1, 0, 0, EP, order)
         turn(2, 2)
         pair_pass(1, 0, 1, EP, order)
-        interleave_f(0, 1, 0, 64)
+        interleave_f(0, 1, 0, 80)
         empty_pass(1, 1)
         empty_turn(2, 2)
         block_pass(1, 0, 0, order)
@@ -364,7 +360,6 @@ def tile_clipped_feedback_control_s3_kernel(
         block_pass(0, 1, 0, late)
         interleave_f(1, 1)
         quantize_x(1, 2)
-        widen_limits()
         quantize_f(2, 1)
         for t in range(4):
             clip(0, 0, t)
@@ -375,8 +370,6 @@ def tile_clipped_feedback_control_s3_kernel(
         for t in range(4):
             empty_action(1, 0, t, t >= 2)
         interleave_u(0, 0, 0)
-        for t in range(2):
-            clip(1, 0, t)
         halves = (slice(0, W // 2), slice(W // 2, W))
         for t in range(4):
             empty_action(0, 1, t, True, halves[0])
@@ -387,10 +380,12 @@ def tile_clipped_feedback_control_s3_kernel(
             action(1, 1, t)
         quantize_u(0, 0, 0)
         interleave_u(0, 1, 0, True)
-        quantize_u(0, 0, 1)
+        for t in range(2):
+            clip(1, 0, t)
         quantize_u(0, 1, 0)
         for t in range(4):
             clip(0, 1, t, halves[1])
+        quantize_u(0, 0, 1)
         interleave_u(1, 0, 0)
         interleave_u(0, 1, 1)
         for t in range(2):
@@ -400,8 +395,8 @@ def tile_clipped_feedback_control_s3_kernel(
         for s, (i, n) in enumerate(steps):
             if s == 3:
                 action(1, 1, 2)
-                empty_action(1, 1, 2)
                 interleave_u(1, 0, 1)
+                empty_action(1, 1, 2)
             if s == 5:
                 action(1, 1, 3)
                 empty_action(1, 1, 3)
@@ -415,15 +410,15 @@ def tile_clipped_feedback_control_s3_kernel(
                 quantize_u(0, 1, 1)
                 quantize_u(1, 0, 0)
             if s == 5 - 1:
-                for t in range(3):
+                for t in range(2):
                     clip(1, 1, t)
+                quantize_u(1, 0, 1)
             if s == 5:
+                clip(1, 1, 2)
                 clip(1, 1, 3)
                 interleave_u(1, 1, 0)
                 interleave_u(1, 1, 1)
             if s == 9:
                 quantize_u(1, 1, 0)
-            if s == 13:
-                quantize_u(1, 0, 1)
             if s == 15:
                 quantize_u(1, 1, 1)

@@ -128,13 +128,13 @@ def tile_clipped_feedback_control_s3_kernel(
                 nc.scalar.copy(out=xv[j][:, i, cols], in_=xb[j][:, i, cols].bitcast(FP8))
 
         def turn(j, c, tag="turn"):
-            bank = psum.tile([P, 2, P, 2], F32, name=f"xt{j}{c}", tag=tag)
+            bank = psum.tile([P, 2, 2 * P], F32, name=f"xt{j}{c}", tag=tag)
             live["xt", j, c] = bank
             for i in range(2):
                 src = xv[j][:, i, W * c:W * c + W] if c < XP else eb[j][:, E * i:E * i + E]
                 words = src.bitcast(F32)
                 for u in range(2):
-                    nc.tensor.transpose(bank[:, i, :, u], words[:, u::2], ident[:])
+                    nc.tensor.transpose(bank[:, u, P * i:P * i + P], words[:, u::2], ident[:])
 
         def grouped_half(j, c):
             h, half = divmod(j, 2)
@@ -144,23 +144,25 @@ def tile_clipped_feedback_control_s3_kernel(
 
         def scaled(engine, j, c, values):
             engine.tensor_tensor(
-                out=grouped_half(j, c).rearrange("p (s t) -> p s t", t=4), in0=values.rearrange("p (s t) -> p s t", t=4),
-                in1=scale_col[:, c:c + 1, :].to_broadcast([P, 2 * P, 4]), op=ALU.mult,
+                out=grouped_half(j, c).rearrange("p (s u e) -> p s u e", u=2, e=2), in0=values,
+                in1=scale_col[:, c:c + 1, :].rearrange("p o (u e) -> p o u e", u=2).to_broadcast([P, 2 * P, 2, 2]), op=ALU.mult,
             )
 
         def empty_turn(j, c):
-            words = live["xt", j, c][:].rearrange("p i r u -> p (i r u)")
+            bank = live["xt", j, c][:]
             if c == EP:
-                nc.scalar.copy(out=grouped_half(j, c).bitcast(F32), in_=words)
+                nc.scalar.copy(
+                    out=grouped_half(j, c).bitcast(F32).rearrange("p (s u) -> p s u", u=2), in_=bank.rearrange("p u s -> p s u")
+                )
             else:
-                scaled(nc.vector, j, c, words.bitcast(BF16))
+                scaled(nc.vector, j, c, bank.bitcast(BF16).rearrange("p u (s e) -> p s u e", e=2))
 
         def park_turn(j, c):
-            live["xp", j, c] = stage.tile([P, W], F32, name=f"xp{j}{c}", tag="xp", bufs=2)
-            nc.scalar.copy(out=live["xp", j, c][:], in_=live["xt", j, c][:].rearrange("p i r u -> p (i r u)"))
+            live["xp", j, c] = stage.tile([P, 2 * P, 2], F32, name=f"xp{j}{c}", tag="xp", bufs=2)
+            nc.scalar.copy(out=live["xp", j, c][:], in_=live["xt", j, c][:].rearrange("p u s -> p s u"))
 
         def scale_parked(j, c):
-            scaled(nc.gpsimd, j, c, live["xp", j, c][:].bitcast(BF16))
+            scaled(nc.gpsimd, j, c, live["xp", j, c][:].bitcast(BF16).rearrange("p s (u e) -> p s u e", u=2))
 
         def quantize_x(h, c):
             nc.vector.quantize_mx(out=xq[h][c][:].bitcast(FP8X4), scales=xs[h][c][:], in_=live["xg", h, c][:])

@@ -18,6 +18,7 @@ FP4X4 = mybir.dt.float4_e2m1fn_x4
 ALU = mybir.AluOpType
 P = 128
 W = 512
+Q = 256
 XP = S // W
 EP = XP
 
@@ -28,8 +29,8 @@ def tile_clipped_feedback_control_s3_kernel(
     nc = tc.nc
     with ExitStack() as ctx:
         keep = ctx.enter_context(tc.tile_pool(name="keep", bufs=1))
-        stage = ctx.enter_context(tc.tile_pool(name="stage", bufs=4))
-        psum = ctx.enter_context(tc.psum_pool(name="psum", bufs=4))
+        stage = ctx.enter_context(tc.tile_pool(name="stage", bufs=1))
+        psum = ctx.enter_context(tc.psum_pool(name="psum", bufs=1))
         ctx.enter_context(tc.manual_schedule())
 
         ident = keep.tile([P, P], F32, name="ident")
@@ -44,12 +45,18 @@ def tile_clipped_feedback_control_s3_kernel(
         lim_bf = [keep.tile([P, 2, 4], BF16, name=f"lim_bf{k}") for k in range(2)]
         xb = [keep.tile([P, 2, S], U8, name=f"xb{j}") for j in range(4)]
         eb = [keep.tile([P, 2 * E], BF16, name=f"eb{j}") for j in range(4)]
-        fr = [[keep.tile([P, 4, W], BF16, name=f"fr{c}{g}") for g in range(2)] for c in range(XP)]
         bw = keep.tile([P, 2, 2 * S], U8, name="bw", align_bytes=256)
         dr = [keep.tile([P, 2, S], BF16, name=f"dr{j}") for j in range(4)]
+        lw = keep.tile([P, 2, 4, 256], U8, name="lw", align_bytes=256)
+        ls = keep.tile([P, 2, 4, P], U8, name="ls", align_bytes=256)
+        columns_of = {"f": XP * A, "x": (XP + 1) * M, "u": 2 * M}
+        codes = {kind: keep.tile([P, n], U32, name=f"{kind}_codes", align_bytes=256) for kind, n in columns_of.items()}
+        planes = {kind: keep.tile([P, n], U8, name=f"{kind}_plane", align_bytes=256) for kind, n in columns_of.items()}
+        taken = {"f": [], "x": [], "u": []}
+        live = {}
 
         def pair_rows(t, j):
-            return t[256 * j:256 * j + 256, :].rearrange("(p i) k -> p i k", i=2)
+            return t[Q * j:Q * j + Q, :].rearrange("(p i) k -> p i k", i=2)
 
         def load_x(j):
             nc.sync.dma_start(out=xb[j][:], in_=pair_rows(x_bytes, j))
@@ -57,58 +64,40 @@ def tile_clipped_feedback_control_s3_kernel(
         def load_e(j):
             nc.sync.dma_start(out=eb[j][:], in_=pair_rows(e, j).rearrange("p i k -> p (i k)"))
 
-        def load_f(c, g):
-            nc.sync.dma_start(
-                out=fr[c][g][:], in_=F[W * c:W * c + W, W * g:W * g + W].rearrange("(p j) a -> p j a", j=4)
-            )
+        def load_f(c, first, last):
+            tile = keep.tile([P, 4, W * (last - first)], BF16, name=f"fr{c}{first}")
+            nc.sync.dma_start(out=tile[:], in_=F[W * c:W * c + W, W * first:W * last].rearrange("(p j) a -> p j a", j=4))
+            for g in range(first, last):
+                live["fr", c, g] = tile[:, :, W * (g - first):W * (g - first) + W]
 
-        load_x(0)
-        nc.sync.dma_start(out=scale_col[:], in_=x_scale.rearrange("o (c p j) -> p (o c) j", p=P, j=4))
-        load_x(1)
-        for q in range(4):
-            nc.sync.dma_start(
-                out=l_plane[32 * q:32 * q + 4, :].bitcast(I32), in_=L_scales[0, 4 * q:4 * q + 4, :].bitcast(I32)
-            )
-        load_f(0, 0)
-        nc.sync.dma_start(out=l_raw[:], in_=L_words[0])
-        load_e(0)
-        load_e(1)
-        load_f(1, 0)
-        load_f(2, 0)
-        load_x(2)
-        load_e(2)
-        load_e(3)
-        load_x(3)
-        load_f(0, 1)
-        nc.sync.dma_start(out=lim_bf[0][:], in_=hi.rearrange("(g p t) -> p g t", p=P, t=4))
-        nc.sync.dma_start(out=lim_bf[1][:], in_=lo.rearrange("(g p t) -> p g t", p=P, t=4))
-        load_f(2, 1)
-        load_f(1, 1)
-        nc.sync.dma_start(out=bw[:], in_=B_words.rearrange("g p n -> p g n"))
-        for q in range(4):
-            nc.sync.dma_start(
-                out=b_plane[32 * q:32 * q + 4, :, :].bitcast(I32),
-                in_=B_scales[:, 4 * q:4 * q + 4, :].rearrange("g q n -> q g n").bitcast(I32),
-            )
-        for j in range(4):
+        def load_scale():
+            nc.sync.dma_start(out=scale_col[:], in_=x_scale.rearrange("o (c p j) -> p (o c) j", p=P, j=4))
+
+        def load_l_scales():
+            for q in range(4):
+                nc.sync.dma_start(
+                    out=l_plane[32 * q:32 * q + 4, :].bitcast(I32), in_=L_scales[0, 4 * q:4 * q + 4, :].bitcast(I32)
+                )
+
+        def load_l_words():
+            nc.sync.dma_start(out=l_raw[:], in_=L_words[0])
+
+        def load_limits():
+            nc.sync.dma_start(out=lim_bf[0][:], in_=hi.rearrange("(g p t) -> p g t", p=P, t=4))
+            nc.sync.dma_start(out=lim_bf[1][:], in_=lo.rearrange("(g p t) -> p g t", p=P, t=4))
+
+        def load_b_words():
+            nc.sync.dma_start(out=bw[:], in_=B_words.rearrange("g p n -> p g n"))
+
+        def load_b_scales():
+            for q in range(4):
+                nc.sync.dma_start(
+                    out=b_plane[32 * q:32 * q + 4, :, :].bitcast(I32),
+                    in_=B_scales[:, 4 * q:4 * q + 4, :].rearrange("g q n -> q g n").bitcast(I32),
+                )
+
+        def load_drift(j):
             nc.sync.dma_start(out=dr[j][:], in_=pair_rows(drift, j))
-
-        lw = keep.tile([P, 2, 4, 256], U8, name="lw", align_bytes=256)
-        ls = keep.tile([P, 2, 4, P], U8, name="ls", align_bytes=256)
-        fq = [[keep.tile([P, W], U32, name=f"fq{c}{g}", align_bytes=256) for g in range(2)] for c in range(XP)]
-        fs = [[keep.tile([P, W], U8, name=f"fs{c}{g}", align_bytes=256) for g in range(2)] for c in range(XP)]
-        xq = [[keep.tile([P, W], U32, name=f"xq{h}{c}", align_bytes=256) for c in range(XP + 1)] for h in range(2)]
-        xs = [[keep.tile([P, W], U8, name=f"xs{h}{c}", align_bytes=256) for c in range(XP + 1)] for h in range(2)]
-        uq = [[keep.tile([P, W], U32, name=f"uq{h}{g}", align_bytes=256) for g in range(2)] for h in range(2)]
-        us = [[keep.tile([P, W], U8, name=f"us{h}{g}", align_bytes=256) for g in range(2)] for h in range(2)]
-        xv = [stage.tile([P, 2, S], BF16, name=f"xv{j}", tag="xv", bufs=2) for j in range(4)]
-        live = {}
-
-        follows = {"fg20": "fg00", "fg01": "fg00", "xg10": "xg02", "xg12": "xg02", "xg11": "xg03", "fg11": "xg03",
-                   "xg13": "xg00", "fg21": "xg01"}
-
-        def grouped(name):
-            return stage.tile([P, 4 * W], BF16, name=name, tag=follows.get(name, name), bufs=1, align_bytes=256)
 
         def permute_l_words(g):
             nc.vector.tensor_copy(
@@ -122,305 +111,407 @@ def tile_clipped_feedback_control_s3_kernel(
                 in_=l_plane[:, W * g:W * g + W].rearrange("p (m t) -> p m t", t=4),
             )
 
-        def widen_x(j, first=0, last=XP):
+        def widen_x(j, first, last):
+            if ("xv", j) not in live:
+                live["xv", j] = stage.tile([P, 2, S], BF16, name=f"xv{j}", tag=f"xv{j % 2}")
             for i in range(2):
                 cols = slice(W * first, W * last)
-                nc.scalar.copy(out=xv[j][:, i, cols], in_=xb[j][:, i, cols].bitcast(FP8))
+                nc.scalar.copy(out=live["xv", j][:, i, cols], in_=xb[j][:, i, cols].bitcast(FP8))
 
-        def turn(j, c, tag="turn"):
-            bank = psum.tile([P, 2, 2 * P], F32, name=f"xt{j}{c}", tag=tag)
-            live["xt", j, c] = bank
+        def turn(j, c, bank):
+            tile = psum.tile([P, 2, Q], F32, name=f"xt{j}{c}", tag=f"bank{bank}")
+            live["xt", j, c] = tile
             for i in range(2):
-                src = xv[j][:, i, W * c:W * c + W] if c < XP else eb[j][:, E * i:E * i + E]
+                src = live["xv", j][:, i, W * c:W * c + W] if c < XP else eb[j][:, E * i:E * i + E]
                 words = src.bitcast(F32)
                 for u in range(2):
-                    nc.tensor.transpose(bank[:, u, P * i:P * i + P], words[:, u::2], ident[:])
+                    nc.tensor.transpose(tile[:, u, P * i:P * i + P], words[:, u::2], ident[:])
 
-        def grouped_half(j, c):
-            h, half = divmod(j, 2)
-            if ("xg", h, c) not in live:
-                live["xg", h, c] = grouped(f"xg{h}{c}")
-            return live["xg", h, c][:, 2 * W * half:2 * W * half + 2 * W]
+        def operand(kind, key, buffer, columns):
+            live[kind + "g", key] = stage.tile([P, 4 * columns], BF16, name=f"{kind}g{key}", tag=buffer, align_bytes=256)
+            start = columns * len(taken[kind])
+            taken[kind].append(key)
+            live[kind + "q", key] = codes[kind][:, start:start + columns]
+            live[kind + "s", key] = planes[kind][:, start:start + columns]
 
-        def scaled(engine, j, c, values):
+        def x_place(j, c):
+            return (f"{group[j]}{c}", Q * (j % 2)) if group[j] in ("a", "b") else (f"{j}{c // 2}", Q * (c % 2))
+
+        def x_grouped(j, c, buffer):
+            key, first = x_place(j, c)
+            if ("xg", key) not in live:
+                operand("x", key, buffer, W)
+            return live["xg", key][:, 4 * first:4 * first + 4 * Q]
+
+        def scaled(engine, j, c, values, buffer):
             engine.tensor_tensor(
-                out=grouped_half(j, c).rearrange("p (s u e) -> p s u e", u=2, e=2), in0=values,
-                in1=scale_col[:, c:c + 1, :].rearrange("p o (u e) -> p o u e", u=2).to_broadcast([P, 2 * P, 2, 2]), op=ALU.mult,
+                out=x_grouped(j, c, buffer).rearrange("p (s u e) -> p s u e", u=2, e=2), in0=values,
+                in1=scale_col[:, c:c + 1, :].rearrange("p o (u e) -> p o u e", u=2).to_broadcast([P, Q, 2, 2]), op=ALU.mult,
             )
 
-        def empty_turn(j, c):
-            bank = live["xt", j, c][:]
-            if c == EP:
-                nc.scalar.copy(
-                    out=grouped_half(j, c).bitcast(F32).rearrange("p (s u) -> p s u", u=2), in_=bank.rearrange("p u s -> p s u")
-                )
-            else:
-                scaled(nc.vector, j, c, bank.bitcast(BF16).rearrange("p u (s e) -> p s u e", e=2))
+        def empty_x(j, c, buffer=None):
+            scaled(nc.vector, j, c, live["xt", j, c][:].bitcast(BF16).rearrange("p u (s e) -> p s u e", e=2), buffer)
 
-        def park_turn(j, c):
-            live["xp", j, c] = stage.tile([P, 2 * P, 2], F32, name=f"xp{j}{c}", tag="xp", bufs=2)
+        def empty_e(j, buffer=None):
+            nc.scalar.copy(
+                out=x_grouped(j, EP, buffer).bitcast(F32).rearrange("p (s u) -> p s u", u=2), in_=live["xt", j, EP][:].rearrange("p u s -> p s u")
+            )
+
+        def park_x(j, c, buffer):
+            live["xp", j, c] = stage.tile([P, Q, 2], F32, name=f"xp{j}{c}", tag=buffer)
             nc.scalar.copy(out=live["xp", j, c][:], in_=live["xt", j, c][:].rearrange("p u s -> p s u"))
 
-        def scale_parked(j, c):
-            scaled(nc.gpsimd, j, c, live["xp", j, c][:].bitcast(BF16).rearrange("p s (u e) -> p s u e", u=2))
+        def scale_parked(j, c, buffer=None):
+            scaled(nc.gpsimd, j, c, live["xp", j, c][:].bitcast(BF16).rearrange("p s (u e) -> p s u e", u=2), buffer)
 
-        def quantize_x(h, c):
-            nc.vector.quantize_mx(out=xq[h][c][:].bitcast(FP8X4), scales=xs[h][c][:], in_=live["xg", h, c][:])
-
-        def interleave_f(c, g, first=0, last=128, engine=nc.scalar):
-            if ("fg", c, g) not in live:
-                live["fg", c, g] = grouped(f"fg{c}{g}")
+        def interleave(engine, dst, src):
             if engine is nc.gpsimd:
-                src = fr[c][g][:].rearrange("p j (m t) -> p m t j", t=4)[:, first:last]
-                dst = live["fg", c, g][:].rearrange("p (t m j) -> p m t j", t=4, j=4)[:, first:last]
+                nc.gpsimd.tensor_scalar(
+                    out=dst.rearrange("p (s t) -> p s t", t=4), in0=src.rearrange("p t s -> p s t"),
+                    scalar1=1.0, scalar2=0.0, op0=ALU.mult, op1=ALU.add,
+                )
+                return
+            src = src.rearrange("p t (c i) -> p c t i", i=4)
+            dst = dst.rearrange("p (c i t) -> p c t i", i=4, t=4)
+            if engine is nc.vector:
+                nc.vector.tensor_copy(out=dst, in_=src)
+            else:
+                nc.scalar.copy(out=dst, in_=src)
+
+        def quantize(kind, key):
+            nc.vector.quantize_mx(out=live[kind + "q", key].bitcast(FP8X4), scales=live[kind + "s", key], in_=live[kind + "g", key][:])
+
+        def interleave_f(engine, c, g, first, last, buffer=None):
+            if ("fg", f"{c}{g}") not in live:
+                operand("f", f"{c}{g}", buffer, W)
+            raw, grouped = live["fr", c, g], live["fg", f"{c}{g}"][:]
+            if engine is nc.gpsimd:
+                src = raw.rearrange("p j (m t) -> p t m j", t=4)[:, :, first:last]
+                dst = grouped.rearrange("p (t m j) -> p t m j", t=4, j=4)[:, :, first:last]
                 nc.gpsimd.tensor_scalar(out=dst, in0=src, scalar1=1.0, scalar2=0.0, op0=ALU.mult, op1=ALU.add)
                 return
             m = slice(first // 2, last // 2)
-            src = fr[c][g][:].rearrange("p j (m r t) -> p m t j r", r=2, t=4)[:, m]
-            dst = live["fg", c, g][:].rearrange("p (t m r j) -> p m t j r", t=4, r=2, j=4)[:, m]
+            src = raw.rearrange("p j (m r t) -> p m t j r", r=2, t=4)[:, m]
+            dst = grouped.rearrange("p (t m r j) -> p m t j r", t=4, r=2, j=4)[:, m]
             if engine is nc.vector:
                 nc.vector.tensor_copy(out=dst, in_=src)
             else:
                 nc.scalar.copy(out=dst, in_=src)
 
         def quantize_f(c, g):
-            nc.vector.quantize_mx(out=fq[c][g][:].bitcast(FP8X4), scales=fs[c][g][:], in_=live["fg", c, g][:])
+            quantize("f", f"{c}{g}")
 
-        def action_pass(h, g, t, c, order):
-            if c == order[0]:
-                live["acc", h, g, t] = psum.tile([P, W], F32, name=f"acc{h}{g}{t}", tag="turn" if (h, g) == (0, 1) else "acc")
+        def action_pass(acc, key, first, width, g, t, c, order):
             cols = slice(P * t, P * t + P)
             if c < XP:
-                w, ws = fq[c][g][:, cols].bitcast(FP8X4), fs[c][g][:, cols]
+                w, ws = live["fq", f"{c}{g}"][:, cols].bitcast(FP8X4), live["fs", f"{c}{g}"][:, cols]
             else:
                 w, ws = lw[:, g, t, :].bitcast(FP4X4), ls[:, g, t, :]
             nc.tensor.matmul_mx(
-                out=live["acc", h, g, t][:], lhsT=w, lhsT_scale=ws,
-                rhs=xq[h][c][:].bitcast(FP8X4), rhs_scale=xs[h][c][:],
+                out=acc, lhsT=w, lhsT_scale=ws,
+                rhs=live["xq", key][:, first:first + width].bitcast(FP8X4), rhs_scale=live["xs", key][:, first:first + width],
                 start=(c == order[0]), stop=(c == order[-1]),
             )
 
-        def action(h, g, t):
-            for c in range(XP + 1):
-                action_pass(h, g, t, c, range(XP + 1))
+        def half_pass(h, g, c, order, banks, tiles=range(4)):
+            for t in tiles:
+                if c == order[0]:
+                    live["acc", h, g, t] = psum.tile([P, W], F32, name=f"acc{h}{g}{t}", tag=f"bank{banks[t]}")
+                action_pass(live["acc", h, g, t][:], f"{h}{c}", 0, W, g, t, c, order)
 
-        def empty_action(h, g, t, on_vector=False, cols=slice(0, W)):
-            if ("up", h, g) not in live:
-                live["up", h, g] = stage.tile([P, 4, W], BF16, name=f"up{h}{g}", tag="up", bufs=4)
-            u = live["up", h, g][:, t, cols]
-            if on_vector:
-                nc.vector.tensor_scalar(
-                    out=u, in0=live["acc", h, g, t][:, cols], scalar1=lim_bf[0][:, g, t:t + 1], scalar2=lim_bf[1][:, g, t:t + 1],
-                    op0=ALU.min, op1=ALU.max,
-                )
-            else:
-                nc.scalar.copy(out=u, in_=live["acc", h, g, t][:, cols])
+        def quarter_bank(j, g, k, bank):
+            acc = psum.tile([P, 2, Q], F32, name=f"acc{j}{g}{k}", tag=f"bank{bank}")
+            live["acc", j, g, k] = acc
+            for r in range(2):
+                for c in range(XP + 1):
+                    key, first = x_place(j, c)
+                    action_pass(acc[:, r, :], key, first, Q, g, 2 * k + r, c, range(XP + 1))
 
-        def clip(h, g, t, cols=slice(0, W)):
-            u = live["up", h, g][:, t, cols]
+        def planes_u(key, g, width):
+            if ("up", key, g) not in live:
+                live["up", key, g] = stage.tile([P, 4, width], BF16, name=f"up{key}{g}", tag=planes_in.get((key, g), f"up{key}{g}"))
+            return live["up", key, g]
+
+        def clipped(dst, src, g, t):
             nc.vector.tensor_scalar(
-                out=u, in0=u, scalar1=lim_bf[0][:, g, t:t + 1], scalar2=lim_bf[1][:, g, t:t + 1], op0=ALU.min, op1=ALU.max
+                out=dst, in0=src, scalar1=lim_bf[0][:, g, t:t + 1], scalar2=lim_bf[1][:, g, t:t + 1], op0=ALU.min, op1=ALU.max
             )
 
-        def interleave_u(h, g, k, on_vector=False):
-            ug = stage.tile([P, 2 * W], BF16, name=f"ug{h}{g}{k}", tag="ug", bufs=4, align_bytes=256)
-            live["ug", h, g, k] = ug
-            src = live["up", h, g][:, :, 256 * k:256 * k + 256].rearrange("p t (c i) -> p c t i", i=4)
-            dst = ug[:].rearrange("p (c i t) -> p c t i", i=4, t=4)
+        def empty_half(h, g, t, on_vector=False, cols=slice(0, W)):
+            dst, src = planes_u(h, g, W)[:, t, cols], live["acc", h, g, t][:, cols]
             if on_vector:
-                nc.vector.tensor_copy(out=dst, in_=src)
+                clipped(dst, src, g, t)
             else:
                 nc.scalar.copy(out=dst, in_=src)
 
-        def quantize_u(h, g, k):
-            m = slice(256 * k, 256 * k + 256)
-            nc.vector.quantize_mx(out=uq[h][g][:, m].bitcast(FP8X4), scales=us[h][g][:, m], in_=live["ug", h, g, k][:])
+        def empty_quarter(j, g, k, on_vector=False):
+            up, acc = planes_u(j, g, Q), live["acc", j, g, k]
+            if on_vector:
+                for r in range(2):
+                    clipped(up[:, 2 * k + r, :], acc[:, r, :], g, 2 * k + r)
+            else:
+                nc.scalar.copy(out=up[:, 2 * k:2 * k + 2, :], in_=acc[:])
 
-        def rate(i, n, tag):
-            h, cols = i // 4, slice(P * (i % 4), P * (i % 4) + P)
-            acc = psum.tile([P, W], F32, name=f"y{i}{n}", tag=tag)
-            live["y", i, n] = acc
+        def clip(key, g, tiles=range(4), cols=slice(None)):
+            for t in tiles:
+                u = live["up", key, g][:, t, cols]
+                clipped(u, u, g, t)
+
+        def interleave_u(engine, j, g, buffer):
+            operand("u", f"{j}{g}", buffer, Q)
+            src = live["up", j, g][:] if ("up", j, g) in live else live["up", group[j], g][:, :, Q * (j % 2):Q * (j % 2) + Q]
+            interleave(engine, live["ug", f"{j}{g}"][:], src)
+
+        def rate(j, n, bank):
+            i, cols = divmod(n, XP)
+            acc = psum.tile([P, W], F32, name=f"y{j}{n}", tag=f"bank{bank}")
+            live["y", j, n] = acc
             for g in range(2):
                 nc.tensor.matmul_mx(
                     out=acc[:],
-                    lhsT=uq[h][g][:, cols].bitcast(FP8X4), lhsT_scale=us[h][g][:, cols],
-                    rhs=bw[:, g, 2 * W * n:2 * W * n + 2 * W].bitcast(FP4X4),
-                    rhs_scale=b_plane[:, g, W * n:W * n + W],
+                    lhsT=live["uq", f"{j}{g}"][:, P * i:P * i + P].bitcast(FP8X4), lhsT_scale=live["us", f"{j}{g}"][:, P * i:P * i + P],
+                    rhs=bw[:, g, 2 * W * cols:2 * W * cols + 2 * W].bitcast(FP4X4),
+                    rhs_scale=b_plane[:, g, W * cols:W * cols + W],
                     start=(g == 0), stop=(g == 1),
                 )
 
-        def add_drift(i, n):
-            j, chunk = i // 2, XP * (i % 2) + n
-            if chunk == 0:
-                live["ot", j] = stage.tile([P, 2 * S], F32, name=f"ot{j}", tag="ot", bufs=3)
-            cols = slice(W * chunk, W * chunk + W)
-            dst, given = live["ot", j][:, cols], dr[j][:].rearrange("p i k -> p (i k)")[:, cols]
-            if XP * i + n in by_gpsimd:
-                nc.scalar.copy(out=dst, in_=live["y", i, n][:])
-                nc.gpsimd.tensor_tensor(out=dst, in0=dst, in1=given, op=ALU.add)
-            else:
-                nc.vector.tensor_tensor(out=dst, in0=live["y", i, n][:], in1=given, op=ALU.add)
+        def out_cols(j, n):
+            if ("ot", j) not in live:
+                live["ot", j] = stage.tile([P, 2 * S], F32, name=f"ot{j}", tag=f"ot{j % OT}")
+            cols = slice(W * n, W * n + W)
+            return live["ot", j][:, cols], dr[j][:].rearrange("p i k -> p (i k)")[:, cols]
 
-        def store(first, count, queue=nc.sync):
-            j, chunk = divmod(first, 2 * XP)
-            cols = slice(W * chunk, W * (chunk + count))
+        def add_drift(j, n):
+            dst, given = out_cols(j, n)
+            nc.vector.tensor_tensor(out=dst, in0=live["y", j, n][:], in1=given, op=ALU.add)
+
+        def store(j, first, count, queue=nc.sync):
+            cols = slice(W * first, W * (first + count))
             rows = pair_rows(out, j).rearrange("p i k -> p (i k)")
             queue.dma_start(out=rows[:, cols], in_=live["ot", j][:, cols])
 
-        def block_pass(h, g, c, order):
-            for t in range(4):
-                action_pass(h, g, t, c, order)
-
-        def turn_pass(h, c):
-            for j in (2 * h, 2 * h + 1):
-                turn(j, c)
-                empty_turn(j, c)
-
-        def empty_pass(h, c):
-            for j in (2 * h, 2 * h + 1):
-                empty_turn(j, c)
-
-        def pair_pass(h, g, k, c, order):
-            for t in (2 * k, 2 * k + 1):
-                action_pass(h, g, t, c, order)
-
+        act, vec, pool = nc.scalar, nc.vector, nc.gpsimd
+        OT = 3
+        group = ("a", "a", "b", "b")
+        planes_in = {}
         order = (0, EP, 1, 2)
-        for c in (0, 2, 1):
-            widen_x(0, c, c + 1)
-            turn(0, c)
-        widen_x(1, 0, 1)
-        turn(1, 0)
-        park_turn(0, 2)
-        scale_parked(0, 2)
-        widen_x(1, 1, 3)
-        empty_turn(0, 0)
-        turn(1, 1)
-        empty_turn(0, 1)
-        turn(1, 2)
-        empty_turn(1, 0)
-        empty_turn(1, 1)
-        interleave_f(0, 0)
-        turn(0, EP, "acc")
-        turn(1, EP, "acc")
-        empty_pass(0, EP)
-        quantize_x(0, 0)
-        quantize_f(0, 0)
-        block_pass(0, 0, 0, order)
-        permute_l_words(0)
-        quantize_x(0, EP)
-        permute_l_scales(0)
-        interleave_f(1, 0)
-        block_pass(0, 0, EP, order)
-        empty_turn(1, 2)
-        quantize_x(0, 1)
-        turn(2, EP)
-        turn(3, EP)
-        quantize_f(1, 0)
-        interleave_f(2, 0, 0, 64)
-        widen_x(2, 0, 1)
-        widen_x(3, 0, 1)
-        block_pass(0, 0, 1, order)
-        interleave_f(2, 0, 64, 128, nc.vector)
-        quantize_x(0, 2)
-        turn(2, 0)
-        turn(3, 0)
-        empty_pass(1, EP)
-        permute_l_words(1)
-        permute_l_scales(1)
-        quantize_f(2, 0)
-        widen_x(3, 1, 3)
-        widen_x(2, 1, 3)
-        pair_pass(0, 0, 0, 2, order)
-        interleave_f(0, 1, 80, 128, nc.gpsimd)
-        empty_pass(1, 0)
-        turn(3, 2)
-        pair_pass(0, 0, 1, 2, order)
-        turn(2, 1)
-        quantize_x(1, EP)
-        for t in range(2):
-            empty_action(0, 0, t)
-        park_turn(3, 2)
-        for t in range(2, 4):
-            empty_action(0, 0, t)
-        quantize_x(1, 0)
-        scale_parked(3, 2)
-        order = (EP, 0, 1, 2)
-        turn(3, 1)
-        pair_pass(1, 0, 0, EP, order)
-        turn(2, 2)
-        pair_pass(1, 0, 1, EP, order)
-        interleave_f(0, 1, 0, 80)
-        empty_pass(1, 1)
-        empty_turn(2, 2)
-        block_pass(1, 0, 0, order)
-        interleave_f(2, 1)
-        quantize_x(1, 1)
-        quantize_f(0, 1)
+        next_order = (EP, 0, 1, 2)
         late = (EP, 0, 2, 1)
-        block_pass(0, 1, EP, late)
-        block_pass(1, 0, 1, order)
-        block_pass(0, 1, 0, late)
-        interleave_f(1, 1)
-        quantize_x(1, 2)
+        first, second = slice(0, Q), slice(Q, W)
+        load_x(0)
+        load_scale()
+        load_x(1)
+        load_l_scales()
+        load_f(0, 0, 1)
+        load_l_words()
+        load_e(0)
+        load_e(1)
+        load_f(1, 0, 1)
+        load_f(2, 0, 1)
+        load_x(2)
+        load_e(2)
+        load_e(3)
+        load_x(3)
+        load_f(0, 1, 2)
+        load_limits()
+        load_f(2, 1, 2)
+        load_f(1, 1, 2)
+        load_b_words()
+        load_b_scales()
+        load_drift(0)
+        load_drift(1)
+        load_drift(2)
+        load_drift(3)
+        widen_x(0, 0, 1)
+        turn(0, 0, 0)
+        empty_x(0, 0, "xa0")
+        widen_x(0, 2, 3)
+        turn(0, 2, 1)
+        widen_x(0, 1, 2)
+        turn(0, 1, 2)
+        empty_x(0, 1, "xa1")
+        widen_x(1, 0, 1)
+        turn(1, 0, 3)
+        empty_x(1, 0)
+        park_x(0, 2, "xp0")
+        scale_parked(0, 2, "xa2")
+        widen_x(1, 1, 3)
+        turn(1, 1, 0)
+        empty_x(1, 1)
+        interleave_f(act, 0, 0, 0, 128, "f0")
+        turn(1, 2, 1)
+        quantize("x", "a0")
+        turn(0, EP, 4)
+        quantize_f(0, 0)
+        empty_e(0, "xa3")
+        turn(1, EP, 5)
+        permute_l_words(0)
+        empty_e(1)
+        half_pass("a", 0, 0, order, (6, 7, 4, 5))
+        quantize("x", "a3")
+        interleave_f(act, 1, 0, 0, 128, "f1")
+        interleave_f(pool, 2, 0, 0, 36, "xa3")
+        permute_l_scales(0)
+        widen_x(2, 0, 1)
+        half_pass("a", 0, EP, order, None)
+        empty_x(1, 2)
+        interleave_f(act, 2, 0, 36, 128)
+        turn(2, EP, 2)
+        quantize("x", "a1")
+        widen_x(3, 0, 1)
+        turn(3, EP, 3)
+        quantize_f(1, 0)
+        empty_e(2, "xa0")
+        half_pass("a", 0, 1, order, None, (0, 1))
+        quantize("x", "a2")
+        empty_e(3)
+        turn(2, 0, 0)
+        permute_l_words(1)
+        widen_x(3, 1, 3)
+        turn(3, 0, 1)
+        permute_l_scales(1)
+        widen_x(2, 1, 3)
+        half_pass("a", 0, 1, order, None, (2, 3))
+        quantize_f(2, 0)
+        interleave_f(pool, 0, 1, 56, 128, "xa3")
+        half_pass("a", 0, 2, order, None, (0, 1))
+        empty_x(2, 0, "f1")
+        empty_half("a", 0, 0)
+        turn(3, 2, 2)
+        empty_x(3, 0)
+        empty_half("a", 0, 1)
+        half_pass("a", 0, 2, order, None, (2, 3))
+        quantize("x", "b3")
+        park_x(3, 2, "xp0")
+        turn(2, 1, 3)
+        quantize("x", "b0")
+        empty_half("a", 0, 2)
+        scale_parked(3, 2, "f1")
+        turn(3, 1, 0)
+        empty_x(2, 1, "xa2")
+        empty_half("a", 0, 3)
+        half_pass("b", 0, EP, next_order, (6, 7, 4, 5), (0, 1))
+        empty_x(3, 1)
+        interleave_f(act, 0, 1, 0, 56)
+        turn(2, 2, 1)
+        empty_x(2, 2)
+        interleave_f(act, 2, 1, 0, 128, "xa1")
+        half_pass("b", 0, EP, next_order, (6, 7, 4, 5), (2, 3))
+        quantize("x", "b1")
+        interleave_f(act, 1, 1, 0, 128, "f0")
+        half_pass("b", 0, 0, next_order, None)
+        quantize_f(0, 1)
+        half_pass("a", 1, EP, late, (2, 3, 0, 1))
+        quantize("x", "b2")
+        half_pass("b", 0, 1, next_order, None)
+        clip("a", 0)
+        interleave_u(act, 0, 0, "u0")
+        half_pass("a", 1, 0, late, None)
         quantize_f(2, 1)
-        for t in range(4):
-            clip(0, 0, t)
+        half_pass("b", 0, 2, next_order, None)
         quantize_f(1, 1)
-        block_pass(1, 0, 2, order)
-        for c in late[2:]:
-            block_pass(0, 1, c, late)
-        for t in range(4):
-            empty_action(1, 0, t, t >= 2)
-        interleave_u(0, 0, 0)
-        halves = (slice(0, W // 2), slice(W // 2, W))
-        for t in range(4):
-            empty_action(0, 1, t, True, halves[0])
-        interleave_u(0, 0, 1)
-        for t in range(4):
-            empty_action(0, 1, t, False, halves[1])
-        for t in range(2):
-            action(1, 1, t)
-        quantize_u(0, 0, 0)
-        interleave_u(0, 1, 0, True)
-        for t in range(2):
-            clip(1, 0, t)
-        quantize_u(0, 1, 0)
-        for t in range(4):
-            clip(0, 1, t, halves[1])
-        quantize_u(0, 0, 1)
-        interleave_u(1, 0, 0)
-        interleave_u(0, 1, 1)
-        for t in range(2):
-            empty_action(1, 1, t)
-        by_gpsimd = ()
-        steps = [(i, n) for i in range(8) for n in range(3)]
-        for s, (i, n) in enumerate(steps):
-            if s == 3:
-                action(1, 1, 2)
-                interleave_u(1, 0, 1)
-                empty_action(1, 1, 2)
-            if s == 5:
-                action(1, 1, 3)
-                empty_action(1, 1, 3)
-            rate(i, n, "turn" if s % 2 == 0 or s < 8 else "acc")
-            add_drift(i, n)
-            if s < 6 or s >= 22:
-                store(s, 1, nc.scalar if s == 22 else nc.sync)
-            elif s % 2 == 1:
-                store(s - 1, 2, nc.scalar if s >= 10 and s % 4 == 3 else nc.sync)
-            if s == 2:
-                quantize_u(0, 1, 1)
-                quantize_u(1, 0, 0)
-            if s == 5 - 1:
-                for t in range(2):
-                    clip(1, 1, t)
-                quantize_u(1, 0, 1)
-            if s == 5:
-                clip(1, 1, 2)
-                clip(1, 1, 3)
-                interleave_u(1, 1, 0)
-                interleave_u(1, 1, 1)
-            if s == 9:
-                quantize_u(1, 1, 0)
-            if s == 15:
-                quantize_u(1, 1, 1)
+        empty_half("b", 0, 0)
+        half_pass("a", 1, 2, late, None)
+        quantize("u", "00")
+        empty_half("b", 0, 1)
+        half_pass("a", 1, 1, late, None)
+        clip("b", 0, (0, 1))
+        empty_half("b", 0, 2)
+        quarter_bank(2, 1, 0, 6)
+        empty_half("a", 1, 0, True, first)
+        empty_half("b", 0, 3)
+        quarter_bank(2, 1, 1, 7)
+        empty_half("a", 1, 1, True, first)
+        empty_half("a", 1, 0, False, second)
+        empty_half("a", 1, 2, True, first)
+        empty_half("a", 1, 1, False, second)
+        empty_half("a", 1, 3, True, first)
+        empty_half("a", 1, 2, False, second)
+        clip("b", 0, (2, 3))
+        empty_half("a", 1, 3, False, second)
+        interleave_u(vec, 0, 1, "u2")
+        interleave_u(act, 1, 0, "u1")
+        clip("a", 1, (0, 1, 2, 3), second)
+        empty_quarter(2, 1, 0)
+        quantize("u", "01")
+        interleave_u(act, 1, 1, "u0")
+        rate(0, 0, 4)
+        quantize("u", "10")
+        empty_quarter(2, 1, 1)
+        rate(0, 1, 5)
+        add_drift(0, 0)
+        interleave_u(act, 2, 0, "u3")
+        rate(0, 2, 2)
+        add_drift(0, 1)
+        interleave_u(act, 3, 0, "u1")
+        store(0, 0, 2)
+        rate(0, 3, 3)
+        add_drift(0, 2)
+        rate(0, 4, 0)
+        quantize("u", "11")
+        rate(0, 5, 1)
+        add_drift(0, 3)
+        store(0, 2, 2)
+        rate(1, 0, 6)
+        add_drift(0, 4)
+        rate(1, 1, 7)
+        clip(2, 1)
+        interleave_u(act, 2, 1, "u2")
+        rate(1, 2, 4)
+        add_drift(0, 5)
+        store(0, 4, 2)
+        rate(1, 3, 5)
+        add_drift(1, 0)
+        quarter_bank(3, 1, 0, 2)
+        add_drift(1, 1)
+        empty_quarter(3, 1, 0)
+        store(1, 0, 2)
+        quarter_bank(3, 1, 1, 3)
+        add_drift(1, 2)
+        empty_quarter(3, 1, 1)
+        rate(1, 4, 0)
+        add_drift(1, 3)
+        store(1, 2, 2)
+        rate(1, 5, 1)
+        quantize("u", "20")
+        quantize("u", "21")
+        rate(2, 0, 6)
+        quantize("u", "30")
+        rate(2, 1, 7)
+        clip(3, 1, (0, 1))
+        rate(2, 2, 4)
+        add_drift(1, 4)
+        store(1, 4, 1)
+        rate(2, 3, 5)
+        clip(3, 1, (2, 3))
+        interleave_u(act, 3, 1, "u3")
+        rate(2, 4, 2)
+        add_drift(1, 5)
+        store(1, 5, 1)
+        rate(2, 5, 3)
+        add_drift(2, 0)
+        add_drift(2, 1)
+        store(2, 0, 2)
+        add_drift(2, 2)
+        quantize("u", "31")
+        rate(3, 0, 0)
+        add_drift(2, 3)
+        store(2, 2, 2, act)
+        rate(3, 1, 1)
+        add_drift(2, 4)
+        rate(3, 2, 6)
+        add_drift(2, 5)
+        store(2, 4, 2)
+        rate(3, 3, 7)
+        add_drift(3, 0)
+        rate(3, 4, 4)
+        add_drift(3, 1)
+        store(3, 0, 2, act)
+        rate(3, 5, 5)
+        add_drift(3, 2)
+        add_drift(3, 3)
+        store(3, 2, 2)
+        add_drift(3, 4)
+        store(3, 4, 1, act)
+        add_drift(3, 5)
+        store(3, 5, 1)

@@ -73,9 +73,9 @@ def tile_clipped_feedback_control_s3_kernel(
         def load_scale():
             nc.sync.dma_start(out=scale_col[:], in_=x_scale.rearrange("o (c p j) -> p (o c) j", p=P, j=4))
 
-        def load_l_scales():
+        def load_l_scales(queue=nc.sync):
             for q in range(4):
-                nc.sync.dma_start(
+                queue.dma_start(
                     out=l_plane[32 * q:32 * q + 4, :].bitcast(I32), in_=L_scales[0, 4 * q:4 * q + 4, :].bitcast(I32)
                 )
 
@@ -99,16 +99,16 @@ def tile_clipped_feedback_control_s3_kernel(
         def load_drift(j):
             nc.sync.dma_start(out=dr[j][:], in_=pair_rows(drift, j))
 
-        def permute_l_words(g):
+        def permute_l_words(first, last):
             nc.vector.tensor_copy(
-                out=lw[:, g].bitcast(U16).rearrange("p t m -> p m t"),
-                in_=l_raw[:, A * g:A * g + A].bitcast(U16).rearrange("p (m t) -> p m t", t=4),
+                out=lw[:, first:last].bitcast(U16).rearrange("p g t m -> p g m t"),
+                in_=l_raw[:, A * first:A * last].bitcast(U16).rearrange("p (g m t) -> p g m t", m=P, t=4),
             )
 
-        def permute_l_scales(g):
+        def permute_l_scales(first, last):
             nc.vector.tensor_copy(
-                out=ls[:, g].rearrange("p t m -> p m t"),
-                in_=l_plane[:, W * g:W * g + W].rearrange("p (m t) -> p m t", t=4),
+                out=ls[:, first:last].rearrange("p g t m -> p g m t"),
+                in_=l_plane[:, W * first:W * last].rearrange("p (g m t) -> p g m t", m=P, t=4),
             )
 
         def widen_x(j, first, last):
@@ -345,13 +345,13 @@ def tile_clipped_feedback_control_s3_kernel(
         quantize_f(0, 0)
         empty_e(0, "xa3")
         turn(1, EP, 5)
-        permute_l_words(0)
+        permute_l_words(0, 1)
         empty_e(1)
         half_pass("a", 0, 0, order, (6, 7, 4, 5))
         quantize("x", "a3")
         interleave_f(act, 1, 0, 0, 128, "f1")
         interleave_f(pool, 2, 0, 0, 36, "xa3")
-        permute_l_scales(0)
+        permute_l_scales(0, 1)
         widen_x(2, 0, 1)
         half_pass("a", 0, EP, order, None)
         empty_x(1, 2)
@@ -366,10 +366,10 @@ def tile_clipped_feedback_control_s3_kernel(
         quantize("x", "a2")
         empty_e(3)
         turn(2, 0, 0)
-        permute_l_words(1)
+        permute_l_words(1, 2)
         widen_x(3, 1, 3)
         turn(3, 0, 1)
-        permute_l_scales(1)
+        permute_l_scales(1, 2)
         widen_x(2, 1, 3)
         half_pass("a", 0, 1, order, None, (2, 3))
         quantize_f(2, 0)
@@ -398,7 +398,7 @@ def tile_clipped_feedback_control_s3_kernel(
         interleave_f(act, 2, 1, 0, 128, "xa1")
         half_pass("b", 0, EP, next_order, (6, 7, 4, 5), (2, 3))
         quantize("x", "b1")
-        interleave_f(act, 1, 1, 0, 128, "f0")
+        interleave_f(act, 1, 1, 0, 64, "f0")
         half_pass("b", 0, 0, next_order, None)
         quantize_f(0, 1)
         half_pass("a", 1, EP, late, (2, 3, 0, 1))
@@ -409,41 +409,41 @@ def tile_clipped_feedback_control_s3_kernel(
         half_pass("a", 1, 0, late, None)
         quantize_f(2, 1)
         half_pass("b", 0, 2, next_order, None)
-        quantize_f(1, 1)
+        interleave_f(vec, 1, 1, 64, 128)
         empty_half("b", 0, 0)
         half_pass("a", 1, 2, late, None)
-        quantize("u", "00")
+        quantize_f(1, 1)
         empty_half("b", 0, 1)
         half_pass("a", 1, 1, late, None)
-        clip("b", 0, (0, 1))
-        empty_half("b", 0, 2)
-        quarter_bank(2, 1, 0, 6)
-        empty_half("a", 1, 0, True, first)
-        empty_half("b", 0, 3)
-        quarter_bank(2, 1, 1, 7)
-        empty_half("a", 1, 1, True, first)
-        empty_half("a", 1, 0, False, second)
-        empty_half("a", 1, 2, True, first)
-        empty_half("a", 1, 1, False, second)
-        empty_half("a", 1, 3, True, first)
-        empty_half("a", 1, 2, False, second)
-        clip("b", 0, (2, 3))
-        empty_half("a", 1, 3, False, second)
-        interleave_u(vec, 0, 1, "u2")
+        empty_half("b", 0, 2, True)
         interleave_u(act, 1, 0, "u1")
-        clip("a", 1, (0, 1, 2, 3), second)
+        quarter_bank(2, 1, 0, 6)
+        empty_half("b", 0, 3, True)
+        quarter_bank(2, 1, 1, 7)
+        quantize("u", "00")
+        empty_half("a", 1, 0, True, first)
+        empty_half("a", 1, 0, False, second)
+        empty_half("a", 1, 1, True, first)
+        empty_half("a", 1, 1, False, second)
+        empty_half("a", 1, 2, True, first)
+        empty_half("a", 1, 2, False, second)
+        empty_half("a", 1, 3, True, first)
+        empty_half("a", 1, 3, False, second)
+        clip("b", 0, (0, 1))
         empty_quarter(2, 1, 0)
-        quantize("u", "01")
+        interleave_u(vec, 0, 1, "u2")
+        clip("a", 1, (0, 1, 2, 3), second)
         interleave_u(act, 1, 1, "u0")
+        quantize("u", "01")
+        empty_quarter(2, 1, 1)
         rate(0, 0, 4)
         quantize("u", "10")
-        empty_quarter(2, 1, 1)
+        interleave_u(act, 2, 0, "u3")
         rate(0, 1, 5)
         add_drift(0, 0)
-        interleave_u(act, 2, 0, "u3")
+        interleave_u(act, 3, 0, "u1")
         rate(0, 2, 2)
         add_drift(0, 1)
-        interleave_u(act, 3, 0, "u1")
         store(0, 0, 2)
         rate(0, 3, 3)
         add_drift(0, 2)
@@ -490,28 +490,33 @@ def tile_clipped_feedback_control_s3_kernel(
         store(1, 5, 1)
         rate(2, 5, 3)
         add_drift(2, 0)
+        store(2, 0, 1)
         add_drift(2, 1)
-        store(2, 0, 2)
+        store(2, 1, 1, act)
         add_drift(2, 2)
+        store(2, 2, 1)
         quantize("u", "31")
         rate(3, 0, 0)
         add_drift(2, 3)
-        store(2, 2, 2, act)
+        store(2, 3, 1, act)
         rate(3, 1, 1)
         add_drift(2, 4)
+        store(2, 4, 1)
         rate(3, 2, 6)
         add_drift(2, 5)
-        store(2, 4, 2)
+        store(2, 5, 1, act)
         rate(3, 3, 7)
         add_drift(3, 0)
+        store(3, 0, 1)
         rate(3, 4, 4)
         add_drift(3, 1)
-        store(3, 0, 2, act)
+        store(3, 1, 1, act)
         rate(3, 5, 5)
         add_drift(3, 2)
+        store(3, 2, 1)
         add_drift(3, 3)
-        store(3, 2, 2)
+        store(3, 3, 1, act)
         add_drift(3, 4)
-        store(3, 4, 1, act)
+        store(3, 4, 1)
         add_drift(3, 5)
-        store(3, 5, 1)
+        store(3, 5, 1, act)

@@ -300,17 +300,17 @@ def tile_clipped_feedback_control_s3_kernel(
         first, second = slice(0, Q), slice(Q, W)
         load_x(0)
         load_scale()
-        load_x(1)
-        load_l_scales()
-        load_f(0, 0, 1)
         load_l_words()
+        load_x(1)
+        load_f(0, 0, 1)
         load_e(0)
         load_e(1)
-        load_f(1, 0, 1)
-        load_f(2, 0, 1)
-        load_x(2)
         load_e(2)
         load_e(3)
+        load_f(1, 0, 1)
+        load_l_scales()
+        load_f(2, 0, 1)
+        load_x(2)
         load_x(3)
         load_f(0, 1, 2)
         load_limits()
@@ -322,6 +322,7 @@ def tile_clipped_feedback_control_s3_kernel(
         load_drift(1)
         load_drift(2)
         load_drift(3)
+        permute_l_words(0, 2)
         widen_x(0, 0, 1)
         turn(0, 0, 0)
         empty_x(0, 0, "xa0")
@@ -345,78 +346,77 @@ def tile_clipped_feedback_control_s3_kernel(
         quantize_f(0, 0)
         empty_e(0, "xa3")
         turn(1, EP, 5)
-        permute_l_words(0, 1)
         empty_e(1)
-        half_pass("a", 0, 0, order, (6, 7, 4, 5))
+        turn(2, EP, 2)
         quantize("x", "a3")
         interleave_f(act, 1, 0, 0, 128, "f1")
-        interleave_f(pool, 2, 0, 0, 36, "xa3")
+        interleave_f(pool, 2, 0, 0, 24, "xa3")
+        turn(3, EP, 3)
+        quantize("x", "a1")
+        empty_e(2, "xa0")
+        half_pass("a", 0, 0, order, (6, 7, 4, 5))
         permute_l_scales(0, 1)
         widen_x(2, 0, 1)
         half_pass("a", 0, EP, order, None)
         empty_x(1, 2)
-        interleave_f(act, 2, 0, 36, 128)
-        turn(2, EP, 2)
-        quantize("x", "a1")
-        widen_x(3, 0, 1)
-        turn(3, EP, 3)
-        quantize_f(1, 0)
-        empty_e(2, "xa0")
-        half_pass("a", 0, 1, order, None, (0, 1))
-        quantize("x", "a2")
-        empty_e(3)
+        interleave_f(act, 2, 0, 72, 128)
         turn(2, 0, 0)
-        permute_l_words(1, 2)
-        widen_x(3, 1, 3)
-        turn(3, 0, 1)
+        quantize_f(1, 0)
+        widen_x(3, 0, 1)
+        half_pass("a", 0, 1, order, None)
         permute_l_scales(1, 2)
-        widen_x(2, 1, 3)
-        half_pass("a", 0, 1, order, None, (2, 3))
-        quantize_f(2, 0)
-        interleave_f(pool, 0, 1, 56, 128, "xa3")
-        half_pass("a", 0, 2, order, None, (0, 1))
-        empty_x(2, 0, "f1")
-        empty_half("a", 0, 0)
+        widen_x(3, 2, 3)
+        turn(3, 0, 1)
+        interleave_f(vec, 2, 0, 24, 72)
+        empty_e(3)
         turn(3, 2, 2)
-        empty_x(3, 0)
-        empty_half("a", 0, 1)
-        half_pass("a", 0, 2, order, None, (2, 3))
-        quantize("x", "b3")
-        park_x(3, 2, "xp0")
+        quantize("x", "a2")
+        widen_x(2, 1, 2)
+        quantize_f(2, 0)
+        widen_x(3, 1, 2)
+        interleave_f(pool, 0, 1, 52, 128, "xa3")
+        half_pass("a", 0, 2, order, None)
+        empty_x(2, 0, "f1")
+        widen_x(2, 2, 3)
         turn(2, 1, 3)
-        quantize("x", "b0")
-        empty_half("a", 0, 2)
-        scale_parked(3, 2, "f1")
+        empty_x(3, 0)
+        empty_half("a", 0, 0)
         turn(3, 1, 0)
-        empty_x(2, 1, "xa2")
-        empty_half("a", 0, 3)
+        quantize("x", "b3")
+        empty_half("a", 0, 1)
         half_pass("b", 0, EP, next_order, (6, 7, 4, 5), (0, 1))
-        empty_x(3, 1)
-        interleave_f(act, 0, 1, 0, 56)
+        quantize("x", "b0")
+        park_x(3, 2, "xp0")
+        scale_parked(3, 2, "f1")
         turn(2, 2, 1)
-        empty_x(2, 2)
-        interleave_f(act, 2, 1, 0, 128, "xa1")
+        empty_x(2, 1, "xa2")
+        empty_half("a", 0, 2)
+        empty_x(3, 1)
+        empty_half("a", 0, 3)
         half_pass("b", 0, EP, next_order, (6, 7, 4, 5), (2, 3))
-        quantize("x", "b1")
-        interleave_f(act, 1, 1, 0, 64, "f0")
+        empty_x(2, 2)
+        interleave_f(act, 0, 1, 0, 52)
         half_pass("b", 0, 0, next_order, None)
-        quantize_f(0, 1)
+        quantize("x", "b1")
+        interleave_f(act, 2, 1, 0, 128, "xa1")
         half_pass("a", 1, EP, late, (2, 3, 0, 1))
-        quantize("x", "b2")
+        quantize_f(0, 1)
+        interleave_f(act, 1, 1, 0, 64, "f0")
         half_pass("b", 0, 1, next_order, None)
+        quantize("x", "b2")
+        half_pass("a", 1, 0, late, None)
         clip("a", 0)
         interleave_u(act, 0, 0, "u0")
-        half_pass("a", 1, 0, late, None)
-        quantize_f(2, 1)
         half_pass("b", 0, 2, next_order, None)
         interleave_f(vec, 1, 1, 64, 128)
         empty_half("b", 0, 0)
+        quantize_f(2, 1)
+        empty_half("b", 0, 1)
         half_pass("a", 1, 2, late, None)
         quantize_f(1, 1)
-        empty_half("b", 0, 1)
+        interleave_u(act, 1, 0, "u1")
         half_pass("a", 1, 1, late, None)
         empty_half("b", 0, 2, True)
-        interleave_u(act, 1, 0, "u1")
         quarter_bank(2, 1, 0, 6)
         empty_half("b", 0, 3, True)
         quarter_bank(2, 1, 1, 7)
@@ -442,16 +442,16 @@ def tile_clipped_feedback_control_s3_kernel(
         rate(0, 1, 5)
         add_drift(0, 0)
         interleave_u(act, 3, 0, "u1")
+        store(0, 0, 1)
         rate(0, 2, 2)
         add_drift(0, 1)
-        store(0, 0, 2)
         rate(0, 3, 3)
         add_drift(0, 2)
+        store(0, 1, 2)
         rate(0, 4, 0)
         quantize("u", "11")
         rate(0, 5, 1)
         add_drift(0, 3)
-        store(0, 2, 2)
         rate(1, 0, 6)
         add_drift(0, 4)
         rate(1, 1, 7)
@@ -459,20 +459,22 @@ def tile_clipped_feedback_control_s3_kernel(
         interleave_u(act, 2, 1, "u2")
         rate(1, 2, 4)
         add_drift(0, 5)
-        store(0, 4, 2)
+        store(0, 3, 3)
         rate(1, 3, 5)
         add_drift(1, 0)
-        quarter_bank(3, 1, 0, 2)
+        rate(1, 4, 2)
         add_drift(1, 1)
-        empty_quarter(3, 1, 0)
         store(1, 0, 2)
-        quarter_bank(3, 1, 1, 3)
+        rate(1, 5, 3)
         add_drift(1, 2)
-        empty_quarter(3, 1, 1)
-        rate(1, 4, 0)
+        quarter_bank(3, 1, 0, 0)
         add_drift(1, 3)
+        empty_quarter(3, 1, 0)
         store(1, 2, 2)
-        rate(1, 5, 1)
+        quarter_bank(3, 1, 1, 1)
+        add_drift(1, 4)
+        add_drift(1, 5)
+        store(1, 4, 2)
         quantize("u", "20")
         quantize("u", "21")
         rate(2, 0, 6)
@@ -480,43 +482,34 @@ def tile_clipped_feedback_control_s3_kernel(
         rate(2, 1, 7)
         clip(3, 1, (0, 1))
         rate(2, 2, 4)
-        add_drift(1, 4)
-        store(1, 4, 1)
-        rate(2, 3, 5)
-        clip(3, 1, (2, 3))
+        empty_quarter(3, 1, 1, True)
         interleave_u(act, 3, 1, "u3")
-        rate(2, 4, 2)
-        add_drift(1, 5)
-        store(1, 5, 1)
-        rate(2, 5, 3)
+        rate(2, 3, 5)
         add_drift(2, 0)
         store(2, 0, 1)
+        rate(2, 4, 2)
         add_drift(2, 1)
-        store(2, 1, 1, act)
+        store(2, 1, 1)
+        rate(2, 5, 3)
         add_drift(2, 2)
-        store(2, 2, 1)
+        add_drift(2, 3)
+        store(2, 2, 2, act)
         quantize("u", "31")
         rate(3, 0, 0)
-        add_drift(2, 3)
-        store(2, 3, 1, act)
-        rate(3, 1, 1)
         add_drift(2, 4)
-        store(2, 4, 1)
-        rate(3, 2, 6)
+        rate(3, 1, 1)
         add_drift(2, 5)
-        store(2, 5, 1, act)
-        rate(3, 3, 7)
+        store(2, 4, 2)
+        rate(3, 2, 6)
         add_drift(3, 0)
-        store(3, 0, 1)
-        rate(3, 4, 4)
+        rate(3, 3, 7)
         add_drift(3, 1)
-        store(3, 1, 1, act)
-        rate(3, 5, 5)
+        store(3, 0, 2, act)
+        rate(3, 4, 4)
         add_drift(3, 2)
-        store(3, 2, 1)
+        rate(3, 5, 5)
         add_drift(3, 3)
-        store(3, 3, 1, act)
+        store(3, 2, 2)
         add_drift(3, 4)
-        store(3, 4, 1)
         add_drift(3, 5)
-        store(3, 5, 1, act)
+        store(3, 4, 2, act)

@@ -70,8 +70,8 @@ def tile_clipped_feedback_control_s3_kernel(
             for g in range(first, last):
                 live["fr", c, g] = tile[:, :, W * (g - first):W * (g - first) + W]
 
-        def load_scale():
-            nc.sync.dma_start(out=scale_col[:], in_=x_scale.rearrange("o (c p j) -> p (o c) j", p=P, j=4))
+        def load_scale(queue=nc.sync):
+            queue.dma_start(out=scale_col[:], in_=x_scale.rearrange("o (c p j) -> p (o c) j", p=P, j=4))
 
         def load_l_scales(queue=nc.sync):
             for q in range(4):
@@ -82,9 +82,9 @@ def tile_clipped_feedback_control_s3_kernel(
         def load_l_words():
             nc.sync.dma_start(out=l_raw[:], in_=L_words[0])
 
-        def load_limits():
-            nc.sync.dma_start(out=lim_bf[0][:], in_=hi.rearrange("(g p t) -> p g t", p=P, t=4))
-            nc.sync.dma_start(out=lim_bf[1][:], in_=lo.rearrange("(g p t) -> p g t", p=P, t=4))
+        def load_limits(queue=nc.sync):
+            queue.dma_start(out=lim_bf[0][:], in_=hi.rearrange("(g p t) -> p g t", p=P, t=4))
+            queue.dma_start(out=lim_bf[1][:], in_=lo.rearrange("(g p t) -> p g t", p=P, t=4))
 
         def load_b_words():
             nc.sync.dma_start(out=bw[:], in_=B_words.rearrange("g p n -> p g n"))
@@ -101,22 +101,26 @@ def tile_clipped_feedback_control_s3_kernel(
 
         def permute_l_words(first, last):
             nc.vector.tensor_copy(
-                out=lw[:, first:last].bitcast(U16).rearrange("p g t m -> p g m t"),
-                in_=l_raw[:, A * first:A * last].bitcast(U16).rearrange("p (g m t) -> p g m t", m=P, t=4),
+                out=lw[:, first:last].bitcast(U16).rearrange("p g t (c m) -> p g c t m", m=8),
+                in_=l_raw[:, A * first:A * last].bitcast(U16).rearrange("p (g c m t) -> p g c t m", c=P // 8, m=8, t=4),
             )
 
         def permute_l_scales(first, last):
             nc.vector.tensor_copy(
-                out=ls[:, first:last].rearrange("p g t m -> p g m t"),
-                in_=l_plane[:, W * first:W * last].rearrange("p (g m t) -> p g m t", m=P, t=4),
+                out=ls[:, first:last].rearrange("p g t (c m) -> p g c t m", m=16),
+                in_=l_plane[:, W * first:W * last].rearrange("p (g c m t) -> p g c t m", c=P // 16, m=16, t=4),
             )
 
-        def widen_x(j, first, last):
+        def widen_x(j, first, last, engine=nc.scalar):
             if ("xv", j) not in live:
                 live["xv", j] = stage.tile([P, 2, S], BF16, name=f"xv{j}", tag=f"xv{j % 2}")
+            cols = slice(W * first, W * last)
             for i in range(2):
-                cols = slice(W * first, W * last)
-                nc.scalar.copy(out=live["xv", j][:, i, cols], in_=xb[j][:, i, cols].bitcast(FP8))
+                dst, src = live["xv", j][:, i, cols], xb[j][:, i, cols].bitcast(FP8)
+                if engine is nc.vector:
+                    nc.vector.tensor_copy(out=dst, in_=src)
+                else:
+                    nc.scalar.copy(out=dst, in_=src)
 
         def turn(j, c, bank):
             tile = psum.tile([P, 2, Q], F32, name=f"xt{j}{c}", tag=f"bank{bank}")
@@ -143,10 +147,10 @@ def tile_clipped_feedback_control_s3_kernel(
                 operand("x", key, buffer, W)
             return live["xg", key][:, 4 * first:4 * first + 4 * Q]
 
-        def scaled(engine, j, c, values, buffer):
+        def scaled(engine, j, c, values, buffer, first=0, last=Q):
             engine.tensor_tensor(
-                out=x_grouped(j, c, buffer).rearrange("p (s u e) -> p s u e", u=2, e=2), in0=values,
-                in1=scale_col[:, c:c + 1, :].rearrange("p o (u e) -> p o u e", u=2).to_broadcast([P, Q, 2, 2]), op=ALU.mult,
+                out=x_grouped(j, c, buffer).rearrange("p (s u e) -> p s u e", u=2, e=2)[:, first:last], in0=values[:, first:last],
+                in1=scale_col[:, c:c + 1, :].rearrange("p o (u e) -> p o u e", u=2).to_broadcast([P, last - first, 2, 2]), op=ALU.mult,
             )
 
         def empty_x(j, c, buffer=None):
@@ -161,8 +165,8 @@ def tile_clipped_feedback_control_s3_kernel(
             live["xp", j, c] = stage.tile([P, Q, 2], F32, name=f"xp{j}{c}", tag=buffer)
             nc.scalar.copy(out=live["xp", j, c][:], in_=live["xt", j, c][:].rearrange("p u s -> p s u"))
 
-        def scale_parked(j, c, buffer=None):
-            scaled(nc.gpsimd, j, c, live["xp", j, c][:].bitcast(BF16).rearrange("p s (u e) -> p s u e", u=2), buffer)
+        def scale_parked(j, c, buffer=None, engine=nc.gpsimd, first=0, last=Q):
+            scaled(engine, j, c, live["xp", j, c][:].bitcast(BF16).rearrange("p s (u e) -> p s u e", u=2), buffer, first, last)
 
         def interleave(engine, dst, src):
             if engine is nc.gpsimd:
@@ -262,31 +266,31 @@ def tile_clipped_feedback_control_s3_kernel(
             src = live["up", j, g][:] if ("up", j, g) in live else live["up", group[j], g][:, :, Q * (j % 2):Q * (j % 2) + Q]
             interleave(engine, live["ug", f"{j}{g}"][:], src)
 
-        def rate(j, n, bank):
-            i, cols = divmod(n, XP)
-            acc = psum.tile([P, W], F32, name=f"y{j}{n}", tag=f"bank{bank}")
-            live["y", j, n] = acc
+        def rate(j, n, bank, first=0, last=W):
+            i, part = divmod(n, XP)
+            acc = psum.tile([P, last - first], F32, name=f"y{j}{n}{first}", tag=f"bank{bank}")
+            live["y", j, n, first] = acc
+            cols = slice(W * part + first, W * part + last)
             for g in range(2):
                 nc.tensor.matmul_mx(
                     out=acc[:],
                     lhsT=live["uq", f"{j}{g}"][:, P * i:P * i + P].bitcast(FP8X4), lhsT_scale=live["us", f"{j}{g}"][:, P * i:P * i + P],
-                    rhs=bw[:, g, 2 * W * cols:2 * W * cols + 2 * W].bitcast(FP4X4),
-                    rhs_scale=b_plane[:, g, W * cols:W * cols + W],
+                    rhs=bw[:, g, 2 * cols.start:2 * cols.stop].bitcast(FP4X4), rhs_scale=b_plane[:, g, cols],
                     start=(g == 0), stop=(g == 1),
                 )
 
-        def out_cols(j, n):
+        def out_cols(j, n, first=0, last=W):
             if ("ot", j) not in live:
                 live["ot", j] = stage.tile([P, 2 * S], F32, name=f"ot{j}", tag=f"ot{j % OT}")
-            cols = slice(W * n, W * n + W)
+            cols = slice(W * n + first, W * n + last)
             return live["ot", j][:, cols], dr[j][:].rearrange("p i k -> p (i k)")[:, cols]
 
-        def add_drift(j, n):
-            dst, given = out_cols(j, n)
-            nc.vector.tensor_tensor(out=dst, in0=live["y", j, n][:], in1=given, op=ALU.add)
+        def add_drift(j, n, first=0, last=W):
+            dst, given = out_cols(j, n, first, last)
+            nc.vector.tensor_tensor(out=dst, in0=live["y", j, n, first][:], in1=given, op=ALU.add)
 
         def store(j, first, count, queue=nc.sync):
-            cols = slice(W * first, W * (first + count))
+            cols = slice(int(W * first), int(W * (first + count)))
             rows = pair_rows(out, j).rearrange("p i k -> p (i k)")
             queue.dma_start(out=rows[:, cols], in_=live["ot", j][:, cols])
 
@@ -299,8 +303,8 @@ def tile_clipped_feedback_control_s3_kernel(
         late = (EP, 0, 2, 1)
         first, second = slice(0, Q), slice(Q, W)
         load_x(0)
-        load_scale()
         load_l_words()
+        load_scale()
         load_x(1)
         load_f(0, 0, 1)
         load_e(0)

@@ -353,48 +353,47 @@ def tile_clipped_feedback_control_s3_kernel(
         empty_e(1)
         turn(2, EP, 2)
         quantize("x", "a3")
-        interleave_f(act, 1, 0, 0, 128, "f1")
-        interleave_f(pool, 2, 0, 0, 24, "xa3")
+        empty_e(2, "xa0")
         turn(3, EP, 3)
         quantize("x", "a1")
-        empty_e(2, "xa0")
+        interleave_f(act, 1, 0, 0, 128, "f1")
         half_pass("a", 0, 0, order, (6, 7, 4, 5))
         permute_l_scales(0, 1)
-        widen_x(2, 0, 1)
+        interleave_f(act, 2, 0, 64, 128, "xa3")
         half_pass("a", 0, EP, order, None)
         empty_x(1, 2)
-        interleave_f(act, 2, 0, 72, 128)
-        turn(2, 0, 0)
+        widen_x(2, 0, 1)
         quantize_f(1, 0)
-        widen_x(3, 0, 1)
+        empty_e(3)
         half_pass("a", 0, 1, order, None)
-        permute_l_scales(1, 2)
+        interleave_f(vec, 2, 0, 0, 64)
+        widen_x(3, 0, 1)
+        turn(2, 0, 0)
+        quantize("x", "a2")
         widen_x(3, 2, 3)
         turn(3, 0, 1)
-        interleave_f(vec, 2, 0, 24, 72)
-        empty_e(3)
-        turn(3, 2, 2)
-        quantize("x", "a2")
-        widen_x(2, 1, 2)
         quantize_f(2, 0)
-        widen_x(3, 1, 2)
+        widen_x(2, 1, 2)
         interleave_f(pool, 0, 1, 52, 128, "xa3")
         half_pass("a", 0, 2, order, None)
+        quantize("x", "b3")
+        widen_x(3, 1, 2)
+        turn(3, 2, 2)
         empty_x(2, 0, "f1")
         widen_x(2, 2, 3)
         turn(2, 1, 3)
         empty_x(3, 0)
         empty_half("a", 0, 0)
-        turn(3, 1, 0)
-        quantize("x", "b3")
+        permute_l_scales(1, 2)
         empty_half("a", 0, 1)
         half_pass("b", 0, EP, next_order, (6, 7, 4, 5), (0, 1))
         quantize("x", "b0")
         park_x(3, 2, "xp0")
         scale_parked(3, 2, "f1")
-        turn(2, 2, 1)
+        turn(3, 1, 0)
         empty_x(2, 1, "xa2")
         empty_half("a", 0, 2)
+        turn(2, 2, 1)
         empty_x(3, 1)
         empty_half("a", 0, 3)
         half_pass("b", 0, EP, next_order, (6, 7, 4, 5), (2, 3))

from contextlib import ExitStack

import concourse.mybir as mybir
from concourse.masks import make_identity

M, S, E, A = 1024, 1536, 512, 1024
FLOPS = 2 * M * A * (S + E) + 2 * M * A * S

F32 = mybir.dt.float32
BF16 = mybir.dt.bfloat16
U32 = mybir.dt.uint32
I32 = mybir.dt.int32
U8 = mybir.dt.uint8
U16 = mybir.dt.uint16
FP8 = mybir.dt.float8_e4m3fn
FP8X4 = mybir.dt.float8_e4m3fn_x4
FP4X4 = mybir.dt.float4_e2m1fn_x4
ALU = mybir.AluOpType
P = 128
W = 512
Q = 256
XP = S // W
EP = XP


def tile_clipped_feedback_control_s3_kernel(
    tc, x_bytes, x_scale, e, F, L_words, L_scales, lo, hi, B_words, B_scales, drift, out
):
    nc = tc.nc
    with ExitStack() as ctx:
        keep = ctx.enter_context(tc.tile_pool(name="keep", bufs=1))
        stage = ctx.enter_context(tc.tile_pool(name="stage", bufs=1))
        psum = ctx.enter_context(tc.psum_pool(name="psum", bufs=1))
        ctx.enter_context(tc.manual_schedule())

        ident = keep.tile([P, P], F32, name="ident")
        make_identity(nc, ident[:])
        l_plane = keep.tile([P, A], U8, name="l_plane", align_bytes=256)
        b_plane = keep.tile([P, 2, S], U8, name="b_plane", align_bytes=256)
        nc.vector.memset(l_plane[:].bitcast(I32), 0)
        nc.vector.memset(b_plane[:].rearrange("p g n -> p (g n)").bitcast(I32), 0)

        scale_col = keep.tile([P, XP, 4], F32, name="scale_col")
        l_raw = keep.tile([P, 2 * A], U8, name="l_raw")
        lim_bf = [keep.tile([P, 2, 4], BF16, name=f"lim_bf{k}") for k in range(2)]
        xb = [keep.tile([P, 2, S], U8, name=f"xb{j}") for j in range(4)]
        eb = [keep.tile([P, 2 * E], BF16, name=f"eb{j}") for j in range(4)]
        bw = keep.tile([P, 2, 2 * S], U8, name="bw", align_bytes=256)
        dr = [keep.tile([P, 2, S], BF16, name=f"dr{j}") for j in range(4)]
        lw = keep.tile([P, 2, 4, 256], U8, name="lw", align_bytes=256)
        ls = keep.tile([P, 2, 4, P], U8, name="ls", align_bytes=256)
        columns_of = {"f": XP * A, "x": (XP + 1) * M, "u": 2 * M}
        codes = {kind: keep.tile([P, n], U32, name=f"{kind}_codes", align_bytes=256) for kind, n in columns_of.items()}
        planes = {kind: keep.tile([P, n], U8, name=f"{kind}_plane", align_bytes=256) for kind, n in columns_of.items()}
        taken = {"f": [], "x": [], "u": []}
        live = {}

        def pair_rows(t, j):
            return t[Q * j:Q * j + Q, :].rearrange("(p i) k -> p i k", i=2)

        def load_x(j):
            nc.sync.dma_start(out=xb[j][:], in_=pair_rows(x_bytes, j))

        def load_e(j):
            nc.sync.dma_start(out=eb[j][:], in_=pair_rows(e, j).rearrange("p i k -> p (i k)"))

        def load_f(c, first, last):
            tile = keep.tile([P, 4, W * (last - first)], BF16, name=f"fr{c}{first}")
            nc.sync.dma_start(out=tile[:], in_=F[W * c:W * c + W, W * first:W * last].rearrange("(p j) a -> p j a", j=4))
            for g in range(first, last):
                live["fr", c, g] = tile[:, :, W * (g - first):W * (g - first) + W]

        def load_scale(queue=nc.sync):
            queue.dma_start(out=scale_col[:], in_=x_scale.rearrange("o (c p j) -> p (o c) j", p=P, j=4))

        def load_l_scales(queue=nc.sync):
            for q in range(4):
                queue.dma_start(
                    out=l_plane[32 * q:32 * q + 4, :].bitcast(I32), in_=L_scales[0, 4 * q:4 * q + 4, :].bitcast(I32)
                )

        def load_l_words():
            nc.sync.dma_start(out=l_raw[:], in_=L_words[0])

        def load_limits(queue=nc.sync):
            queue.dma_start(out=lim_bf[0][:], in_=hi.rearrange("(g p t) -> p g t", p=P, t=4))
            queue.dma_start(out=lim_bf[1][:], in_=lo.rearrange("(g p t) -> p g t", p=P, t=4))

        def load_b_words():
            nc.sync.dma_start(out=bw[:], in_=B_words.rearrange("g p n -> p g n"))

        def load_b_scales():
            for q in range(4):
                nc.sync.dma_start(
                    out=b_plane[32 * q:32 * q + 4, :, :].bitcast(I32),
                    in_=B_scales[:, 4 * q:4 * q + 4, :].rearrange("g q n -> q g n").bitcast(I32),
                )

        def load_drift(j):
            nc.sync.dma_start(out=dr[j][:], in_=pair_rows(drift, j))

        def permute_l_words(first, last):
            nc.vector.tensor_copy(
                out=lw[:, first:last].bitcast(U16).rearrange("p g t (c m) -> p g c t m", m=8),
                in_=l_raw[:, A * first:A * last].bitcast(U16).rearrange("p (g c m t) -> p g c t m", c=P // 8, m=8, t=4),
            )

        def permute_l_scales(first, last):
            nc.vector.tensor_copy(
                out=ls[:, first:last].rearrange("p g t (c m) -> p g c t m", m=16),
                in_=l_plane[:, W * first:W * last].rearrange("p (g c m t) -> p g c t m", c=P // 16, m=16, t=4),
            )

        def widen_x(j, first, last, engine=nc.scalar):
            if ("xv", j) not in live:
                live["xv", j] = stage.tile([P, 2, S], BF16, name=f"xv{j}", tag=f"xv{j % 2}")
            cols = slice(W * first, W * last)
            for i in range(2):
                dst, src = live["xv", j][:, i, cols], xb[j][:, i, cols].bitcast(FP8)
                if engine is nc.vector:
                    nc.vector.tensor_copy(out=dst, in_=src)
                else:
                    nc.scalar.copy(out=dst, in_=src)

        def turn(j, c, bank):
            tile = psum.tile([P, 2, Q], F32, name=f"xt{j}{c}", tag=f"bank{bank}")
            live["xt", j, c] = tile
            for i in range(2):
                src = live["xv", j][:, i, W * c:W * c + W] if c < XP else eb[j][:, E * i:E * i + E]
                words = src.bitcast(F32)
                for u in range(2):
                    nc.tensor.transpose(tile[:, u, P * i:P * i + P], words[:, u::2], ident[:])

        def operand(kind, key, buffer, columns):
            live[kind + "g", key] = stage.tile([P, 4 * columns], BF16, name=f"{kind}g{key}", tag=buffer, align_bytes=256)
            start = columns * len(taken[kind])
            taken[kind].append(key)
            live[kind + "q", key] = codes[kind][:, start:start + columns]
            live[kind + "s", key] = planes[kind][:, start:start + columns]

        def x_place(j, c):
            return (f"{group[j]}{c}", Q * (j % 2)) if group[j] in ("a", "b") else (f"{j}{c // 2}", Q * (c % 2))

        def x_grouped(j, c, buffer):
            key, first = x_place(j, c)
            if ("xg", key) not in live:
                operand("x", key, buffer, W)
            return live["xg", key][:, 4 * first:4 * first + 4 * Q]

        def scaled(engine, j, c, values, buffer, first=0, last=Q):
            engine.tensor_tensor(
                out=x_grouped(j, c, buffer).rearrange("p (s u e) -> p s u e", u=2, e=2)[:, first:last], in0=values[:, first:last],
                in1=scale_col[:, c:c + 1, :].rearrange("p o (u e) -> p o u e", u=2).to_broadcast([P, last - first, 2, 2]), op=ALU.mult,
            )

        def empty_x(j, c, buffer=None):
            scaled(nc.vector, j, c, live["xt", j, c][:].bitcast(BF16).rearrange("p u (s e) -> p s u e", e=2), buffer)

        def empty_e(j, buffer=None):
            nc.scalar.copy(
                out=x_grouped(j, EP, buffer).bitcast(F32).rearrange("p (s u) -> p s u", u=2), in_=live["xt", j, EP][:].rearrange("p u s -> p s u")
            )

        def park_x(j, c, buffer):
            live["xp", j, c] = stage.tile([P, Q, 2], F32, name=f"xp{j}{c}", tag=buffer)
            nc.scalar.copy(out=live["xp", j, c][:], in_=live["xt", j, c][:].rearrange("p u s -> p s u"))

        def scale_parked(j, c, buffer=None, engine=nc.gpsimd, first=0, last=Q):
            scaled(engine, j, c, live["xp", j, c][:].bitcast(BF16).rearrange("p s (u e) -> p s u e", u=2), buffer, first, last)

        def interleave(engine, dst, src):
            if engine is nc.gpsimd:
                nc.gpsimd.tensor_scalar(
                    out=dst.rearrange("p (s t) -> p s t", t=4), in0=src.rearrange("p t s -> p s t"),
                    scalar1=1.0, scalar2=0.0, op0=ALU.mult, op1=ALU.add,
                )
                return
            src = src.rearrange("p t (c i) -> p c t i", i=4)
            dst = dst.rearrange("p (c i t) -> p c t i", i=4, t=4)
            if engine is nc.vector:
                nc.vector.tensor_copy(out=dst, in_=src)
            else:
                nc.scalar.copy(out=dst, in_=src)

        def quantize(kind, key):
            nc.vector.quantize_mx(out=live[kind + "q", key].bitcast(FP8X4), scales=live[kind + "s", key], in_=live[kind + "g", key][:])

        def interleave_f(engine, c, g, first, last, buffer=None):
            if ("fg", f"{c}{g}") not in live:
                operand("f", f"{c}{g}", buffer, W)
            raw, grouped = live["fr", c, g], live["fg", f"{c}{g}"][:]
            if engine is nc.gpsimd:
                src = raw.rearrange("p j (m t) -> p t m j", t=4)[:, :, first:last]
                dst = grouped.rearrange("p (t m j) -> p t m j", t=4, j=4)[:, :, first:last]
                nc.gpsimd.tensor_scalar(out=dst, in0=src, scalar1=1.0, scalar2=0.0, op0=ALU.mult, op1=ALU.add)
                return
            m = slice(first // 2, last // 2)
            src = raw.rearrange("p j (m r t) -> p m t j r", r=2, t=4)[:, m]
            dst = grouped.rearrange("p (t m r j) -> p m t j r", t=4, r=2, j=4)[:, m]
            if engine is nc.vector:
                nc.vector.tensor_copy(out=dst, in_=src)
            else:
                nc.scalar.copy(out=dst, in_=src)

        def quantize_f(c, g):
            quantize("f", f"{c}{g}")

        def action_pass(acc, key, first, width, g, t, c, order):
            cols = slice(P * t, P * t + P)
            if c < XP:
                w, ws = live["fq", f"{c}{g}"][:, cols].bitcast(FP8X4), live["fs", f"{c}{g}"][:, cols]
            else:
                w, ws = lw[:, g, t, :].bitcast(FP4X4), ls[:, g, t, :]
            nc.tensor.matmul_mx(
                out=acc, lhsT=w, lhsT_scale=ws,
                rhs=live["xq", key][:, first:first + width].bitcast(FP8X4), rhs_scale=live["xs", key][:, first:first + width],
                start=(c == order[0]), stop=(c == order[-1]),
            )

        def half_pass(h, g, c, order, banks, tiles=range(4)):
            for t in tiles:
                if c == order[0]:
                    live["acc", h, g, t] = psum.tile([P, W], F32, name=f"acc{h}{g}{t}", tag=f"bank{banks[t]}")
                action_pass(live["acc", h, g, t][:], f"{h}{c}", 0, W, g, t, c, order)

        def quarter_bank(j, g, k, bank):
            acc = psum.tile([P, 2, Q], F32, name=f"acc{j}{g}{k}", tag=f"bank{bank}")
            live["acc", j, g, k] = acc
            for r in range(2):
                for c in range(XP + 1):
                    key, first = x_place(j, c)
                    action_pass(acc[:, r, :], key, first, Q, g, 2 * k + r, c, range(XP + 1))

        def planes_u(key, g, width):
            if ("up", key, g) not in live:
                live["up", key, g] = stage.tile([P, 4, width], BF16, name=f"up{key}{g}", tag=planes_in.get((key, g), f"up{key}{g}"))
            return live["up", key, g]

        def clipped(dst, src, g, t):
            nc.vector.tensor_scalar(
                out=dst, in0=src, scalar1=lim_bf[0][:, g, t:t + 1], scalar2=lim_bf[1][:, g, t:t + 1], op0=ALU.min, op1=ALU.max
            )

        def empty_half(h, g, t, on_vector=False, cols=slice(0, W)):
            dst, src = planes_u(h, g, W)[:, t, cols], live["acc", h, g, t][:, cols]
            if on_vector:
                clipped(dst, src, g, t)
            else:
                nc.scalar.copy(out=dst, in_=src)

        def empty_quarter(j, g, k, on_vector=False):
            up, acc = planes_u(j, g, Q), live["acc", j, g, k]
            if on_vector:
                for r in range(2):
                    clipped(up[:, 2 * k + r, :], acc[:, r, :], g, 2 * k + r)
            else:
                nc.scalar.copy(out=up[:, 2 * k:2 * k + 2, :], in_=acc[:])

        def clip(key, g, tiles=range(4), cols=slice(None)):
            for t in tiles:
                u = live["up", key, g][:, t, cols]
                clipped(u, u, g, t)

        def interleave_u(engine, j, g, buffer):
            operand("u", f"{j}{g}", buffer, Q)
            src = live["up", j, g][:] if ("up", j, g) in live else live["up", group[j], g][:, :, Q * (j % 2):Q * (j % 2) + Q]
            interleave(engine, live["ug", f"{j}{g}"][:], src)

        def rate(j, n, bank, first=0, last=W):
            i, part = divmod(n, XP)
            acc = psum.tile([P, last - first], F32, name=f"y{j}{n}{first}", tag=f"bank{bank}")
            live["y", j, n, first] = acc
            cols = slice(W * part + first, W * part + last)
            for g in range(2):
                nc.tensor.matmul_mx(
                    out=acc[:],
                    lhsT=live["uq", f"{j}{g}"][:, P * i:P * i + P].bitcast(FP8X4), lhsT_scale=live["us", f"{j}{g}"][:, P * i:P * i + P],
                    rhs=bw[:, g, 2 * cols.start:2 * cols.stop].bitcast(FP4X4), rhs_scale=b_plane[:, g, cols],
                    start=(g == 0), stop=(g == 1),
                )

        def out_cols(j, n, first=0, last=W):
            if ("ot", j) not in live:
                live["ot", j] = stage.tile([P, 2 * S], F32, name=f"ot{j}", tag=f"ot{j % OT}")
            cols = slice(W * n + first, W * n + last)
            return live["ot", j][:, cols], dr[j][:].rearrange("p i k -> p (i k)")[:, cols]

        def add_drift(j, n, first=0, last=W):
            dst, given = out_cols(j, n, first, last)
            nc.vector.tensor_tensor(out=dst, in0=live["y", j, n, first][:], in1=given, op=ALU.add)

        def store(j, first, count, queue=nc.sync):
            cols = slice(int(W * first), int(W * (first + count)))
            rows = pair_rows(out, j).rearrange("p i k -> p (i k)")
            queue.dma_start(out=rows[:, cols], in_=live["ot", j][:, cols])

        act, vec, pool = nc.scalar, nc.vector, nc.gpsimd
        OT = 3
        group = ("a", "a", "b", "b")
        planes_in = {}
        order = (0, EP, 1, 2)
        next_order = (EP, 0, 1, 2)
        late = (EP, 0, 2, 1)
        first, second = slice(0, Q), slice(Q, W)
        load_x(0)
        load_l_words()
        load_scale()
        load_x(1)
        load_f(0, 0, 1)
        load_e(0)
        load_e(1)
        load_e(2)
        load_e(3)
        load_f(1, 0, 1)
        load_l_scales()
        load_f(2, 0, 1)
        load_x(2)
        load_x(3)
        load_f(0, 1, 2)
        load_limits()
        load_f(2, 1, 2)
        load_f(1, 1, 2)
        load_b_words()
        load_b_scales()
        load_drift(0)
        load_drift(1)
        load_drift(2)
        load_drift(3)
        permute_l_words(0, 2)
        widen_x(0, 0, 1)
        turn(0, 0, 0)
        empty_x(0, 0, "xa0")
        widen_x(0, 2, 3)
        turn(0, 2, 1)
        widen_x(0, 1, 2)
        turn(0, 1, 2)
        empty_x(0, 1, "xa1")
        widen_x(1, 0, 1)
        turn(1, 0, 3)
        empty_x(1, 0)
        park_x(0, 2, "xp0")
        scale_parked(0, 2, "xa2")
        widen_x(1, 1, 3)
        turn(1, 1, 0)
        empty_x(1, 1)
        interleave_f(act, 0, 0, 0, 128, "f0")
        turn(1, 2, 1)
        quantize("x", "a0")
        turn(0, EP, 4)
        quantize_f(0, 0)
        empty_e(0, "xa3")
        turn(1, EP, 5)
        empty_e(1)
        turn(2, EP, 2)
        quantize("x", "a3")
        empty_e(2, "xa0")
        turn(3, EP, 3)
        quantize("x", "a1")
        interleave_f(act, 1, 0, 0, 128, "f1")
        half_pass("a", 0, 0, order, (6, 7, 4, 5))
        permute_l_scales(0, 1)
        interleave_f(act, 2, 0, 64, 128, "xa3")
        half_pass("a", 0, EP, order, None)
        empty_x(1, 2)
        widen_x(2, 0, 1)
        quantize_f(1, 0)
        empty_e(3)
        half_pass("a", 0, 1, order, None)
        interleave_f(vec, 2, 0, 0, 64)
        widen_x(3, 0, 1)
        turn(2, 0, 0)
        quantize("x", "a2")
        widen_x(3, 2, 3)
        turn(3, 0, 1)
        quantize_f(2, 0)
        widen_x(2, 1, 2)
        interleave_f(pool, 0, 1, 52, 128, "xa3")
        half_pass("a", 0, 2, order, None)
        quantize("x", "b3")
        widen_x(3, 1, 2)
        turn(3, 2, 2)
        empty_x(2, 0, "f1")
        widen_x(2, 2, 3)
        turn(2, 1, 3)
        empty_x(3, 0)
        empty_half("a", 0, 0)
        permute_l_scales(1, 2)
        empty_half("a", 0, 1)
        half_pass("b", 0, EP, next_order, (6, 7, 4, 5), (0, 1))
        quantize("x", "b0")
        park_x(3, 2, "xp0")
        scale_parked(3, 2, "f1")
        turn(3, 1, 0)
        empty_x(2, 1, "xa2")
        empty_half("a", 0, 2)
        turn(2, 2, 1)
        empty_x(3, 1)
        empty_half("a", 0, 3)
        half_pass("b", 0, EP, next_order, (6, 7, 4, 5), (2, 3))
        empty_x(2, 2)
        interleave_f(act, 0, 1, 0, 52)
        half_pass("b", 0, 0, next_order, None)
        quantize("x", "b1")
        interleave_f(act, 2, 1, 0, 128, "xa1")
        half_pass("a", 1, EP, late, (2, 3, 0, 1))
        quantize_f(0, 1)
        interleave_f(act, 1, 1, 0, 64, "f0")
        half_pass("b", 0, 1, next_order, None)
        quantize("x", "b2")
        half_pass("a", 1, 0, late, None)
        clip("a", 0)
        interleave_u(act, 0, 0, "u0")
        half_pass("b", 0, 2, next_order, None)
        interleave_f(vec, 1, 1, 64, 128)
        empty_half("b", 0, 0)
        quantize_f(2, 1)
        empty_half("b", 0, 1)
        half_pass("a", 1, 2, late, None)
        quantize_f(1, 1)
        interleave_u(act, 1, 0, "u1")
        half_pass("a", 1, 1, late, None)
        empty_half("b", 0, 2, True)
        quarter_bank(2, 1, 0, 6)
        empty_half("b", 0, 3, True)
        quarter_bank(2, 1, 1, 7)
        quantize("u", "00")
        empty_half("a", 1, 0, True, first)
        empty_half("a", 1, 0, False, second)
        empty_half("a", 1, 1, True, first)
        empty_half("a", 1, 1, False, second)
        empty_half("a", 1, 2, True, first)
        empty_half("a", 1, 2, False, second)
        empty_half("a", 1, 3, True, first)
        empty_half("a", 1, 3, False, second)
        clip("b", 0, (0, 1))
        empty_quarter(2, 1, 0)
        interleave_u(vec, 0, 1, "u2")
        clip("a", 1, (0, 1, 2, 3), second)
        interleave_u(act, 1, 1, "u0")
        quantize("u", "01")
        empty_quarter(2, 1, 1)
        rate(0, 0, 4)
        quantize("u", "10")
        interleave_u(act, 2, 0, "u3")
        rate(0, 1, 5)
        add_drift(0, 0)
        interleave_u(act, 3, 0, "u1")
        store(0, 0, 1)
        rate(0, 2, 2)
        add_drift(0, 1)
        rate(0, 3, 3)
        add_drift(0, 2)
        store(0, 1, 2)
        rate(0, 4, 0)
        quantize("u", "11")
        rate(0, 5, 1)
        add_drift(0, 3)
        rate(1, 0, 6)
        add_drift(0, 4)
        rate(1, 1, 7)
        clip(2, 1)
        interleave_u(act, 2, 1, "u2")
        rate(1, 2, 4)
        add_drift(0, 5)
        store(0, 3, 3)
        rate(1, 3, 5)
        add_drift(1, 0)
        rate(1, 4, 2)
        add_drift(1, 1)
        store(1, 0, 2)
        rate(1, 5, 3)
        add_drift(1, 2)
        quarter_bank(3, 1, 0, 0)
        add_drift(1, 3)
        empty_quarter(3, 1, 0)
        store(1, 2, 2)
        quarter_bank(3, 1, 1, 1)
        add_drift(1, 4)
        add_drift(1, 5)
        store(1, 4, 2)
        quantize("u", "20")
        quantize("u", "21")
        rate(2, 0, 6)
        quantize("u", "30")
        rate(2, 1, 7)
        clip(3, 1, (0, 1))
        rate(2, 2, 4)
        empty_quarter(3, 1, 1, True)
        interleave_u(act, 3, 1, "u3")
        rate(2, 3, 5)
        add_drift(2, 0)
        store(2, 0, 1)
        rate(2, 4, 2)
        add_drift(2, 1)
        store(2, 1, 1)
        rate(2, 5, 3)
        add_drift(2, 2)
        add_drift(2, 3)
        store(2, 2, 2, act)
        quantize("u", "31")
        rate(3, 0, 0)
        add_drift(2, 4)
        rate(3, 1, 1)
        add_drift(2, 5)
        store(2, 4, 2)
        rate(3, 2, 6)
        add_drift(3, 0)
        rate(3, 3, 7)
        add_drift(3, 1)
        store(3, 0, 2, act)
        rate(3, 4, 4)
        add_drift(3, 2)
        rate(3, 5, 5)
        add_drift(3, 3)
        store(3, 2, 2)
        add_drift(3, 4)
        add_drift(3, 5)
        store(3, 4, 2, act)
